import numpy as np, ml_dtypes
CORES = [1,5,17,21,33,37,49,53]
N = 8
BF = ml_dtypes.bfloat16
M, P, W, ST, SH, VM = 8192, 512, 384, 3, 3, 1024
NB, VB = 8161, 1023
AIM = np.array([255] * 14 + [16, 1])
def spot(u):
    return ((u * 241) >> 6) & (P - 1)
def lanes(u):
    b = u % 255
    return np.array([min(15, max(0, u // 255 - 15 * i)) for i in range(14)] + [b // 16, b % 16])
def aim(rng, c):
    u = np.arange(53000); return lanes(int(rng.choice(u[spot(u) == c])))
def below(rng, n):
    return (rng.random((N, 8, 16, n.shape[3]), dtype=np.float32) * n.astype(np.float32)).astype(np.int32)
def names(rng, pool, share, n):
    z = (N, 8, 16, n); p = np.take_along_axis(np.broadcast_to(pool, (N,) + pool.shape), rng.integers(0, pool.shape[2], z), 3)
    return np.where(rng.random(z) < share, p, rng.integers(0, M, z))
def parts(rng):
    g = below(rng, rng.integers(5, 17, (N, 8, 1, M))); e = below(rng, rng.integers(4, 17, (N, 8, 1, M)))
    pool = rng.integers(0, M, (8, 16, 6)); asl = rng.random((N, 8, 16, W)) < 0.5
    nm = np.where(asl, names(rng, pool, 0.8, W), names(rng, pool, 0.0, W))
    k = np.where(rng.random((N, 8, 16, P)) < 0.7, names(rng, pool, 0.7, P), M)
    return {"g": g, "e": e, "y": below(rng, rng.integers(8, 17, (N, 8, 1, P))), "k": k, "x": rng.integers(0, 16, (N, 8, 16, W)), "nm": nm, "asl": asl,
            "d": rng.integers(4, 15, (N, 8, 16, ST)), "h": rng.integers(0, 256, (N, 8, 16, 1)), "th": rng.integers(50, 101, (N, 8, 1, 1))}
def pack(s):
    def fl(a, n): return np.ascontiguousarray(a.reshape(N, 128, n)).astype(np.float32).astype(BF)
    def wh(a, n): return np.ascontiguousarray(a.reshape(N, 128, n)).astype(np.int32)
    return {"fx": fl(s["g"] + 16 * s["e"], M), "y0": fl(s["y"], P), "k0": wh(s["k"], P), "x0": fl(s["x"], W), "t0": wh(s["nm"] + M * s["asl"].astype(np.int64), W),
            "dw": wh(s["d"], ST), "hw": wh(s["h"], 1), "th": wh(np.repeat(s["th"], 16, axis=2), 1)}
def setup_inputs(rng):
    return pack(parts(rng))
def setup_inputs_spread(rng):
    s = parts(rng)
    s["g"] = below(rng, np.exp2(4 * rng.random((N, 8, 1, M))).astype(np.int64) + 1); s["e"] = below(rng, np.exp2(4 * rng.random((N, 8, 1, M))).astype(np.int64) + 1)
    s["g"] = np.minimum(s["g"], 15); s["e"] = np.minimum(s["e"], 15)
    s["x"] = np.minimum(below(rng, np.exp2(1 + 3 * rng.random((N, 8, 1, W))).astype(np.int64) + 1), 15)
    s["y"] = np.minimum(below(rng, np.exp2(1 + 3 * rng.random((N, 8, 1, P))).astype(np.int64) + 1), 15)
    s["asl"] = rng.random((N, 8, 16, W)) < rng.random((N, 8, 1, W))
    uneven = np.minimum(np.exp2(np.log2(M) * rng.random((N, 8, 16, W))).astype(np.int64) - 1, M - 1)
    s["nm"] = np.where(rng.random((N, 8, 1, W)) < 0.5, uneven, s["nm"])
    s["k"] = np.where(rng.random((N, 8, 16, P)) < rng.random((N, 8, 1, P)), s["k"], M)
    s["h"] = np.minimum(np.exp2(8 * rng.random((N, 8, 16, 1))).astype(np.int64), 255)
    s["d"] = rng.integers(1, 17, (N, 8, 16, ST)); s["th"] = rng.integers(0, 241, (N, 8, 1, 1))
    return pack(s)
def setup_inputs_ends(rng):
    s = parts(rng); z = (N, 8, 16, W)
    f = np.where(rng.random((N, 8, 1, M)) < 0.8, 255 * rng.integers(0, 2, (N, 8, 16, M)), s["g"] + 16 * s["e"])
    f[..., 0] = 0; f[..., 1] = 48; f[..., NB] = 0; f[..., M - 1] = 255
    s["g"] = f & 15; s["e"] = f >> 4
    th = np.where((np.arange(N)[:, None] + np.arange(8)[None, :]) % 2 == 0, 240, 0).reshape(N, 8, 1, 1)
    th[::2, 6] = 239; th[1::2, 6] = 1; s["th"] = th
    r = rng.random((N, 8, 1, P)); s["y"] = np.where(r < 0.3, 15, np.where(r < 0.6, 0, 15 * rng.integers(0, 2, (N, 8, 16, P))))
    s["y"][..., spot(61200)] = np.where(th[..., 0] >= 239, 0, 15)
    for q in range(1, N, 2):
        b = (q >> 1) & 1; s["y"][q, 6, 15, spot(61200)] = 14 - b; s["y"][q, 6, :, 0] = 0; s["y"][q, 6, 15, 0] = 2 - b
    r = rng.random((N, 8, 16, P)); s["k"] = np.where(r < 0.4, 0, np.where(r < 0.8, M, np.where(r < 0.9, M - 1, s["k"])))
    kind = rng.choice(4, (N, 8, 1, W), p=[0.3, 0.2, 0.3, 0.2]); kind[..., W - 4:] = np.array([3, 2, 1, 0])
    x = np.where(kind == 0, 15, np.where(kind == 1, 0, np.where(kind == 2, 15 * rng.integers(0, 2, z), 7)))
    both = (2 * M - 1) * rng.integers(0, 2, z); r = rng.random(z)
    t = np.where((kind == 0) | (r < 0.75), both, np.where(r < 0.85, M - 1, np.where(r < 0.95, M, s["nm"] + M * s["asl"])))
    t = np.where(kind == 3, np.where((np.arange(16) % 2 == 0)[None, None, :, None], 1, 2 * M - 1), t)
    h = 255 * rng.integers(0, 2, (N, 8, 16, 1)); h[:, 0] = 255; h[:, 6] = 255; h[:, 7] = 255; h[:, 3] = 0; h[:, 5, :, 0] = AIM
    for q in range(N):
        for w in (1, W - 6, W - 5):
            x[q, 5, :, w] = aim(rng, P - 1); t[q, 5, :, w] = both[q, 5, :, w]
        for w in (2, W - 8):
            x[q, 5, :, w] = lanes(int(rng.choice(np.arange(VB, 53000, VM)))); t[q, 5, :, w] = NB
    s["x"] = x; s["nm"] = t & (M - 1); s["asl"] = t >= M; s["h"] = h
    s["d"] = np.where(rng.random((N, 8, 16, ST)) < 0.5, 16, 1)
    return pack(s)
def setup_inputs_corners(rng):
    s = parts(rng); z = (N, 8, 16, W); row = np.arange(16)[None, None, :, None]
    o = np.argsort(rng.random((N, 8, 16, 64)), axis=2); s["g"][..., :64] = np.where(o < 8 + np.arange(64) % 4, 0, 15)
    s["g"][..., M - 1] = 0; s["e"][..., M - 1] = 0; s["g"][..., M - 2] = 15
    kind = rng.integers(0, 8, (N, 8, 1, W)); kind[:, 5, :, :8] = 1; kind[:, 5, :, W - 8:] = 1
    x = np.where(kind == 7, s["x"], rng.integers(1, 14, z)); one = rng.integers(0, 16, (N, 8, 1, W)); end = 15 * rng.integers(0, 2, (N, 8, 1, W))
    low = rng.integers(0, 64, z); nm = s["nm"]
    asl = np.where(kind == 0, True, np.where(kind <= 4, False, np.where(kind == 5, row != end, s["asl"])))
    nm = np.where(kind == 1, M - 1, np.where(kind == 2, M - 2, np.where(kind == 3, np.where(row == one, M - 1, M - 2), nm)))
    nm = np.where((kind == 4) | ((kind == 5) & (row == end)), low, np.where(kind == 6, (M - 1) * rng.integers(0, 2, z), nm))
    s["h"][:, 5, :, 0] = AIM; s["h"][:, 2] = 255; s["h"][:, 6, 15] = 0
    s["d"] = rng.choice(np.array([1, 2, 8, 15, 16]), (N, 8, 16, ST))
    s["th"] = rng.choice(np.array([0, 1, 60, 240]), (N, 8, 1, 1)); s["th"][:, 0] = 1; s["th"][:, 4] = 0; s["th"][:, 7] = 240
    r = rng.random((N, 8, 1, P)); s["k"] = np.where(r < 0.25, M, np.where((r < 0.5) & (s["k"] == M), (M - 1) * rng.integers(0, 2, (N, 8, 16, P)), s["k"]))
    for q in range(N):
        for w in list(range(8)) + list(range(W - 8, W)):
            x[q, 5, :, w] = aim(rng, (0, P - 1)[(w + q) & 1])
        for g in range(8):
            w = np.flatnonzero(kind[q, g, 0] == 0)
            if len(w) == 0: continue
            xs = np.array(x[q, g][:, w]); c = spot(np.add.reduce(s["h"][q, g] * xs, axis=0))
            xs[15] = xs[15] + rng.integers(0, 3, len(w)); s["y"][q, g][:, c] = xs
            m = rng.random((16, len(w))); own = nm[q, g][:, w]
            s["k"][q, g][:, c] = np.where(m < 0.6, own, np.where(m < 0.8, M, (own + 1) & (M - 1)))
    s["x"] = x; s["nm"] = nm; s["asl"] = asl
    return pack(s)
def setup_inputs_crowd(rng):
    s = parts(rng); row = np.arange(16)[None, None, :, None]; w = np.arange(W)[None, None, None, :]
    s["e"][:, :3] = 0; s["g"][:, 0] = 0; a = rng.integers(0, 16, (8, 16, 1)); a[:, 0] = 2; s["x"][:, :3] = a[None, :3]
    for q in range(N): s["x"][q, 1, :, (0, W - 1)[q & 1]] = 15 - a[1, :, 0]
    b = rng.integers(0, 3, (N, 1, W)); s["x"][:, 2] = np.where(b == 0, a[None, 2], np.where(b == 1, 15 - a[None, 2], (a[None, 2] + 5) & 15))
    s["h"][:, 3] = 0
    one = rng.integers(0, 16, (N, 1, 1, W)); s["asl"][:, :1] = np.where(w % 4 == 0, False, np.where(w % 4 == 1, row == one, s["asl"][:, :1]))
    two = rng.integers(0, M, (8, 16, 2)); t = names(rng, two, 1.0, W); k = names(rng, two, 1.0, P)
    s["nm"][:, :4] = np.where(s["asl"], t, s["nm"])[:, :4]; s["k"][:, :4] = np.where(s["k"] < M, k, M)[:, :4]
    s["th"][:, 0] = 0; s["th"][:, 1] = 240 * rng.integers(0, 2, (N, 1, 1))
    s["e"][:, 4] = 0; s["h"][:, 4, :, 0] = AIM
    s["asl"][:, 5] = True; s["x"][:, 5] = rng.integers(1, 15, (N, 16, W)); s["g"][:, 5, :, 0] = 0; s["e"][:, 5, :, 0] = 15; s["d"][:, 5, :, 0] = 1
    for q in range(N):
        o = rng.permutation(53000); i = np.unique(spot(o), return_index=True)[1]
        i = rng.permutation(np.concatenate([i[:1], i[-1:], rng.permutation(i[1:-1])[:W - 2]]))
        s["x"][q, 4] = np.stack([lanes(int(j)) for j in o[i]], axis=1); s["th"][q, 4] = 16 * (q & 1)
        m = (2, 4, 8, W)[q & 3]; at = np.arange(m - 1, W, m); ro = rng.integers(0, 15, len(at))
        s["asl"][q, 5, ro, at] = False; s["nm"][q, 5, ro, at] = 0
    s["asl"][:, 6] = False; s["g"][:, 6] = 15; s["g"][:, 6, :, 0] = 0; s["e"][:, 6, :, 0] = np.minimum(s["e"][:, 6, :, 0], 14); s["x"][:, 6] = np.minimum(s["x"][:, 6], 14)
    s["nm"][:, 6] = np.where(row[0] == one[:, 0], 0, np.maximum(s["nm"][:, 6], 1))
    return pack(s)
def check_inputs(d):
    bad = []
    for k, lo, hi in (("fx", 0, 255), ("y0", 0, 15), ("k0", 0, M), ("x0", 0, 15), ("t0", 0, 2 * M - 1), ("dw", 1, 16), ("hw", 0, 255), ("th", 0, 240)):
        a = np.asarray(d[k]).astype(np.float64)
        if not (np.min(a) >= lo and np.max(a) <= hi): bad.append("range of " + k)
        elif not np.all(a == np.floor(a)): bad.append("whole numbers in " + k)
    a = np.asarray(d["th"]).reshape(-1, 16)
    if not np.all(a == a[:, :1]): bad.append("th alike in a group")
    return bad
def reference(fx, y0, k0, x0, t0, dw, hw, th):
    F = fx.astype(np.float32).astype(np.int32).reshape(N, 8, 16, M); Y = y0.astype(np.float32).astype(np.int32).reshape(N, 8, 16, P); K = np.array(k0, np.int32).reshape(N, 8, 16, P)
    X = x0.astype(np.float32).astype(np.int32).reshape(N, 8, 16, W); t1 = np.array(t0, np.int32).reshape(N, 8, 16, W)
    T = t1 & (M - 1); S = t1 >= M; A = np.zeros((N, 8, W), np.int32)
    dd = dw.reshape(N, 8, 16, ST); hh = hw.astype(np.int32).reshape(N, 8, 16, 1); top = th.reshape(N, 8, 16)[:, :, :1]
    row = np.arange(16, dtype=np.int32)[None, :, None]; turn = (np.arange(W) & 3)[None, :]
    for t in range(ST):
        if t > 0: X = np.roll(X, SH, axis=0); T = np.roll(T, SH, axis=0); S = np.roll(S, SH, axis=0); A = np.roll(A, SH, axis=0)
        for q in range(N):
            x = X[q]; nm = T[q]; asl = S[q]
            f = np.take_along_axis(F[q], nm.reshape(8, 1, 16 * W), 2).reshape(8, 16, 16, W)
            gu = f & 15; ef = f >> 4; xx = x[:, :, None, :]
            en = np.add.reduce((xx >= gu).astype(np.int32), axis=1) >= 9 + A[q][:, None, :]
            cand = en & ~asl; ci = cand.astype(np.int32); before = np.add.accumulate(ci, axis=1) - ci
            pos = np.minimum(turn, np.add.reduce(ci, axis=1) - 1)[:, None, :]
            go = cand & (before == pos)
            e = np.add.reduce(ef * go[:, None, :, :].astype(np.int32), axis=2, dtype=np.int32); ee = e[:, :, None, :]
            asl = asl | (cand & (before < pos))
            differ = np.abs(np.abs(xx - ef) - ee) != np.abs(np.abs(xx - ee) - ef)
            asl = asl & (np.add.reduce(differ.astype(np.int32), axis=1) < dd[q][:, :, t:t + 1])
            x = np.abs(x - e)
            u = np.add.reduce(hh[q] * x, axis=1); v = (u & (VM - 1))[:, None, :]
            nm = np.where(asl, nm, (((nm * (2 * v + 1)) >> 5) + nm + 37 * row) & (M - 1))
            c = ((u * 241) >> 6) & (P - 1)
            yc = np.take_along_axis(Y[q], c[:, None, :], 2); kc = np.take_along_axis(K[q], c[:, None, :], 2)
            hit = np.add.reduce(np.abs(yc - x), axis=1) <= top[q]; hb = hit[:, None, :]
            same = asl & (kc == nm)
            y1 = np.where(hb, yc, x); k1 = np.where(hb, np.where(same, kc, M), np.where(asl, nm, M))
            get = hb & (kc < M) & ~same
            nm = np.where(get, kc, nm); asl = asl & ~get
            for g in range(8):
                win = np.full(P, -1); np.maximum.at(win, c[g], np.arange(W)); at = np.flatnonzero(win >= 0)
                Y[q, g][:, at] = y1[g][:, win[at]]; K[q, g][:, at] = k1[g][:, win[at]]
            X[q] = x; T[q] = nm; S[q] = asl; A[q] = hit
    return {"yx": X.reshape(N, 128, W).astype(np.float32).astype(BF), "yt": (T + M * S.astype(np.int32)).reshape(N, 128, W).astype(np.float32),
            "yy": Y.reshape(N, 128, P).astype(np.float32).astype(BF), "yk": K.reshape(N, 128, P).astype(np.float32)}

@@ -1,0 +1,492 @@
+from concourse.mybir import AluOpType, ActivationFunctionType
+
+NM, NP, NW, ST, SH, NR = 8192, 512, 384, 3, 3, 8
+C = 192
+PIECE = 48
+FXP = 1024
+V_GATHERS = (3,)
+S_EVAC = (1, 3)
+S_EVAC_G = (0, 1, 2, 3)
+TP = 512.0625
+CB = -0.0625 - 16.0 - 49152.0
+MAGIC = 1.5 * 2.0 ** 31
+WTS = [1.0, -1.0, -16.0, -0.25, 6.0, 0.0625, -0.9375, 512.0, 32768.0, -16384.0, -60.0, 8.0, 0.03125, -1088.0, 16384.0,
+       16.0, 0.5, -0.5, 8192.0, 245.0 * 8192, 243.0 * 8192, -131072.0, -2048.0]
+LEAD, LATE = 5000, 10000
+SHIFT = {0:1,1:4,4:1,7:-8,8:-32,9:-16,10:-16,11:-3,14:-16,15:-16,16:-24,17:-16,18:-16,19:-12,20:-16,21:-16,24:12,25:12,26:-4,27:-4,28:-6,29:-18,30:-2,31:-2,32:14,33:2,34:2,35:11,36:10,37:2,38:2,39:-16,41:-2,42:12,43:8,44:8,45:8,46:24,49:-4,50:-4,51:-3,55:5,56:-3,57:-4,58:-4,59:-4,60:-4,61:-2,63:-8,65:4,66:-4,67:-16,71:-8,72:-6,73:-6,74:2,75:2,76:2,78:-4,79:-2,84:4,87:2,90:16,94:-8,98:-16,99:-16,103:-16,110:-8,111:-8,114:1,115:-9,116:-5,117:-3,118:-3,119:-3,120:-3,121:-3,122:-3,123:-5,128:2,137:-4,149:8,151:-2,155:2,156:-2,157:-6,158:-14,159:-14,160:-14,161:2,162:2,163:-14,164:2,165:2,166:2,167:2,168:16,171:-2,172:-2,173:6,174:6,175:-1,176:6,177:6,178:6,179:6,180:6,181:-2,183:-8,185:4,187:-4,192:-1,193:-1,194:-1,195:-1,196:-1,197:3,198:3,199:-5,200:4,201:-13,202:3,203:8,204:4,205:4,206:8,207:4,208:-12,213:-16}
+
+SCRATCH = {}
+for _n, _w, _d in [
+        ("F", NM, "bfloat16"), ("E16", NM, "bfloat16"), ("Zt", NM, "bfloat16"), ("Gt", NM, "bfloat16"),
+        ("ioa", 2048, "bfloat16"), ("zero", 128, "bfloat16"), ("Sall", 2048, "bfloat16"), ("Hall", 2048, "bfloat16"),
+        ("Rall", 2048, "bfloat16"), ("ioc", 256, "bfloat16"), ("mats", 128 * 8, "bfloat16"), ("Iw", 128 * len(WTS), "bfloat16"),
+        ("cm", 256, "bfloat16"), ("Dg", 128 * ST, "bfloat16"), ("ones", C, "bfloat16"), ("turn7", 2 * C, "bfloat16"),
+        ("base", 32, "float32"), ("mask", NW, "float32"), ("coli", 32, "int32"), ("colj", 8, "int32"), ("colf", 32, "float32"),
+        ("t0s", NW, "int32"), ("y0s", NP, "bfloat16"), ("k0s", NP, "int32"), ("ytmp", NP, "float32"), ("W", NP + 16, "float32"),
+        ("ent", NW, "float32"), ("cf", 24, "float16"), ("cint", 24, "int32"), ("Eq", NW, "bfloat16"), ("dd", 48, "float32"),
+        ("soff", 48, "uint16"), ("oyt", NW, "float32"), ("oy1", NP, "bfloat16"), ("oy2", NP, "bfloat16"), ("oyk", NP, "float32")]:
+    SCRATCH[_n] = ("sbuf", [128, _w], _d)
+for _c in range(2):
+    for _n, _w, _d in [("VG", 16 * C, "bfloat16"), ("VE", 16 * C + 8, "float32"), ("ca", 16 * C, "bfloat16"), ("cb", 16 * C, "float16"),
+                       ("b", 20 * C, "bfloat16"), ("f", 8 * C, "float32"), ("i", 5 * C, "int32"), ("tf", 64, "float32"),
+                       ("ti", 16, "int32"), ("tu", 32, "uint16")]:
+        SCRATCH[_n + str(_c)] = ("sbuf", [128, _w], _d)
+    for _t in range(ST):
+        for _p in "rs":
+            SCRATCH["%sb%d%d" % (_p, _t, _c)] = ("sbuf", [128, 3 * C], "bfloat16")
+            SCRATCH["%sn%d%d" % (_p, _t, _c)] = ("sbuf", [128, C], "int32")
+            SCRATCH["%su%d%d" % (_p, _t, _c)] = ("sbuf", [128, C], "uint16")
+for _k in range(8):
+    SCRATCH["ps%d" % _k] = ("psum", [128, 512], "float32")
+DRAM = ("fx", "y0", "k0", "x0", "t0", "dw", "hw", "th", "yx", "yt", "yy", "yk")
+NDMA = NM // FXP + 14
+SEMAPHORES = ["V", "S", "P", "G", "sent"] + ["d%d" % _k for _k in range(NDMA)] + ["a%d" % _k for _k in range(12)]
+
+
+def A(name, lo, hi, step=1):
+    return (name, lo, hi, step)
+
+
+def IND(win, off):
+    return ("@", win, off)
+
+
+def count(ap):
+    if ap[0] == "@":
+        return 16 * (ap[2][2] - ap[2][1])
+    return (ap[2] - ap[1] + ap[3] - 1) // ap[3]
+
+
+def narrow(ap):
+    return ap[0] in SCRATCH and SCRATCH[ap[0]][2] in ("bfloat16", "float16", "uint16")
+
+
+def describe():
+    ops = []
+
+    def tt(o, a, b, op): ops.append(("V", "tt", o, [a, b], op))
+    def ts(o, a, s1, s2, op0, op1=None): ops.append(("V", "ts", o, [a, s1, s2], (op0, op1)))
+    def cp(o, a): ops.append(("V", "cp", o, [a], None))
+    def ms(o, v): ops.append(("V", "ms", o, [], v))
+    def act(o, a, f, bias=0.0, scale=1.0): ops.append(("S", "act", o, [a, bias, scale], f))
+    def io(o, pat, base, cm): ops.append(("G", "iota", o, [], (pat, base, cm)))
+    def sel(o, a, pat, fill, base, cm): ops.append(("G", "sel", o, [a], (pat, base, cm, fill)))
+    def dma(q, o, a): ops.append((q, "dma", o, [a], None))
+    def Iw(w): return A("Iw", 128 * WTS.index(w), 128 * WTS.index(w) + 128)
+    def mat(j): return A("mats", 128 * j, 128 * j + 128)
+    def blk(n, a): return A(n, 128 * a, 128 * a + 128)
+    def cf(j): return A("colf", j, j + 1)
+
+    def lin(o, terms):
+        for j, (l, r) in enumerate(terms):
+            ops.append(("P", "mm", o, [Iw(l) if isinstance(l, float) else l, r], (j == 0, j == len(terms) - 1)))
+
+    dma("Y", A("F", 0, FXP), A("fx", 0, FXP))
+    dma("Y", A("t0s", 0, NW), A("t0", 0, NW))
+    for j in range(1, NM // FXP):
+        dma("Y", A("F", j * FXP, (j + 1) * FXP), A("fx", j * FXP, (j + 1) * FXP))
+    for c in range(2):
+        dma("Y", A("rb0%d" % c, 0, C), A("x0", c * C, (c + 1) * C))
+    dma("Y", A("y0s", 0, NP), A("y0", 0, NP))
+    dma("Y", A("k0s", 0, NP), A("k0", 0, NP))
+    io(A("ioc", 0, 128), [[1, 128]], 0, -1)
+    io(A("colj", 0, 1), [[1, 1]], 0, 1)
+    io(A("ioa", 0, 2048), [[-1, 16], [1, 128]], 0, 0)
+    io(A("ioc", 128, 256), [[16, 8], [0, 16]], 0, 0)
+    io(A("turn7", 0, C), [[0, C // 4], [1, 4]], 0, 0)
+    io(A("base", 0, 24), [[-1, 2], [256, 12]], 16, 0)
+    dma("G", A("coli", 0, 1), A("hw", 0, 1))
+    dma("G", A("coli", 8, 9), A("th", 0, 1))
+    dma("G", A("coli", 16, 19), A("dw", 0, 3))
+    io(A("mask", 0, C), [[1, 16], [0, 12]], 0, 0)
+    ZERO = A("zero", 0, 128)
+    ms(ZERO, 0.0)
+    for w in WTS:
+        sel(Iw(w), ZERO, [[1, 128]], w, 0, -1)
+    sel(A("cm", 0, 128), ZERO, [[0, 128]], 129.0 * 2048, 0, 1)
+    sel(A("cm", 128, 256), A("cm", 0, 128), [[0, 128]], 1.0, -1, 1)
+    for a in range(16):
+        sel(blk("Rall", a), Iw(-1.0), [[16, 8], [0, 16]], 1.0, a, -1)
+    ts(A("colj", 1, 2), A("colj", 0, 1), 112, None, "bitwise_and")
+    ts(A("colj", 2, 3), A("colj", 0, 1), 15, None, "bitwise_and")
+    GP, KC, KH, K37, K512, K16, H1, H2, THC, DN = 0, 1, 2, 3, 4, 5, 6, 7, 8, 9
+    cp(A("colf", 0, 2), A("colj", 1, 3))
+    ts(cf(KH), cf(KC), -0.5, None, "mult")
+    ts(cf(K37), cf(KC), 37.0, None, "mult")
+    ts(cf(K512), cf(KC), float(NP), None, "add")
+    ts(cf(K16), cf(KC), 16.0, None, "mult")
+    cp(cf(H1), A("coli", 0, 1))
+    ts(cf(H2), A("coli", 0, 1), 2.0, None, "mult")
+    ts(cf(THC), A("coli", 8, 9), 0.5, None, "add")
+    ts(A("colf", DN, DN + 3), A("coli", 16, 19), -0.03125, None, "mult")
+    ts(A("Sall", 0, 2048), A("ioa", 0, 2048), cf(GP), 0.5, "is_equal", "mult")
+    ts(A("Hall", 0, 2048), A("ioa", 0, 2048), cf(GP), cf(H1), "is_equal", "mult")
+    BD, HB, LO, UP, SHF = 0, 1, 2, 3, 4
+    ts(mat(BD), A("ioc", 128, 256), cf(GP), None, "is_equal")
+    ts(mat(HB), A("ioc", 128, 256), cf(GP), cf(H2), "is_equal", "mult")
+    ts(mat(5), A("ioc", 0, 128), 0.0, -0.5, "is_ge", "mult")
+    ts(mat(6), A("ioc", 0, 128), 0.0, 0.5, "is_le", "mult")
+    ts(mat(7), A("ioc", 0, 128), -1.0, None, "is_equal")
+    for j in range(3):
+        tt(mat(LO + j), mat(5 + j), mat(BD), "mult")
+    for t in range(ST):
+        ts(blk("Dg", t), A("ioc", 0, 128), 0.0, cf(DN + t), "is_equal", "mult")
+    ONE = A("ones", 0, C)
+    ms(ONE, 1.0)
+    ms(A("turn7", C, 2 * C), 7.5)
+    ts(A("base", 0, 24), A("base", 0, 24), cf(K16), None, "add")
+    ts(A("mask", 0, C), A("mask", 0, C), cf(KC), 0.5, "is_ge", "mult")
+    ms(A("W", NP, NP + 16), 0.0)
+    ms(A("soff", 0, 48), 0)
+    act(A("ytmp", 0, NP), A("y0s", 0, NP), "Identity", 129.0 * 16384, 16384.0)
+    tt(A("W", 0, NP), A("ytmp", 0, NP), A("k0s", 0, NP), "add")
+    for c in range(2):
+        ms(A("VE%d" % c, 0, 8), 0.0)
+        ts(A("rn0%d" % c, 0, C), A("t0s", c * C, (c + 1) * C), NM - 1, None, "bitwise_and")
+        cp(A("ru0%d" % c, 0, C), A("rn0%d" % c, 0, C))
+        ts(A("rb0%d" % c, C, 2 * C), A("t0s", c * C, (c + 1) * C), float(NM), None, "is_ge")
+        ms(A("rb0%d" % c, 2 * C, 3 * C), -1.0)
+    for j in range(NM // 512):
+        lo, hi = 512 * j, 512 * j + 512
+        if j % 2 == 0: ts(A("E16", lo, lo + FXP), A("F", lo, lo + FXP), 2056.5, None, "add")
+        pb = A("ps%d" % (j % 8), 0, 512)
+        lin(pb, [(1.0, A("F", lo, hi)), (-1.0, A("E16", lo, hi))])
+        if j % 4 in S_EVAC_G: act(A("Gt", lo, hi), pb, "Identity", 2064.0)
+        else: ts(A("Gt", lo, hi), pb, 2064.0, None, "add")
+    for j in range(NM // FXP):
+        lo, hi = FXP * j, FXP * j + FXP
+        ts(A("Zt", lo, hi), A("F", lo, hi), 16.0, -1056.0, "is_lt", "mult")
+    for j in range(NM // 512):
+        lo, hi = 512 * j, 512 * j + 512
+        pb = A("ps%d" % (j % 4 + 4), 0, 512)
+        lin(pb, [(1.0, A("Zt", lo, hi)), (1.0, A("E16", lo, hi))])
+        if j % 4 in S_EVAC: act(A("Zt", lo, hi), pb, "Identity")
+        else: cp(A("Zt", lo, hi), pb)
+
+    arr = [0]
+    for t in range(ST):
+        for c in range(2):
+            cs_ = str(c)
+            def B(j): return A("b" + cs_, j * C, (j + 1) * C)
+            def Fl(j): return A("f" + cs_, j * C, (j + 1) * C)
+            def In(j): return A("i" + cs_, j * C, (j + 1) * C)
+            def ps(k, j, n=1): return A("ps%d" % (4 * c + k), j * C, (j + n) * C)
+            def tf(lo, hi): return A("tf" + cs_, lo, hi)
+            rb, sb = "rb%d%d" % (t, c), "sb%d%d" % (t, c)
+            x, s, hp = A(rb, 0, C), A(rb, C, 2 * C), A(rb, 2 * C, 3 * C)
+            xn, s6, hs = A(sb, 0, C), A(sb, C, 2 * C), A(sb, 2 * C, 3 * C)
+            n32, nn32, nn16 = A("rn%d%d" % (t, c), 0, C), A("sn%d%d" % (t, c), 0, C), A("su%d%d" % (t, c), 0, C)
+            VG, VE, ca, cb = "VG" + cs_, "VE" + cs_, "ca" + cs_, "cb" + cs_
+            cand, Aa, Bb, e, sx, se, sg, ap_, pre, asl, yc, ad, hy, nv, adk, hv, hn, g1, rr, ur = [B(j) for j in range(20)]
+            for j in range(C // PIECE):
+                off = A("ru%d%d" % (t, c), j * PIECE, (j + 1) * PIECE)
+                o = A(VG, 16 * j * PIECE, 16 * (j + 1) * PIECE)
+                if j in V_GATHERS: cp(o, IND(A("Gt", 0, NM), off))
+                else: act(o, IND(A("Gt", 0, NM), off), "Identity")
+            for j in range(C // PIECE):
+                off = A("ru%d%d" % (t, c), j * PIECE, (j + 1) * PIECE)
+                act(A(VE, 8 + 16 * j * PIECE, 8 + 16 * (j + 1) * PIECE), IND(A("Zt", 0, NM), off), "Identity", -129.0 * TP - CB, TP / 16)
+            for h in range(2):
+                lin(A("ps%d" % (4 * c), h, 2 * C, 2), [(1.0, x)])
+            for k in range(8):
+                tt(A(ca, 2 * k * C, 2 * (k + 1) * C), A(VG, k, 16 * C, 8), ps(0, 0, 2), "is_le")
+            lin(ps(1, 0), [(-16.0, s), (-0.25, hp)] + [(blk("Sall", k + 8 * h), A(ca, 2 * k * C + h, 2 * (k + 1) * C, 2))
+                                                       for k in range(8) for h in range(2)])
+            act(cand, ps(1, 0), "Sign", -4.5)
+            lin(ps(1, 0), [(1.0, A("turn7", 0, C)), (mat(LO), cand)])
+            lin(ps(1, 1), [(1.0, A("turn7", C, 2 * C)), (mat(UP), cand)])
+            act(A("b" + cs_, C, 3 * C), ps(1, 0, 2), "Sign", cf(KH))
+            pd = "ps%d" % (4 * c + 2)
+            lin(A(pd, 0, 24), [(blk("Sall", a), A("b" + cs_, C + a, 3 * C, 16)) for a in range(16)])
+            tt(tf(0, 24), A(pd, 0, 24), A("base", 0, 24), "add")
+            act(tf(24, 36), A(pd, 12, 24), "Identity", 7.5 * 16384, 16384.0)
+            tt(tf(36, 48), tf(0, 12), tf(12, 24), "min")
+            tt(tf(48, 60), tf(36, 48), tf(24, 36), "min")
+            cp(A("tu" + cs_, 0, 12), tf(48, 60))
+            lin(ps(3, 0), [(1.0, cand), (1.0, Aa), (mat(SHF), Bb), (6.0, s)])
+            act(pre, ps(3, 0), "Sign", -2.5)
+            act(e, IND(A(VE, 0, 16 * C + 8), A("tu" + cs_, 0, 12)), "Relu", CB / TP, 1.0 / TP)
+            ts(sx, x, 0.0, None, "is_gt")
+            ts(se, e, 0.0, None, "is_gt")
+            lin(ps(2, 0), [(1.0, x), (-1.0, e)])
+            act(sg, ps(2, 0), "Sign", 0.5)
+            act(xn, ps(2, 0), "Abs")
+            lin(ps(3, 1), [(0.0625, x), (-0.9375, sx), (-0.9375, se)])
+            act(Fl(0), ps(3, 1), "Identity", -16384.0 - 8.0 + 30.5 / 16 - CB)
+            lin(ps(0, 0), [(32768.0, sx), (512.0, e), (0.0625, e), (-16384.0, sg)])
+            tt(ps(0, 0), Fl(0), ps(0, 0), "max")
+            for k in range(16):
+                tt(A(cb, k * C, (k + 1) * C), A(VE, 8 + k, 8 + 16 * C, 16), ps(0, 0), "subtract")
+            lin(ps(1, 0), [(-60.0, ONE)] + [(blk("Sall", k), A(cb, k * C, (k + 1) * C)) for k in range(16)])
+            pu = A("ps%d" % (4 * c + 3), 2 * C, 2 * C + 12)
+            lin(pu, [(blk("Hall", a), A(sb, a, C, 16)) for a in range(16)])
+            ts(A("ti" + cs_, 0, 12), pu, 241.0, None, "mult")
+            cint = A("cint", 12 * c, 12 * c + 12)
+            ts(cint, A("ti" + cs_, 0, 12), 6, NP - 1, "arith_shift_right", "bitwise_and")
+            cp(A("tu" + cs_, 16, 28), cint)
+            cp(A("cf", 12 * c, 12 * c + 12), cint)
+            lin(ps(2, 1), [(mat(HB), xn)])
+            act(rr, ps(2, 1), "Identity", 128.5 + 1.0 / 2048, 1.0 / 2048)
+            act(Fl(1), IND(A("W", 0, NP + 16), A("tu" + cs_, 16, 28)), "Identity")
+            act(yc, Fl(1), "Identity", -0.25, 1.0 / 16384)
+            lin(ps(2, 0), [(-1.0, xn), (1.0, yc)])
+            act(ad, ps(2, 0), "Abs", -129.0)
+            lin(ps(2, 1), [(mat(BD), ad)])
+            act(hs, ps(2, 1), "Sign", cf(THC), -1.0)
+            lin(ps(3, 0), [(16384.0, yc)])
+            tt(ps(3, 0), Fl(1), ps(3, 0), "subtract")
+            act(nv, ps(3, 0), "Relu", -8191.0)
+            tt(Fl(2), ps(3, 0), n32, "subtract")
+            act(adk, Fl(2), "Abs")
+            lin(ps(2, 0), [(-1.0, xn), (1.0, yc), (16.0, hs)])
+            act(hy, ps(2, 0), "Relu", -129.0)
+            lin(ps(3, 1), [(0.5, hs), (-1.0, nv)])
+            act(hv, ps(3, 1), "Relu", 0.5)
+            lin(ps(3, 0), [(1.0, hv)])
+            tt(ps(3, 0), Fl(2), ps(3, 0), "mult")
+            tt(ps(3, 0), n32, ps(3, 0), "add")
+            p3, Eq, dd = "ps%d" % (4 * c + 3), A("Eq", c * C, (c + 1) * C), 24 * c
+            for a in range(16):
+                lin(A(p3, C + 12 * a, C + 12 * a + 12), [(blk("Rall", a), A("cf", 12 * c, 12 * c + 12))])
+            tt(Eq, ps(3, 1), A("mask", 0, C), "is_equal")
+            lin(A(p3, 400, 412), [(blk("Sall", a), A("Eq", c * C + 12 * a, c * C + 12 * a + 12)) for a in range(16)])
+            ts(A("dd", dd, dd + 12), A(p3, 400, 412), 0.0, 4096.0, "is_gt", "mult")
+            tt(A("dd", dd + 12, dd + 24), A("dd", dd, dd + 12), cint, "add")
+            ts(A("soff", dd, dd + 24, 2), A("dd", dd + 12, dd + 24), cf(K512), None, "min")
+            lin(ps(2, 0), [(16384.0, hs), (1.0, adk)])
+            lin(ps(2, 1), [(16384.0, hv), (1.0, adk)])
+            act(A("b" + cs_, 16 * C, 18 * C), ps(2, 0, 2), "Sign", -16384.5)
+            lin(ps(2, 1), [(A("cm", 128, 256), ONE), (mat(HB), xn), (-2048.0, rr)])
+            lin(ps(2, 0), [(243.0 * 8192, ONE), (16384.0, xn), (-131072.0, hs), (16384.0, hy)])
+            ts(Fl(3), ps(1, 0), MAGIC, MAGIC, "add", "subtract")
+            tt(Fl(4), ps(1, 0), Fl(3), "subtract")
+            act(ap_, Fl(4), "Identity", 135.5, 0.125)
+            lin(ps(0, 0), [(blk("Dg", t), ONE), (-1088.0, pre), (8.0, ap_), (0.03125, ap_)])
+            tt(asl, Fl(4), ps(0, 0), "is_gt")
+            lin(ps(1, 0), [(-1.0, hv), (-1.0, asl)])
+            act(ur, ps(1, 0), "Relu", 1.0)
+            act(Fl(5), ps(1, 0), "Relu", cf(K37), cf(K37))
+            tt(ps(2, 1), ur, ps(2, 1), "mult")
+            tt(In(2), n32, ps(2, 1), "mult")
+            ts(In(3), In(2), 5, NM - 1, "arith_shift_right", "bitwise_and")
+            lin(ps(0, 1), [(-0.5, g1), (1.0, asl)])
+            act(s6, ps(0, 1), "Relu", -0.5)
+            tt(ps(3, 0), Fl(5), ps(3, 0), "add")
+            tt(In(4), In(3), ps(3, 0), "add")
+            ts(nn32, In(4), NM - 1, None, "bitwise_and")
+            if t < ST - 1:
+                cp(nn16, nn32)
+                for p_, w_ in (("b", 3 * C), ("n", C), ("u", C)):
+                    ops.append(("G", "send", None, [A("s%s%d%d" % (p_, t, c), 0, w_)], ("r%s%d%d" % (p_, t + 1, c), arr[0])))
+                    ops.append(("R", "recv", A("r%s%d%d" % (p_, t + 1, c), 0, w_), [], arr[0]))
+                    arr[0] += 1
+            else:
+                lin(ps(0, 0), [(8192.0, s6)])
+                tt(A("oyt", c * C, (c + 1) * C), nn32, ps(0, 0), "add")
+                dma("Y", A("yt", c * C, (c + 1) * C), A("oyt", c * C, (c + 1) * C))
+                dma("Y", A("yx", c * C, (c + 1) * C), xn)
+            lin(ps(3, 1), [(245.0 * 8192, ONE), (8192.0, hn), (16384.0, xn), (-131072.0, hs), (16384.0, hy), (-16384.0, asl)])
+            tt(Fl(6), n32, ps(3, 1), "add")
+            tt(A("ent", c * C, (c + 1) * C), Fl(6), ps(2, 0), "min")
+        for b in range(24):
+            cp(IND(A("W", 0, NP + 16), A("soff", 2 * b, 2 * b + 1)), A("ent", 16 * b, 16 * b + 16))
+    for j, lo in enumerate(range(0, NP, C)):
+        hi = min(NP, lo + C)
+        act(A("oy1", lo, hi), A("W", lo, hi), "Identity", -0.25, 1.0 / 16384)
+        lin(A("ps%d" % j, 0, hi - lo), [(16384.0, A("oy1", lo, hi))])
+        tt(A("oyk", lo, hi), A("W", lo, hi), A("ps%d" % j, 0, hi - lo), "subtract")
+    dma("Y", A("yk", 0, NP), A("oyk", 0, NP))
+    act(A("oy2", 0, NP), A("oy1", 0, NP), "Identity", -129.0)
+    dma("Y", A("yy", 0, NP), A("oy2", 0, NP))
+    return ops
+
+
+def regions(op):
+    rd, wr = [], []
+    for a in op[3]:
+        if isinstance(a, tuple):
+            rd += [a[1], a[2]] if a[0] == "@" else [a]
+    o = op[2]
+    if o is not None:
+        if o[0] == "@":
+            wr.append(o[1]); rd.append(o[2])
+        else:
+            wr.append(o)
+    return [r for r in rd if r[0] not in DRAM], [r for r in wr if r[0] not in DRAM]
+
+
+SC = {"gather": 1.56, "scatter": 3.8, "call": 40, "pe": 0.5, "lat": 60, "bw": 250.0, "link": 2500}
+
+
+def cost(op, sc=SC):
+    q, kind, o, ins, par = op
+    if kind == "mm":
+        d = 20 + sc["pe"] * max(64, count(o)); return d, d + sc["lat"]
+    if kind == "dma":
+        return 100, 2000 + count(o) * 128 * (2 if narrow(o) or narrow(ins[0]) else 4) / sc["bw"]
+    if kind == "send": return 500, 500
+    if kind == "recv": return 0, sc["link"]
+    n = count(o)
+    if kind in ("iota", "sel"): d = 170 + 2 * n
+    elif o[0] == "@": d = 60 + sc["scatter"] * n
+    elif ins and ins[0][0] == "@": d = 70 + sc["gather"] * n
+    elif kind == "act": d = 20 + sc["call"] + max(64, n)
+    elif kind == "tt":
+        d = sc["call"] + max(64, n * (1 if "ps" in (ins[0][0][:2], ins[1][0][:2]) else 1.5 if narrow(o) else 2))
+    else: d = sc["call"] + max(64, n * (0.5 if narrow(o) and (not ins or narrow(ins[0])) else 1))
+    return d, d + sc["lat"]
+
+
+def links():
+    ops = describe()
+    n = len(ops)
+    hard = [set() for _ in range(n)]
+    soft = [set() for _ in range(n)]
+    hist, bank, sends = {}, {}, {}
+    for i, op in enumerate(ops):
+        rd, wr = regions(op)
+        for r, isw in [(r, False) for r in rd] + [(r, True) for r in wr]:
+            for j, lo, hi, w in hist.get(r[0], []):
+                if j != i and (w or isw) and lo < r[2] and r[1] < hi:
+                    (soft if op[0] == "P" and ops[j][0] == "P" else hard)[i].add(j)
+            if r[0][:2] == "ps":
+                j = bank.get(r[0])
+                if j is not None and j != i:
+                    (soft if ops[j][0] == op[0] else hard)[i].add(j)
+                bank[r[0]] = i
+        for r in wr:
+            hist[r[0]] = [h for h in hist.get(r[0], []) if not (r[3] == 1 and r[1] <= h[1] and h[2] <= r[2])] + [(i, r[1], r[2], True)]
+        for r in rd:
+            hist.setdefault(r[0], []).append((i, r[1], r[2], False))
+        if op[1] == "send": sends[op[4][1]] = i
+        if op[1] == "recv": soft[i].add(sends[op[4]])
+    lead = [i for i, op in enumerate(ops) if op[1] == "sel"][1]
+    for i, op in enumerate(ops):
+        if op[0] == "G" and not (op[1] == "sel" and i <= lead): soft[i].add(lead)
+    kinds, cls = {}, []
+    for op in ops:
+        o = op[2] or op[3][0]
+        o = o[1] if o[0] == "@" else o
+        name = o[0][:2] + o[0][3:] if o[0][:2] in ("rb", "rn", "ru", "sb", "sn", "su") else o[0]
+        whole = name[:2] in ("ca", "cb", "Gt", "Zt", "E1", "Iw", "Ra", "F", "co", "ma", "Dg") or name[:2] == "ps" and o[2] - o[1] == 12
+        cls.append(kinds.setdefault((op[0], op[1], name, 0 if whole else o[1]), len(kinds)))
+    return ops, hard, soft, cls
+
+
+def plan(shift=None, window=30, base=None):
+    ops, hard, soft, cls = base or links()
+    shift = shift or SHIFT
+    n = len(ops)
+    cst = [cost(op) for op in ops]
+    users = [[] for _ in range(n)]
+    for i in range(n):
+        for j in hard[i] | soft[i]: users[j].append(i)
+    prio = [0.0] * n
+    for i in range(n - 1, -1, -1):
+        prio[i] = cst[i][1] + max([prio[u] for u in users[i]] + [0.0])
+    for i in range(n):
+        prio[i] += 500.0 * shift.get(cls[i], 0)
+        o = ops[i][2] or ops[i][3][0]
+        name = o[1][0] if o[0] == "@" else o[0]
+        if name[-1] == "0" and name[:2] != "ps" or name in ("ps0", "ps1", "ps2", "ps3"): prio[i] += LEAD
+        if ops[i][1] in ("act", "cp") and ops[i][3][0][0] == "@" and count(o) > C: prio[i] -= LATE
+        if name == "zero" or name == "Iw" and o[1] < 256: prio[i] += 1e6
+    left = [len(hard[i] | soft[i]) for i in range(n)]
+    ready = [i for i in range(n) if left[i] == 0]
+    at = [0.0] * n
+    start = [0.0] * n
+    free = {q: 0.0 for q in "VSPGYR"}
+    dmafree = [0.0]
+    order = []
+    while ready:
+        first = min(max(at[i], free[ops[i][0]]) for i in ready)
+        i = max((i for i in ready if max(at[i], free[ops[i][0]]) <= first + window), key=lambda k: (prio[k], -k))
+        ready.remove(i)
+        q = ops[i][0]
+        start[i] = max(at[i], free[q]); free[q] = start[i] + cst[i][0]
+        end = start[i] + cst[i][1]
+        if ops[i][1] == "dma":
+            dmafree[0] = max(dmafree[0], start[i] + 2000) + cst[i][1] - 2000
+            end = dmafree[0]
+        order.append(i)
+        for u in users[i]:
+            at[u] = max(at[u], end + 40 if i in hard[u] else start[i] + cst[i][0])
+            left[u] -= 1
+            if left[u] == 0: ready.append(u)
+    needed = set()
+    for i in range(n): needed |= hard[i]
+    return ops, hard, order, needed, start, soft
+
+
+PLAN = []
+
+
+def rank_program(g, core, T, topo):
+    rank = T.rank_of(core)
+    if rank is None:
+        return
+    if not PLAN:
+        PLAN.append(plan())
+    ops, hard, order, needed = PLAN[0][:4]
+    dst = T.cores[(rank + SH) % NR]
+    src = T.cores[(rank - SH) % NR]
+    rid, pid, _e = topo.addr(dst)
+    nout, nin = len(topo.engines(core, dst)), len(topo.engines(src, core))
+    queue = {"V": g.vector, "S": g.scalar, "P": g.tensor, "G": g, "Y": g.sync}
+    alu = {"add": AluOpType.add, "subtract": AluOpType.subtract, "mult": AluOpType.mult, "max": AluOpType.max, "min": AluOpType.min,
+           "is_ge": AluOpType.is_ge, "is_gt": AluOpType.is_gt, "is_le": AluOpType.is_le, "is_lt": AluOpType.is_lt,
+           "is_equal": AluOpType.is_equal, "not_equal": AluOpType.not_equal, "bitwise_and": AluOpType.bitwise_and,
+           "arith_shift_right": AluOpType.arith_shift_right}
+    fun = {"Identity": ActivationFunctionType.Identity, "Sign": ActivationFunctionType.Sign, "Relu": ActivationFunctionType.Relu,
+           "Abs": ActivationFunctionType.Abs}
+
+    def ap(a):
+        if not isinstance(a, tuple): return a
+        if a[0] == "@": return ap(a[1]).indirect(ap(a[2]))
+        return T[a[0]][:, a[1]:a[2]] if a[3] == 1 else T[a[0]][:, a[1]:a[2]:a[3]]
+
+    mark, total, seen, ndma = {}, {}, {}, [0]
+
+    def wait(q, name, val):
+        if seen.get((q, name), 0) < val:
+            queue[q].wait_ge(T.sem[name], val)
+            seen[(q, name)] = val
+
+    for i in order:
+        q, kind, o, ins, par = ops[i]
+        if kind == "recv":
+            mark[i] = ("a%d" % par, nin); total["a%d" % par] = nin
+            continue
+        want = {}
+        for j in hard[i]:
+            want[mark[j][0]] = max(want.get(mark[j][0], 0), mark[j][1])
+        for name in sorted(want):
+            wait(q, name, want[name])
+        e = queue[q]
+        if kind == "send":
+            g.remote_dma(T[par[0]][:], ap(ins[0]), T.sem["a%d" % par[1]], T.sem.sent, pid, rid, topo.mask(core, dst))
+            total["sent"] = total.get("sent", 0) + nout
+            continue
+        if kind == "dma":
+            name = "d%d" % ndma[0]; ndma[0] += 1
+            if q == "G": ins_ = g.dma_start(ap(o), ap(ins[0]), allow_slow_non_contiguous=True)
+            else: ins_ = e.dma_start(ap(o), ap(ins[0]))
+            ins_.then_inc(T.sem[name], 16)
+            mark[i] = (name, 16); total[name] = 16
+            continue
+        if kind == "tt": ins_ = e.tensor_tensor(ap(o), ap(ins[0]), ap(ins[1]), alu[par])
+        elif kind == "ts" and par[1] is None: ins_ = e.tensor_scalar(ap(o), ap(ins[0]), ap(ins[1]), None, alu[par[0]])
+        elif kind == "ts": ins_ = e.tensor_scalar(ap(o), ap(ins[0]), ap(ins[1]), ap(ins[2]), alu[par[0]], alu[par[1]])
+        elif kind == "cp": ins_ = e.tensor_copy(ap(o), ap(ins[0]))
+        elif kind == "ms": ins_ = e.memset(ap(o), par)
+        elif kind == "act": ins_ = e.activation(ap(o), ap(ins[0]), fun[par], bias=ap(ins[1]), scale=ap(ins[2]))
+        elif kind == "mm": ins_ = e.matmul(ap(o), ap(ins[0]), ap(ins[1]), par[0], par[1])
+        elif kind == "sel": ins_ = g.affine_select(ap(o), ap(ins[0]), par[0], AluOpType.not_equal, par[3], par[1], par[2])
+        elif SCRATCH[o[0]][2] == "int32": ins_ = g.iota(ap(o), par[0], par[1], par[2])
+        else: ins_ = g.iota(ap(o), par[0], par[1], par[2], allow_small_or_imprecise_dtypes=True)
+        if i in needed:
+            total[q] = total.get(q, 0) + 1
+            ins_.then_inc(T.sem[q], 1)
+            mark[i] = (q, total[q])
+    for name in sorted(total):
+        wait("G", name, total[name])

@@ -1,19 +1,23 @@
+from concourse.bass import DstId, RemoteDMATransfer
 from concourse.mybir import AluOpType, ActivationFunctionType
 
 NM, NP, NW, ST, SH, NR = 8192, 512, 384, 3, 3, 8
 C = 192
-PIECE = 48
+NCH, D, R1 = NW // C, C // 16, 512 // C
+PIECE = C // 4
+SPANS = []
 FXP = 1024
-V_GATHERS = (3,)
+V_GATHERS = (2, 3)
 S_EVAC = (1, 3)
 S_EVAC_G = (0, 1, 2, 3)
+OPT = 0
 TP = 512.0625
 CB = -0.0625 - 16.0 - 49152.0
 MAGIC = 1.5 * 2.0 ** 31
 WTS = [1.0, -1.0, -16.0, -0.25, 6.0, 0.0625, -0.9375, 512.0, 32768.0, -16384.0, -60.0, 8.0, 0.03125, -1088.0, 16384.0,
        16.0, 0.5, -0.5, 8192.0, 245.0 * 8192, 243.0 * 8192, -131072.0, -2048.0]
-LEAD, LATE = 5000, 10000
-SHIFT = {0:1,1:4,4:1,7:-8,8:-32,9:-16,10:-16,11:-3,14:-16,15:-16,16:-24,17:-16,18:-16,19:-12,20:-16,21:-16,24:12,25:12,26:-4,27:-4,28:-6,29:-18,30:-2,31:-2,32:14,33:2,34:2,35:11,36:10,37:2,38:2,39:-16,41:-2,42:12,43:8,44:8,45:8,46:24,49:-4,50:-4,51:-3,55:5,56:-3,57:-4,58:-4,59:-4,60:-4,61:-2,63:-8,65:4,66:-4,67:-16,71:-8,72:-6,73:-6,74:2,75:2,76:2,78:-4,79:-2,84:4,87:2,90:16,94:-8,98:-16,99:-16,103:-16,110:-8,111:-8,114:1,115:-9,116:-5,117:-3,118:-3,119:-3,120:-3,121:-3,122:-3,123:-5,128:2,137:-4,149:8,151:-2,155:2,156:-2,157:-6,158:-14,159:-14,160:-14,161:2,162:2,163:-14,164:2,165:2,166:2,167:2,168:16,171:-2,172:-2,173:6,174:6,175:-1,176:6,177:6,178:6,179:6,180:6,181:-2,183:-8,185:4,187:-4,192:-1,193:-1,194:-1,195:-1,196:-1,197:3,198:3,199:-5,200:4,201:-13,202:3,203:8,204:4,205:4,206:8,207:4,208:-12,213:-16}
+LEAD, LATE = 2000, 5000
+SHIFT = {0:4,3:16,4:-4,7:-8,8:-16,9:-12,10:-24,11:-4,12:-20,13:-22,14:-16,15:-15,16:-15,17:9,18:-1,19:1,20:2,21:2,23:-1,24:3,25:-1,29:-2,36:-2,37:-4,38:28,39:-4,40:-4,41:-4,42:-4,43:-4,44:-4,48:2,57:-4,59:8,60:8,65:-4,70:4,71:-1,73:20,74:16,75:16,76:16,77:16,78:16,79:16,80:16,82:-8,83:-1,89:-2,90:-5,91:8,93:1,95:1,96:17,98:-8,99:-8,100:-4,102:8,104:16,105:-1,106:-1,107:-1,108:-1,109:-1,110:15,111:-5,116:16,120:-4,126:-14,129:4,131:1,132:-2,134:-3,135:-2,136:-2,139:-8,141:1,142:-2,143:-4,154:-20,155:-4,156:-4,157:-8,158:4,159:-4,160:-8,161:-4,163:7,164:-1,179:8,180:-4,191:4,201:16,202:-2,203:-2,204:-2,205:-18,206:-2,207:-10,208:-2,209:-2,210:-2,211:-4,212:1,213:-2,214:8,215:-8,216:-8,217:-8,218:-8,219:8}
 
 SCRATCH = {}
 for _n, _w, _d in [
@@ -26,7 +30,7 @@ for _n, _w, _d in [
         ("ent", NW, "float32"), ("cf", 24, "float16"), ("cint", 24, "int32"), ("Eq", NW, "bfloat16"), ("dd", 48, "float32"),
         ("soff", 48, "uint16"), ("oyt", NW, "float32"), ("oy1", NP, "bfloat16"), ("oy2", NP, "bfloat16"), ("oyk", NP, "float32")]:
     SCRATCH[_n] = ("sbuf", [128, _w], _d)
-for _c in range(2):
+for _c in range(NCH):
     for _n, _w, _d in [("VG", 16 * C, "bfloat16"), ("VE", 16 * C + 8, "float32"), ("ca", 16 * C, "bfloat16"), ("cb", 16 * C, "float16"),
                        ("b", 20 * C, "bfloat16"), ("f", 8 * C, "float32"), ("i", 5 * C, "int32"), ("tf", 64, "float32"),
                        ("ti", 16, "int32"), ("tu", 32, "uint16")]:
@@ -39,8 +43,8 @@ for _c in range(2):
 for _k in range(8):
     SCRATCH["ps%d" % _k] = ("psum", [128, 512], "float32")
 DRAM = ("fx", "y0", "k0", "x0", "t0", "dw", "hw", "th", "yx", "yt", "yy", "yk")
-NDMA = NM // FXP + 14
-SEMAPHORES = ["V", "S", "P", "G", "sent"] + ["d%d" % _k for _k in range(NDMA)] + ["a%d" % _k for _k in range(12)]
+NDMA = NM // FXP + 8 + 3 * NCH
+SEMAPHORES = ["V", "S", "P", "G", "sent"] + ["d%d" % _k for _k in range(NDMA)] + ["a%d" % _k for _k in range(8 * NCH)]
 
 
 def A(name, lo, hi, step=1):
@@ -85,7 +89,7 @@ def describe():
     dma("Y", A("t0s", 0, NW), A("t0", 0, NW))
     for j in range(1, NM // FXP):
         dma("Y", A("F", j * FXP, (j + 1) * FXP), A("fx", j * FXP, (j + 1) * FXP))
-    for c in range(2):
+    for c in range(NCH):
         dma("Y", A("rb0%d" % c, 0, C), A("x0", c * C, (c + 1) * C))
     dma("Y", A("y0s", 0, NP), A("y0", 0, NP))
     dma("Y", A("k0s", 0, NP), A("k0", 0, NP))
@@ -94,11 +98,11 @@ def describe():
     io(A("ioa", 0, 2048), [[-1, 16], [1, 128]], 0, 0)
     io(A("ioc", 128, 256), [[16, 8], [0, 16]], 0, 0)
     io(A("turn7", 0, C), [[0, C // 4], [1, 4]], 0, 0)
-    io(A("base", 0, 24), [[-1, 2], [256, 12]], 16, 0)
+    io(A("base", 0, 2 * D), [[-1, 2], [256, D]], 16, 0)
     dma("G", A("coli", 0, 1), A("hw", 0, 1))
     dma("G", A("coli", 8, 9), A("th", 0, 1))
     dma("G", A("coli", 16, 19), A("dw", 0, 3))
-    io(A("mask", 0, C), [[1, 16], [0, 12]], 0, 0)
+    io(A("mask", 0, C), [[1, 16], [0, D]], 0, 0)
     ZERO = A("zero", 0, 128)
     ms(ZERO, 0.0)
     for w in WTS:
@@ -120,7 +124,8 @@ def describe():
     ts(cf(THC), A("coli", 8, 9), 0.5, None, "add")
     ts(A("colf", DN, DN + 3), A("coli", 16, 19), -0.03125, None, "mult")
     ts(A("Sall", 0, 2048), A("ioa", 0, 2048), cf(GP), 0.5, "is_equal", "mult")
-    ts(A("Hall", 0, 2048), A("ioa", 0, 2048), cf(GP), cf(H1), "is_equal", "mult")
+    if OPT & 8: act(A("Hall", 0, 2048), A("Sall", 0, 2048), "Identity", 0.0, cf(H2))
+    else: ts(A("Hall", 0, 2048), A("ioa", 0, 2048), cf(GP), cf(H1), "is_equal", "mult")
     BD, HB, LO, UP, SHF = 0, 1, 2, 3, 4
     ts(mat(BD), A("ioc", 128, 256), cf(GP), None, "is_equal")
     ts(mat(HB), A("ioc", 128, 256), cf(GP), cf(H2), "is_equal", "mult")
@@ -134,18 +139,18 @@ def describe():
     ONE = A("ones", 0, C)
     ms(ONE, 1.0)
     ms(A("turn7", C, 2 * C), 7.5)
-    ts(A("base", 0, 24), A("base", 0, 24), cf(K16), None, "add")
+    ts(A("base", 0, 2 * D), A("base", 0, 2 * D), cf(K16), None, "add")
     ts(A("mask", 0, C), A("mask", 0, C), cf(KC), 0.5, "is_ge", "mult")
     ms(A("W", NP, NP + 16), 0.0)
     ms(A("soff", 0, 48), 0)
     act(A("ytmp", 0, NP), A("y0s", 0, NP), "Identity", 129.0 * 16384, 16384.0)
     tt(A("W", 0, NP), A("ytmp", 0, NP), A("k0s", 0, NP), "add")
-    for c in range(2):
+    for c in range(NCH):
         ms(A("VE%d" % c, 0, 8), 0.0)
         ts(A("rn0%d" % c, 0, C), A("t0s", c * C, (c + 1) * C), NM - 1, None, "bitwise_and")
         cp(A("ru0%d" % c, 0, C), A("rn0%d" % c, 0, C))
-        ts(A("rb0%d" % c, C, 2 * C), A("t0s", c * C, (c + 1) * C), float(NM), None, "is_ge")
-        ms(A("rb0%d" % c, 2 * C, 3 * C), -1.0)
+        ts(A("rb0%d" % c, 2 * C, 3 * C), A("t0s", c * C, (c + 1) * C), float(NM), None, "is_ge")
+        ms(A("rb0%d" % c, C, 2 * C), -1.0)
     for j in range(NM // 512):
         lo, hi = 512 * j, 512 * j + 512
         if j % 2 == 0: ts(A("E16", lo, lo + FXP), A("F", lo, lo + FXP), 2056.5, None, "add")
@@ -165,16 +170,17 @@ def describe():
 
     arr = [0]
     for t in range(ST):
-        for c in range(2):
-            cs_ = str(c)
+        for c in range(NCH):
+            cs_, first = str(c), len(ops)
             def B(j): return A("b" + cs_, j * C, (j + 1) * C)
             def Fl(j): return A("f" + cs_, j * C, (j + 1) * C)
             def In(j): return A("i" + cs_, j * C, (j + 1) * C)
-            def ps(k, j, n=1): return A("ps%d" % (4 * c + k), j * C, (j + n) * C)
+            def ps(k, j, n=1):
+                return A("ps%d" % (4 * c + k if NCH == 2 else 2 * c + k if k < 2 else 4 + k), j * C, (j + n) * C)
             def tf(lo, hi): return A("tf" + cs_, lo, hi)
             rb, sb = "rb%d%d" % (t, c), "sb%d%d" % (t, c)
-            x, s, hp = A(rb, 0, C), A(rb, C, 2 * C), A(rb, 2 * C, 3 * C)
-            xn, s6, hs = A(sb, 0, C), A(sb, C, 2 * C), A(sb, 2 * C, 3 * C)
+            x, hp, s = A(rb, 0, C), A(rb, C, 2 * C), A(rb, 2 * C, 3 * C)
+            xn, hs, s6 = A(sb, 0, C), A(sb, C, 2 * C), A(sb, 2 * C, 3 * C)
             n32, nn32, nn16 = A("rn%d%d" % (t, c), 0, C), A("sn%d%d" % (t, c), 0, C), A("su%d%d" % (t, c), 0, C)
             VG, VE, ca, cb = "VG" + cs_, "VE" + cs_, "ca" + cs_, "cb" + cs_
             cand, Aa, Bb, e, sx, se, sg, ap_, pre, asl, yc, ad, hy, nv, adk, hv, hn, g1, rr, ur = [B(j) for j in range(20)]
@@ -186,28 +192,30 @@ def describe():
             for j in range(C // PIECE):
                 off = A("ru%d%d" % (t, c), j * PIECE, (j + 1) * PIECE)
                 act(A(VE, 8 + 16 * j * PIECE, 8 + 16 * (j + 1) * PIECE), IND(A("Zt", 0, NM), off), "Identity", -129.0 * TP - CB, TP / 16)
-            for h in range(2):
-                lin(A("ps%d" % (4 * c), h, 2 * C, 2), [(1.0, x)])
-            for k in range(8):
-                tt(A(ca, 2 * k * C, 2 * (k + 1) * C), A(VG, k, 16 * C, 8), ps(0, 0, 2), "is_le")
-            lin(ps(1, 0), [(-16.0, s), (-0.25, hp)] + [(blk("Sall", k + 8 * h), A(ca, 2 * k * C + h, 2 * (k + 1) * C, 2))
-                                                       for k in range(8) for h in range(2)])
+            for h in range(R1):
+                lin(A(ps(0, 0)[0], h, R1 * C, R1), [(1.0, x)])
+            for k in range(16 // R1):
+                tt(A(ca, R1 * k * C, R1 * (k + 1) * C), A(VG, k, 16 * C, 16 // R1), ps(0, 0, R1), "is_le")
+            lin(ps(1, 0), [(-16.0, s), (-0.25, hp)] + [(blk("Sall", k + 16 // R1 * h), A(ca, R1 * k * C + h, R1 * (k + 1) * C, R1))
+                                                       for k in range(16 // R1) for h in range(R1)])
             act(cand, ps(1, 0), "Sign", -4.5)
             lin(ps(1, 0), [(1.0, A("turn7", 0, C)), (mat(LO), cand)])
             lin(ps(1, 1), [(1.0, A("turn7", C, 2 * C)), (mat(UP), cand)])
             act(A("b" + cs_, C, 3 * C), ps(1, 0, 2), "Sign", cf(KH))
-            pd = "ps%d" % (4 * c + 2)
-            lin(A(pd, 0, 24), [(blk("Sall", a), A("b" + cs_, C + a, 3 * C, 16)) for a in range(16)])
-            tt(tf(0, 24), A(pd, 0, 24), A("base", 0, 24), "add")
-            act(tf(24, 36), A(pd, 12, 24), "Identity", 7.5 * 16384, 16384.0)
-            tt(tf(36, 48), tf(0, 12), tf(12, 24), "min")
-            tt(tf(48, 60), tf(36, 48), tf(24, 36), "min")
-            cp(A("tu" + cs_, 0, 12), tf(48, 60))
+            pd = ps(2, 0)[0]
+            lin(A(pd, 2 * C, 2 * C + 2 * D), [(blk("Sall", a), A("b" + cs_, C + a, 3 * C, 16)) for a in range(16)])
+            tt(tf(0, 2 * D), A(pd, 2 * C, 2 * C + 2 * D), A("base", 0, 2 * D), "add")
+            act(tf(2 * D, 3 * D), A(pd, 2 * C + D, 2 * C + 2 * D), "Identity", 7.5 * 16384, 16384.0)
+            tt(tf(3 * D, 4 * D), tf(0, D), tf(D, 2 * D), "min")
+            tt(tf(4 * D, 5 * D), tf(3 * D, 4 * D), tf(2 * D, 3 * D), "min")
+            cp(A("tu" + cs_, 0, D), tf(4 * D, 5 * D))
             lin(ps(3, 0), [(1.0, cand), (1.0, Aa), (mat(SHF), Bb), (6.0, s)])
             act(pre, ps(3, 0), "Sign", -2.5)
-            act(e, IND(A(VE, 0, 16 * C + 8), A("tu" + cs_, 0, 12)), "Relu", CB / TP, 1.0 / TP)
-            ts(sx, x, 0.0, None, "is_gt")
-            ts(se, e, 0.0, None, "is_gt")
+            act(e, IND(A(VE, 0, 16 * C + 8), A("tu" + cs_, 0, D)), "Relu", CB / TP, 1.0 / TP)
+            if OPT & 1: act(sx, x, "Sign")
+            else: ts(sx, x, 0.0, None, "is_gt")
+            if OPT & 2: act(se, e, "Sign")
+            else: ts(se, e, 0.0, None, "is_gt")
             lin(ps(2, 0), [(1.0, x), (-1.0, e)])
             act(sg, ps(2, 0), "Sign", 0.5)
             act(xn, ps(2, 0), "Abs")
@@ -218,16 +226,17 @@ def describe():
             for k in range(16):
                 tt(A(cb, k * C, (k + 1) * C), A(VE, 8 + k, 8 + 16 * C, 16), ps(0, 0), "subtract")
             lin(ps(1, 0), [(-60.0, ONE)] + [(blk("Sall", k), A(cb, k * C, (k + 1) * C)) for k in range(16)])
-            pu = A("ps%d" % (4 * c + 3), 2 * C, 2 * C + 12)
+            p3 = ps(3, 0)[0]
+            pu = A(p3, 2 * C, 2 * C + D)
             lin(pu, [(blk("Hall", a), A(sb, a, C, 16)) for a in range(16)])
-            ts(A("ti" + cs_, 0, 12), pu, 241.0, None, "mult")
-            cint = A("cint", 12 * c, 12 * c + 12)
-            ts(cint, A("ti" + cs_, 0, 12), 6, NP - 1, "arith_shift_right", "bitwise_and")
-            cp(A("tu" + cs_, 16, 28), cint)
-            cp(A("cf", 12 * c, 12 * c + 12), cint)
+            ts(A("ti" + cs_, 0, D), pu, 241.0, None, "mult")
+            cint = A("cint", D * c, D * c + D)
+            ts(cint, A("ti" + cs_, 0, D), 6, NP - 1, "arith_shift_right", "bitwise_and")
+            cp(A("tu" + cs_, 16, 16 + D), cint)
+            cp(A("cf", D * c, D * c + D), cint)
             lin(ps(2, 1), [(mat(HB), xn)])
             act(rr, ps(2, 1), "Identity", 128.5 + 1.0 / 2048, 1.0 / 2048)
-            act(Fl(1), IND(A("W", 0, NP + 16), A("tu" + cs_, 16, 28)), "Identity")
+            act(Fl(1), IND(A("W", 0, NP + 16), A("tu" + cs_, 16, 16 + D)), "Identity")
             act(yc, Fl(1), "Identity", -0.25, 1.0 / 16384)
             lin(ps(2, 0), [(-1.0, xn), (1.0, yc)])
             act(ad, ps(2, 0), "Abs", -129.0)
@@ -244,21 +253,25 @@ def describe():
             act(hv, ps(3, 1), "Relu", 0.5)
             lin(ps(3, 0), [(1.0, hv)])
             tt(ps(3, 0), Fl(2), ps(3, 0), "mult")
-            tt(ps(3, 0), n32, ps(3, 0), "add")
-            p3, Eq, dd = "ps%d" % (4 * c + 3), A("Eq", c * C, (c + 1) * C), 24 * c
+            M1, MUL, PB, SL, PA = (ps(3, 0), ps(2, 1), ps(2, 0), ps(0, 1), ps(3, 1)) if NCH == 2 else (ps(0, 1), ps(0, 2), ps(0, 3), ps(1, 1), ps(1, 2))
+            tt(M1, n32, ps(3, 0), "add")
+            Eq, dd = A("Eq", c * C, (c + 1) * C), 2 * D * c
             for a in range(16):
-                lin(A(p3, C + 12 * a, C + 12 * a + 12), [(blk("Rall", a), A("cf", 12 * c, 12 * c + 12))])
+                lin(A(p3, C + D * a, C + D * a + D), [(blk("Rall", a), A("cf", D * c, D * c + D))])
             tt(Eq, ps(3, 1), A("mask", 0, C), "is_equal")
-            lin(A(p3, 400, 412), [(blk("Sall", a), A("Eq", c * C + 12 * a, c * C + 12 * a + 12)) for a in range(16)])
-            ts(A("dd", dd, dd + 12), A(p3, 400, 412), 0.0, 4096.0, "is_gt", "mult")
-            tt(A("dd", dd + 12, dd + 24), A("dd", dd, dd + 12), cint, "add")
-            ts(A("soff", dd, dd + 24, 2), A("dd", dd + 12, dd + 24), cf(K512), None, "min")
+            lin(A(p3, 400, 400 + D), [(blk("Sall", a), A("Eq", c * C + D * a, c * C + D * a + D)) for a in range(16)])
+            ts(A("dd", dd, dd + D), A(p3, 400, 400 + D), 0.0, 4096.0, "is_gt", "mult")
+            tt(A("dd", dd + D, dd + 2 * D), A("dd", dd, dd + D), cint, "add")
+            ts(A("soff", dd, dd + 2 * D, 2), A("dd", dd + D, dd + 2 * D), cf(K512), None, "min")
             lin(ps(2, 0), [(16384.0, hs), (1.0, adk)])
             lin(ps(2, 1), [(16384.0, hv), (1.0, adk)])
             act(A("b" + cs_, 16 * C, 18 * C), ps(2, 0, 2), "Sign", -16384.5)
-            lin(ps(2, 1), [(A("cm", 128, 256), ONE), (mat(HB), xn), (-2048.0, rr)])
-            lin(ps(2, 0), [(243.0 * 8192, ONE), (16384.0, xn), (-131072.0, hs), (16384.0, hy)])
-            ts(Fl(3), ps(1, 0), MAGIC, MAGIC, "add", "subtract")
+            lin(MUL, [(A("cm", 128, 256), ONE), (mat(HB), xn), (-2048.0, rr)])
+            lin(PB, [(243.0 * 8192, ONE), (16384.0, xn), (-131072.0, hs), (16384.0, hy)])
+            if OPT & 4:
+                act(Fl(7), ps(1, 0), "Identity", MAGIC)
+                act(Fl(3), Fl(7), "Identity", -MAGIC)
+            else: ts(Fl(3), ps(1, 0), MAGIC, MAGIC, "add", "subtract")
             tt(Fl(4), ps(1, 0), Fl(3), "subtract")
             act(ap_, Fl(4), "Identity", 135.5, 0.125)
             lin(ps(0, 0), [(blk("Dg", t), ONE), (-1088.0, pre), (8.0, ap_), (0.03125, ap_)])
@@ -266,28 +279,31 @@ def describe():
             lin(ps(1, 0), [(-1.0, hv), (-1.0, asl)])
             act(ur, ps(1, 0), "Relu", 1.0)
             act(Fl(5), ps(1, 0), "Relu", cf(K37), cf(K37))
-            tt(ps(2, 1), ur, ps(2, 1), "mult")
-            tt(In(2), n32, ps(2, 1), "mult")
+            tt(MUL, ur, MUL, "mult")
+            tt(In(2), n32, MUL, "mult")
             ts(In(3), In(2), 5, NM - 1, "arith_shift_right", "bitwise_and")
-            lin(ps(0, 1), [(-0.5, g1), (1.0, asl)])
-            act(s6, ps(0, 1), "Relu", -0.5)
-            tt(ps(3, 0), Fl(5), ps(3, 0), "add")
-            tt(In(4), In(3), ps(3, 0), "add")
+            lin(SL, [(-0.5, g1), (1.0, asl)])
+            act(s6, SL, "Relu", -0.5)
+            tt(M1, Fl(5), M1, "add")
+            tt(In(4), In(3), M1, "add")
             ts(nn32, In(4), NM - 1, None, "bitwise_and")
             if t < ST - 1:
                 cp(nn16, nn32)
-                for p_, w_ in (("b", 3 * C), ("n", C), ("u", C)):
-                    ops.append(("G", "send", None, [A("s%s%d%d" % (p_, t, c), 0, w_)], ("r%s%d%d" % (p_, t + 1, c), arr[0])))
-                    ops.append(("R", "recv", A("r%s%d%d" % (p_, t + 1, c), 0, w_), [], arr[0]))
-                    arr[0] += 1
+                for call in ([("b", 0, 2 * C)], [("u", 0, C), ("b", 2 * C, 3 * C)], [("n", 0, C)]):
+                    to = [A("r%s%d%d" % (p_, t + 1, c), lo, hi) for p_, lo, hi in call]
+                    ops.append(("G", "send", None, [A("s%s%d%d" % (p_, t, c), lo, hi) for p_, lo, hi in call], (to, arr[0])))
+                    for j, o in enumerate(to):
+                        ops.append(("R", "recv", o, [], (arr[0], j, len(to))))
+                    arr[0] += len(to)
             else:
                 lin(ps(0, 0), [(8192.0, s6)])
                 tt(A("oyt", c * C, (c + 1) * C), nn32, ps(0, 0), "add")
                 dma("Y", A("yt", c * C, (c + 1) * C), A("oyt", c * C, (c + 1) * C))
                 dma("Y", A("yx", c * C, (c + 1) * C), xn)
-            lin(ps(3, 1), [(245.0 * 8192, ONE), (8192.0, hn), (16384.0, xn), (-131072.0, hs), (16384.0, hy), (-16384.0, asl)])
-            tt(Fl(6), n32, ps(3, 1), "add")
-            tt(A("ent", c * C, (c + 1) * C), Fl(6), ps(2, 0), "min")
+            lin(PA, [(245.0 * 8192, ONE), (8192.0, hn), (16384.0, xn), (-131072.0, hs), (16384.0, hy), (-16384.0, asl)])
+            tt(Fl(6), n32, PA, "add")
+            tt(A("ent", c * C, (c + 1) * C), Fl(6), PB, "min")
+            SPANS.append((first, len(ops), c))
         for b in range(24):
             cp(IND(A("W", 0, NP + 16), A("soff", 2 * b, 2 * b + 1)), A("ent", 16 * b, 16 * b + 16))
     for j, lo in enumerate(range(0, NP, C)):
@@ -315,7 +331,7 @@ def regions(op):
     return [r for r in rd if r[0] not in DRAM], [r for r in wr if r[0] not in DRAM]
 
 
-SC = {"gather": 1.56, "scatter": 3.8, "call": 40, "pe": 0.5, "lat": 60, "bw": 250.0, "link": 2500}
+SC = {"gather": 1.56, "scatter": 3.8, "call": 40, "pe": 0.45, "lat": 80, "bw": 250.0, "link": 2500, "lbw": 60.0, "cyc": 0.9}
 
 
 def cost(op, sc=SC):
@@ -325,15 +341,16 @@ def cost(op, sc=SC):
     if kind == "dma":
         return 100, 2000 + count(o) * 128 * (2 if narrow(o) or narrow(ins[0]) else 4) / sc["bw"]
     if kind == "send": return 500, 500
-    if kind == "recv": return 0, sc["link"]
-    n = count(o)
-    if kind in ("iota", "sel"): d = 170 + 2 * n
-    elif o[0] == "@": d = 60 + sc["scatter"] * n
-    elif ins and ins[0][0] == "@": d = 70 + sc["gather"] * n
-    elif kind == "act": d = 20 + sc["call"] + max(64, n)
+    if kind == "recv":
+        d = count(o) * 128 * (2 if narrow(o) else 4) / sc["lbw"]; return d, d + sc["link"]
+    n, y = count(o), sc["cyc"]
+    if kind in ("iota", "sel"): d = 170 + 2 * n * y
+    elif o[0] == "@": d = 60 + sc["scatter"] * n * y
+    elif ins and ins[0][0] == "@": d = 70 + sc["gather"] * n * y
+    elif kind == "act": d = 20 + sc["call"] + max(64, n) * y
     elif kind == "tt":
-        d = sc["call"] + max(64, n * (1 if "ps" in (ins[0][0][:2], ins[1][0][:2]) else 1.5 if narrow(o) else 2))
-    else: d = sc["call"] + max(64, n * (0.5 if narrow(o) and (not ins or narrow(ins[0])) else 1))
+        d = sc["call"] + max(64, n * (1 if "ps" in (ins[0][0][:2], ins[1][0][:2]) else 1.5 if narrow(o) else 2)) * y
+    else: d = sc["call"] + max(64, n * (0.5 if narrow(o) and (not ins or narrow(ins[0])) else 1)) * y
     return d, d + sc["lat"]
 
 
@@ -358,8 +375,10 @@ def links():
             hist[r[0]] = [h for h in hist.get(r[0], []) if not (r[3] == 1 and r[1] <= h[1] and h[2] <= r[2])] + [(i, r[1], r[2], True)]
         for r in rd:
             hist.setdefault(r[0], []).append((i, r[1], r[2], False))
-        if op[1] == "send": sends[op[4][1]] = i
-        if op[1] == "recv": soft[i].add(sends[op[4]])
+        if op[1] == "send":
+            if op[3][0][0][:2] == "sn": soft[i].add(max(sends.values()))
+            sends[op[4][1]] = i
+        if op[1] == "recv": soft[i].add(sends[op[4][0]])
     lead = [i for i, op in enumerate(ops) if op[1] == "sel"][1]
     for i, op in enumerate(ops):
         if op[0] == "G" and not (op[1] == "sel" and i <= lead): soft[i].add(lead)
@@ -368,7 +387,7 @@ def links():
         o = op[2] or op[3][0]
         o = o[1] if o[0] == "@" else o
         name = o[0][:2] + o[0][3:] if o[0][:2] in ("rb", "rn", "ru", "sb", "sn", "su") else o[0]
-        whole = name[:2] in ("ca", "cb", "Gt", "Zt", "E1", "Iw", "Ra", "F", "co", "ma", "Dg") or name[:2] == "ps" and o[2] - o[1] == 12
+        whole = name[:2] in ("ca", "cb", "Gt", "Zt", "E1", "Iw", "Ra", "F", "co", "ma", "Dg") or name[:2] == "ps" and o[2] - o[1] == D
         cls.append(kinds.setdefault((op[0], op[1], name, 0 if whole else o[1]), len(kinds)))
     return ops, hard, soft, cls
 
@@ -388,7 +407,7 @@ def plan(shift=None, window=30, base=None):
         prio[i] += 500.0 * shift.get(cls[i], 0)
         o = ops[i][2] or ops[i][3][0]
         name = o[1][0] if o[0] == "@" else o[0]
-        if name[-1] == "0" and name[:2] != "ps" or name in ("ps0", "ps1", "ps2", "ps3"): prio[i] += LEAD
+        prio[i] -= LEAD * sum(c for lo, hi, c in SPANS[:ST * NCH] if lo <= i < hi)
         if ops[i][1] in ("act", "cp") and ops[i][3][0][0] == "@" and count(o) > C: prio[i] -= LATE
         if name == "zero" or name == "Iw" and o[1] < 256: prio[i] += 1e6
     left = [len(hard[i] | soft[i]) for i in range(n)]
@@ -455,7 +474,8 @@ def rank_program(g, core, T, topo):
     for i in order:
         q, kind, o, ins, par = ops[i]
         if kind == "recv":
-            mark[i] = ("a%d" % par, nin); total["a%d" % par] = nin
+            name = "a%d" % (par[0] + par[1])
+            mark[i] = (name, nin // par[2]); total[name] = nin // par[2]
             continue
         want = {}
         for j in hard[i]:
@@ -464,7 +484,13 @@ def rank_program(g, core, T, topo):
             wait(q, name, want[name])
         e = queue[q]
         if kind == "send":
-            g.remote_dma(T[par[0]][:], ap(ins[0]), T.sem["a%d" % par[1]], T.sem.sent, pid, rid, topo.mask(core, dst))
+            if len(ins) == 1:
+                g.remote_dma(ap(par[0][0]), ap(ins[0]), T.sem["a%d" % par[1]], T.sem.sent, pid, rid, topo.mask(core, dst))
+            else:
+                eng, m = topo.engines(core, dst), nout // len(ins)
+                g.remote_dma_fused([RemoteDMATransfer(dst_ids=[DstId(rid=rid, pnc=pid)], remote_sem=T.sem["a%d" % (par[1] + j)],
+                                                      dma_engine_mask=sum(1 << k for k in eng[j * m:(j + 1) * m]),
+                                                      src=ap(ins[j]), dst=ap(par[0][j])) for j in range(len(ins))], local_sem=T.sem.sent)
             total["sent"] = total.get("sent", 0) + nout
             continue
         if kind == "dma":

@@ -3,36 +3,47 @@ from concourse.mybir import AluOpType, ActivationFunctionType
 
 NM, NP, NW, ST, SH, NR = 8192, 512, 384, 3, 3, 8
 C = 192
-NCH, D, R1 = NW // C, C // 16, 512 // C
+NCH, D = NW // C, C // 16
+R1 = 512 // C
+DW = NW // 16
 PIECE = C // 4
 SPANS = []
 FXP = 1024
-V_GATHERS = (2, 3)
-S_EVAC = (1, 3)
-S_EVAC_G = (0, 1, 2, 3)
-OPT = 0
-TP = 512.0625
-CB = -0.0625 - 16.0 - 49152.0
-MAGIC = 1.5 * 2.0 ** 31
-WTS = [1.0, -1.0, -16.0, -0.25, 6.0, 0.0625, -0.9375, 512.0, 32768.0, -16384.0, -60.0, 8.0, 0.03125, -1088.0, 16384.0,
-       16.0, 0.5, -0.5, 8192.0, 245.0 * 8192, 243.0 * 8192, -131072.0, -2048.0]
-LEAD, LATE = 2000, 5000
-SHIFT = {0:4,3:16,4:-4,7:-8,8:-16,9:-12,10:-24,11:-4,12:-20,13:-22,14:-16,15:-15,16:-15,17:9,18:-1,19:1,20:2,21:2,23:-1,24:3,25:-1,29:-2,36:-2,37:-4,38:28,39:-4,40:-4,41:-4,42:-4,43:-4,44:-4,48:2,57:-4,59:8,60:8,65:-4,70:4,71:-1,73:20,74:16,75:16,76:16,77:16,78:16,79:16,80:16,82:-8,83:-1,89:-2,90:-5,91:8,93:1,95:1,96:17,98:-8,99:-8,100:-4,102:8,104:16,105:-1,106:-1,107:-1,108:-1,109:-1,110:15,111:-5,116:16,120:-4,126:-14,129:4,131:1,132:-2,134:-3,135:-2,136:-2,139:-8,141:1,142:-2,143:-4,154:-20,155:-4,156:-4,157:-8,158:4,159:-4,160:-8,161:-4,163:7,164:-1,179:8,180:-4,191:4,201:16,202:-2,203:-2,204:-2,205:-18,206:-2,207:-10,208:-2,209:-2,210:-2,211:-4,212:1,213:-2,214:8,215:-8,216:-8,217:-8,218:-8,219:8}
+V_EVAC = (3,)
+V_DERIVE = (0, 1)
+MAGIC = 1.5 * 2.0 ** 26
+XA, XH = 25600.0, 28672.0
+WTS = [1.0, -1.0, 4.0, 256.0, 6.0, 8.0, 136.0, -512.0, 65536.0, 16384.0, 16.0, 63.0 / 1024, -189.0 / 16, -2048.0, 4096.0, -0.5,
+       -524288.0 + XH / 2, XA, -XH, 8192.0]
+LEAD = 2000
+LATE = 6000
+SUB = 2
+EARLY = True
+SENDS = ([("b", 0, 2 * C)], [("u", 0, C), ("b", 2 * C, 3 * C)], [("n", 0, C)])
+if NCH == 2:
+    SLOTS = {"y1": ("y", 0), "cnt": ("a", 0), "rl": ("z", 0), "Pk": ("z", C), "idx": ("z", 384), "pre": ("w", 0), "dl": ("z", 0),
+             "y2": ("y", 0), "sum": ("a", 0), "u": ("z", 400), "rr": ("w", C), "ad": ("z", 0), "hs": ("z", C), "k3": ("w", 0),
+             "hy": ("z", 0), "thr": ("y", 0), "mul": ("w", C) if EARLY else ("z", C), "add": ("a", C), "s6": ("y", C), "yt": ("y", 0), "ent": ("z", C)}
+else:
+    SLOTS = {"y1": ("y", 0), "cnt": ("a", 0), "rl": ("y", 0), "Pk": ("a", C), "idx": ("y", C), "pre": ("a", 2 * C), "dl": ("a", 3 * C),
+             "y2": ("y", 0), "sum": ("a", 0), "u": ("z", 3 * C), "rr": ("z", 0), "ad": ("z", C), "hs": ("z", 2 * C), "k3": ("z", 0),
+             "hy": ("z", C), "thr": ("y", 0), "mul": ("z", 2 * C), "add": ("a", C), "s6": ("y", C), "yt": ("y", 2 * C), "ent": ("y", 3 * C)}
 
 SCRATCH = {}
 for _n, _w, _d in [
-        ("F", NM, "bfloat16"), ("E16", NM, "bfloat16"), ("Zt", NM, "bfloat16"), ("Gt", NM, "bfloat16"),
+        ("F", NM, "bfloat16"), ("Zt", NM, "bfloat16"),
         ("ioa", 2048, "bfloat16"), ("zero", 128, "bfloat16"), ("Sall", 2048, "bfloat16"), ("Hall", 2048, "bfloat16"),
-        ("Rall", 2048, "bfloat16"), ("ioc", 256, "bfloat16"), ("mats", 128 * 8, "bfloat16"), ("Iw", 128 * len(WTS), "bfloat16"),
-        ("cm", 256, "bfloat16"), ("Dg", 128 * ST, "bfloat16"), ("ones", C, "bfloat16"), ("turn7", 2 * C, "bfloat16"),
-        ("base", 32, "float32"), ("mask", NW, "float32"), ("coli", 32, "int32"), ("colj", 8, "int32"), ("colf", 32, "float32"),
-        ("t0s", NW, "int32"), ("y0s", NP, "bfloat16"), ("k0s", NP, "int32"), ("ytmp", NP, "float32"), ("W", NP + 16, "float32"),
-        ("ent", NW, "float32"), ("cf", 24, "float16"), ("cint", 24, "int32"), ("Eq", NW, "bfloat16"), ("dd", 48, "float32"),
-        ("soff", 48, "uint16"), ("oyt", NW, "float32"), ("oy1", NP, "bfloat16"), ("oy2", NP, "bfloat16"), ("oyk", NP, "float32")]:
+        ("Pall", 2048, "bfloat16"), ("Rall", 2048, "bfloat16"), ("ioc", 256, "bfloat16"), ("mats", 128 * 8, "bfloat16"),
+        ("Iw", 128 * len(WTS), "bfloat16"), ("cm", 128 * 4, "bfloat16"), ("Dg", 128 * ST, "bfloat16"), ("ones", C, "bfloat16"),
+        ("turn", C, "bfloat16"), ("base", 16, "bfloat16"), ("mask", NW, "float32"), ("coli", 32, "int32"), ("colj", 8, "int32"),
+        ("colf", 32, "float32"), ("t0s", NW, "int32"), ("y0s", NP, "bfloat16"), ("k0s", NP, "int32"), ("kz", NP, "bfloat16"),
+        ("W", NP + 16, "float32"), ("ent", NW, "float32"), ("cf", 24, "float16"), ("cint", 24, "int32"), ("Eq", NW, "bfloat16"),
+        ("dd", 48, "float32"), ("soff", 48, "uint16"), ("oyt", NW, "float32"), ("oy1", NP, "bfloat16"), ("oy2", NP, "bfloat16"),
+        ("oyj", NP, "float32"), ("oyk", NP, "float32")]:
     SCRATCH[_n] = ("sbuf", [128, _w], _d)
 for _c in range(NCH):
-    for _n, _w, _d in [("VG", 16 * C, "bfloat16"), ("VE", 16 * C + 8, "float32"), ("ca", 16 * C, "bfloat16"), ("cb", 16 * C, "float16"),
-                       ("b", 20 * C, "bfloat16"), ("f", 8 * C, "float32"), ("i", 5 * C, "int32"), ("tf", 64, "float32"),
+    for _n, _w, _d in [("VF", 16 * C, "bfloat16"), ("VT", 16 * C + 16, "bfloat16"), ("ca", 16 * C, "bfloat16"), ("cb", 16 * C, "float16"),
+                       ("b", 20 * C, "bfloat16"), ("f", 5 * C, "float32"), ("i", 3 * C, "int32"),
                        ("ti", 16, "int32"), ("tu", 32, "uint16")]:
         SCRATCH[_n + str(_c)] = ("sbuf", [128, _w], _d)
     for _t in range(ST):
@@ -93,80 +104,79 @@ def describe():
         dma("Y", A("rb0%d" % c, 0, C), A("x0", c * C, (c + 1) * C))
     dma("Y", A("y0s", 0, NP), A("y0", 0, NP))
     dma("Y", A("k0s", 0, NP), A("k0", 0, NP))
-    io(A("ioc", 0, 128), [[1, 128]], 0, -1)
+    IOC = A("ioc", 0, 128)
+    io(IOC, [[1, 128]], 0, -1)
     io(A("colj", 0, 1), [[1, 1]], 0, 1)
     io(A("ioa", 0, 2048), [[-1, 16], [1, 128]], 0, 0)
     io(A("ioc", 128, 256), [[16, 8], [0, 16]], 0, 0)
-    io(A("turn7", 0, C), [[0, C // 4], [1, 4]], 0, 0)
-    io(A("base", 0, 2 * D), [[-1, 2], [256, D]], 16, 0)
+    TURN = A("turn", 0, C)
+    io(TURN, [[0, C // 4], [1, 4]], 0, 0)
+    io(A("base", 0, D), [[256, D]], 0, 0)
     dma("G", A("coli", 0, 1), A("hw", 0, 1))
     dma("G", A("coli", 8, 9), A("th", 0, 1))
     dma("G", A("coli", 16, 19), A("dw", 0, 3))
-    io(A("mask", 0, C), [[1, 16], [0, D]], 0, 0)
+    io(A("mask", 0, NW), [[1, 16], [0, DW]], 0, 0)
     ZERO = A("zero", 0, 128)
     ms(ZERO, 0.0)
     for w in WTS:
-        sel(Iw(w), ZERO, [[1, 128]], w, 0, -1)
-    sel(A("cm", 0, 128), ZERO, [[0, 128]], 129.0 * 2048, 0, 1)
-    sel(A("cm", 128, 256), A("cm", 0, 128), [[0, 128]], 1.0, -1, 1)
+        ts(Iw(w), IOC, 0.0, w, "is_equal", "mult")
+    CY1, CY2, CENT, CM = blk("cm", 0), blk("cm", 1), blk("cm", 2), blk("cm", 3)
+    for o, parts in ((CY1, (-2560.0, 8.5)), (CY2, (3712.0, 7.875, 1.0 / 512)), (CENT, (121.0 * 65536, 16384.0 + XH / 2)),
+                     (CM, (129.0 * 2048, 1.0))):
+        for j, v in enumerate(parts):
+            sel(o, o if j else ZERO, [[0, 128]], v, -j, 1)
     for a in range(16):
         sel(blk("Rall", a), Iw(-1.0), [[16, 8], [0, 16]], 1.0, a, -1)
     ts(A("colj", 1, 2), A("colj", 0, 1), 112, None, "bitwise_and")
     ts(A("colj", 2, 3), A("colj", 0, 1), 15, None, "bitwise_and")
-    GP, KC, KH, K37, K512, K16, H1, H2, THC, DN = 0, 1, 2, 3, 4, 5, 6, 7, 8, 9
+    GP, KC, KH, K37, K512, KB, H1, H2, THC, PW, DN = 0, 1, 2, 3, 4, 5, 6, 7, 8, 9, 10
     cp(A("colf", 0, 2), A("colj", 1, 3))
-    ts(cf(KH), cf(KC), -0.5, None, "mult")
+    ts(cf(KH), cf(KC), -0.5, 0.5, "mult", "add")
     ts(cf(K37), cf(KC), 37.0, None, "mult")
     ts(cf(K512), cf(KC), float(NP), None, "add")
-    ts(cf(K16), cf(KC), 16.0, None, "mult")
+    ts(cf(KB), cf(KC), 16.0, 23.5 - 2048, "mult", "add")
+    ts(cf(PW), cf(KC), 0.0, 2047.5, "is_equal", "mult")
+    ts(cf(PW), cf(PW), 0.5, None, "add")
     cp(cf(H1), A("coli", 0, 1))
     ts(cf(H2), A("coli", 0, 1), 2.0, None, "mult")
     ts(cf(THC), A("coli", 8, 9), 0.5, None, "add")
-    ts(A("colf", DN, DN + 3), A("coli", 16, 19), -0.03125, None, "mult")
+    ts(A("colf", DN, DN + 3), A("coli", 16, 19), -0.5, -1.0 / 1024, "add", "mult")
     ts(A("Sall", 0, 2048), A("ioa", 0, 2048), cf(GP), 0.5, "is_equal", "mult")
-    if OPT & 8: act(A("Hall", 0, 2048), A("Sall", 0, 2048), "Identity", 0.0, cf(H2))
-    else: ts(A("Hall", 0, 2048), A("ioa", 0, 2048), cf(GP), cf(H1), "is_equal", "mult")
-    BD, HB, LO, UP, SHF = 0, 1, 2, 3, 4
+    ts(A("Pall", 0, 2048), A("ioa", 0, 2048), cf(GP), cf(PW), "is_equal", "mult")
+    ts(A("Hall", 0, 2048), A("ioa", 0, 2048), cf(GP), cf(H1), "is_equal", "mult")
+    BD, HB, BH, LO, SHF = 0, 1, 2, 3, 4
     ts(mat(BD), A("ioc", 128, 256), cf(GP), None, "is_equal")
     ts(mat(HB), A("ioc", 128, 256), cf(GP), cf(H2), "is_equal", "mult")
-    ts(mat(5), A("ioc", 0, 128), 0.0, -0.5, "is_ge", "mult")
-    ts(mat(6), A("ioc", 0, 128), 0.0, 0.5, "is_le", "mult")
-    ts(mat(7), A("ioc", 0, 128), -1.0, None, "is_equal")
-    for j in range(3):
+    ts(mat(BH), A("ioc", 128, 256), cf(GP), -0.5, "is_equal", "mult")
+    ts(mat(5), IOC, 0.0, -0.5, "is_gt", "mult")
+    ts(mat(6), IOC, -1.0, None, "is_equal")
+    for j in range(2):
         tt(mat(LO + j), mat(5 + j), mat(BD), "mult")
     for t in range(ST):
-        ts(blk("Dg", t), A("ioc", 0, 128), 0.0, cf(DN + t), "is_equal", "mult")
+        ts(blk("Dg", t), IOC, 0.0, cf(DN + t), "is_equal", "mult")
     ONE = A("ones", 0, C)
     ms(ONE, 1.0)
-    ms(A("turn7", C, 2 * C), 7.5)
-    ts(A("base", 0, 2 * D), A("base", 0, 2 * D), cf(K16), None, "add")
-    ts(A("mask", 0, C), A("mask", 0, C), cf(KC), 0.5, "is_ge", "mult")
-    ms(A("W", NP, NP + 16), 0.0)
+    ts(A("mask", 0, NW), A("mask", 0, NW), cf(KC), 0.5, "is_ge", "mult")
     ms(A("soff", 0, 48), 0)
-    act(A("ytmp", 0, NP), A("y0s", 0, NP), "Identity", 129.0 * 16384, 16384.0)
-    tt(A("W", 0, NP), A("ytmp", 0, NP), A("k0s", 0, NP), "add")
     for c in range(NCH):
-        ms(A("VE%d" % c, 0, 8), 0.0)
+        ms(A("VT%d" % c, 0, 16), -2304.0)
         ts(A("rn0%d" % c, 0, C), A("t0s", c * C, (c + 1) * C), NM - 1, None, "bitwise_and")
         cp(A("ru0%d" % c, 0, C), A("rn0%d" % c, 0, C))
         ts(A("rb0%d" % c, 2 * C, 3 * C), A("t0s", c * C, (c + 1) * C), float(NM), None, "is_ge")
         ms(A("rb0%d" % c, C, 2 * C), -1.0)
     for j in range(NM // 512):
         lo, hi = 512 * j, 512 * j + 512
-        if j % 2 == 0: ts(A("E16", lo, lo + FXP), A("F", lo, lo + FXP), 2056.5, None, "add")
+        if j % 2 == 0: ts(A("Zt", lo, lo + FXP), A("F", lo, lo + FXP), 16.0, -256.0, "is_lt", "mult")
         pb = A("ps%d" % (j % 8), 0, 512)
-        lin(pb, [(1.0, A("F", lo, hi)), (-1.0, A("E16", lo, hi))])
-        if j % 4 in S_EVAC_G: act(A("Gt", lo, hi), pb, "Identity", 2064.0)
-        else: ts(A("Gt", lo, hi), pb, 2064.0, None, "add")
-    for j in range(NM // FXP):
-        lo, hi = FXP * j, FXP * j + FXP
-        ts(A("Zt", lo, hi), A("F", lo, hi), 16.0, -1056.0, "is_lt", "mult")
-    for j in range(NM // 512):
-        lo, hi = 512 * j, 512 * j + 512
-        pb = A("ps%d" % (j % 4 + 4), 0, 512)
-        lin(pb, [(1.0, A("Zt", lo, hi)), (1.0, A("E16", lo, hi))])
-        if j % 4 in S_EVAC: act(A("Zt", lo, hi), pb, "Identity")
-        else: cp(A("Zt", lo, hi), pb)
+        lin(pb, [(1.0, A("F", lo, hi)), (1.0, A("Zt", lo, hi))])
+        if j % 4 in V_EVAC: cp(A("Zt", lo, hi), pb)
+        else: act(A("Zt", lo, hi), pb, "Identity")
+    ms(A("W", NP, NP + 16), 0.0)
+    ts(A("kz", 0, NP), A("k0s", 0, NP), float(NM), XH, "is_ge", "mult")
+    lin(A("ps3", 0, NP), [(65536.0, A("y0s", 0, NP)), (1.0, A("kz", 0, NP))])
+    tt(A("oyj", 0, NP), A("k0s", 0, NP), A("ps3", 0, NP), "add")
+    act(A("W", 0, NP), A("oyj", 0, NP), "Identity", 129.0 * 65536 + 16384)
+    YB = -0.25 - 61.0 / 128
 
     arr = [0]
     for t in range(ST):
@@ -175,142 +185,136 @@ def describe():
             def B(j): return A("b" + cs_, j * C, (j + 1) * C)
             def Fl(j): return A("f" + cs_, j * C, (j + 1) * C)
             def In(j): return A("i" + cs_, j * C, (j + 1) * C)
-            def ps(k, j, n=1):
-                return A("ps%d" % (4 * c + k if NCH == 2 else 2 * c + k if k < 2 else 4 + k), j * C, (j + n) * C)
-            def tf(lo, hi): return A("tf" + cs_, lo, hi)
+            turn_ = t * NCH + c
+            if NCH == 2: bank = {"y": 4 * c, "a": 4 * c + 1, "z": 4 * c + 2, "w": 4 * c + 3, "d": 2}
+            else: bank = {"y": 2 * c, "a": 2 * c + 1, "z": 6 + turn_ % 2, "d": 7 - turn_ % 2}
+            def ps(name, n=C):
+                k, lo = SLOTS[name]
+                return A("ps%d" % bank[k], lo, lo + n)
             rb, sb = "rb%d%d" % (t, c), "sb%d%d" % (t, c)
             x, hp, s = A(rb, 0, C), A(rb, C, 2 * C), A(rb, 2 * C, 3 * C)
             xn, hs, s6 = A(sb, 0, C), A(sb, C, 2 * C), A(sb, 2 * C, 3 * C)
             n32, nn32, nn16 = A("rn%d%d" % (t, c), 0, C), A("sn%d%d" % (t, c), 0, C), A("su%d%d" % (t, c), 0, C)
-            VG, VE, ca, cb = "VG" + cs_, "VE" + cs_, "ca" + cs_, "cb" + cs_
-            cand, Aa, Bb, e, sx, se, sg, ap_, pre, asl, yc, ad, hy, nv, adk, hv, hn, g1, rr, ur = [B(j) for j in range(20)]
+            VF, VT, ca, cb = "VF" + cs_, "VT" + cs_, "ca" + cs_, "cb" + cs_
+            cand, rl, Pk, e, sx, se, sg, ap_, pre, aw, yc, ad, hy, hv, eh, rr = [B(j) for j in range(16)]
             for j in range(C // PIECE):
-                off = A("ru%d%d" % (t, c), j * PIECE, (j + 1) * PIECE)
-                o = A(VG, 16 * j * PIECE, 16 * (j + 1) * PIECE)
-                if j in V_GATHERS: cp(o, IND(A("Gt", 0, NM), off))
-                else: act(o, IND(A("Gt", 0, NM), off), "Identity")
-            for j in range(C // PIECE):
-                off = A("ru%d%d" % (t, c), j * PIECE, (j + 1) * PIECE)
-                act(A(VE, 8 + 16 * j * PIECE, 8 + 16 * (j + 1) * PIECE), IND(A("Zt", 0, NM), off), "Identity", -129.0 * TP - CB, TP / 16)
+                lo, hi = 16 * j * PIECE, 16 * (j + 1) * PIECE
+                act(A(VF, lo, hi), IND(A("Zt", 0, NM), A("ru%d%d" % (t, c), j * PIECE, (j + 1) * PIECE)), "Identity")
+                if j in V_DERIVE: ts(A(VT, 16 + lo, 16 + hi), A(VF, lo, hi), -1.0, -2552.5, "mult", "add")
+                else: act(A(VT, 16 + lo, 16 + hi), A(VF, lo, hi), "Identity", -2552.5, -1.0)
             for h in range(R1):
-                lin(A(ps(0, 0)[0], h, R1 * C, R1), [(1.0, x)])
-            for k in range(16 // R1):
-                tt(A(ca, R1 * k * C, R1 * (k + 1) * C), A(VG, k, 16 * C, 16 // R1), ps(0, 0, R1), "is_le")
-            lin(ps(1, 0), [(-16.0, s), (-0.25, hp)] + [(blk("Sall", k + 16 // R1 * h), A(ca, R1 * k * C + h, R1 * (k + 1) * C, R1))
-                                                       for k in range(16 // R1) for h in range(R1)])
-            act(cand, ps(1, 0), "Sign", -4.5)
-            lin(ps(1, 0), [(1.0, A("turn7", 0, C)), (mat(LO), cand)])
-            lin(ps(1, 1), [(1.0, A("turn7", C, 2 * C)), (mat(UP), cand)])
-            act(A("b" + cs_, C, 3 * C), ps(1, 0, 2), "Sign", cf(KH))
-            pd = ps(2, 0)[0]
-            lin(A(pd, 2 * C, 2 * C + 2 * D), [(blk("Sall", a), A("b" + cs_, C + a, 3 * C, 16)) for a in range(16)])
-            tt(tf(0, 2 * D), A(pd, 2 * C, 2 * C + 2 * D), A("base", 0, 2 * D), "add")
-            act(tf(2 * D, 3 * D), A(pd, 2 * C + D, 2 * C + 2 * D), "Identity", 7.5 * 16384, 16384.0)
-            tt(tf(3 * D, 4 * D), tf(0, D), tf(D, 2 * D), "min")
-            tt(tf(4 * D, 5 * D), tf(3 * D, 4 * D), tf(2 * D, 3 * D), "min")
-            cp(A("tu" + cs_, 0, D), tf(4 * D, 5 * D))
-            lin(ps(3, 0), [(1.0, cand), (1.0, Aa), (mat(SHF), Bb), (6.0, s)])
-            act(pre, ps(3, 0), "Sign", -2.5)
-            act(e, IND(A(VE, 0, 16 * C + 8), A("tu" + cs_, 0, D)), "Relu", CB / TP, 1.0 / TP)
-            if OPT & 1: act(sx, x, "Sign")
-            else: ts(sx, x, 0.0, None, "is_gt")
-            if OPT & 2: act(se, e, "Sign")
-            else: ts(se, e, 0.0, None, "is_gt")
-            lin(ps(2, 0), [(1.0, x), (-1.0, e)])
-            act(sg, ps(2, 0), "Sign", 0.5)
-            act(xn, ps(2, 0), "Abs")
-            lin(ps(3, 1), [(0.0625, x), (-0.9375, sx), (-0.9375, se)])
-            act(Fl(0), ps(3, 1), "Identity", -16384.0 - 8.0 + 30.5 / 16 - CB)
-            lin(ps(0, 0), [(32768.0, sx), (512.0, e), (0.0625, e), (-16384.0, sg)])
-            tt(ps(0, 0), Fl(0), ps(0, 0), "max")
+                lin(A(ps("y1")[0], h, R1 * C, R1), [(CY1, ONE), (1.0, x)])
+            n, m = C // SUB, 16 // R1
+            for j in range(SUB):
+                lo, hi = j * n, (j + 1) * n
+                for k in range(m):
+                    tt(A(ca, 16 * lo + R1 * k * n, 16 * lo + R1 * (k + 1) * n), A(VF, 16 * lo + k, 16 * hi, m), A(ps("y1")[0], R1 * lo, R1 * hi), "subtract")
+                lin(A(ps("cnt")[0], lo, hi), [(256.0, A(rb, 2 * C + lo, 2 * C + hi)), (4.0, A(rb, C + lo, C + hi))]
+                    + [(blk("Sall", k), A(VT, 16 + 16 * lo + k, 16 + 16 * hi, 16)) for k in range(16)]
+                    + [(blk("Sall", k + m * h), A(ca, 16 * lo + R1 * k * n + h, 16 * lo + R1 * (k + 1) * n, R1)) for k in range(m) for h in range(R1)])
+            act(cand, ps("cnt"), "Sign", -72.0, -1.0)
+            lin(ps("rl"), [(1.0, TURN), (mat(BH), cand)])
+            act(rl, ps("rl"), "Relu", -7.0)
+            lin(ps("Pk"), [(1.0, TURN), (mat(LO), cand), (-1.0, rl)])
+            act(Pk, ps("Pk"), "Sign", cf(KH))
+            pd = ps("idx", D)
+            lin(pd, [(1.0, A("base", 0, D))] + [(blk("Pall", a), A(Pk[0], Pk[1] + a, Pk[2], 16)) for a in range(16)])
+            ts(A("tu" + cs_, 0, D), pd, cf(KB), 0.0, "add", "max")
+            act(e, IND(A(VT, 0, 16 * C + 16), A("tu" + cs_, 0, D)), "Relu", -160.0, -1.0 / 16)
+            lin(ps("pre"), [(6.0, s), (1.0, cand), (mat(SHF), Pk)])
+            act(pre, ps("pre"), "Sign", -1.5)
+            ts(sx, x, 0.0, None, "is_gt")
+            ts(se, e, 0.0, None, "is_gt")
+            lin(ps("dl"), [(1.0, x), (-1.0, e)])
+            act(sg, ps("dl"), "Sign", 0.5)
+            act(xn, ps("dl"), "Abs")
+            lin(ps("y2"), [(CY2, ONE), (8.0, x), (-512.0, sx), (8.0, e), (-512.0, se), (136.0, sg), (8.0, xn)])
             for k in range(16):
-                tt(A(cb, k * C, (k + 1) * C), A(VE, 8 + k, 8 + 16 * C, 16), ps(0, 0), "subtract")
-            lin(ps(1, 0), [(-60.0, ONE)] + [(blk("Sall", k), A(cb, k * C, (k + 1) * C)) for k in range(16)])
-            p3 = ps(3, 0)[0]
-            pu = A(p3, 2 * C, 2 * C + D)
+                tt(A(cb, k * C, (k + 1) * C), A(VT, 16 + k, 16 + 16 * C, 16), ps("y2"), "add")
+            lin(ps("sum"), [(blk("Sall", k), A(cb, k * C, (k + 1) * C)) for k in range(16)])
+            pu = ps("u", D)
             lin(pu, [(blk("Hall", a), A(sb, a, C, 16)) for a in range(16)])
             ts(A("ti" + cs_, 0, D), pu, 241.0, None, "mult")
             cint = A("cint", D * c, D * c + D)
             ts(cint, A("ti" + cs_, 0, D), 6, NP - 1, "arith_shift_right", "bitwise_and")
             cp(A("tu" + cs_, 16, 16 + D), cint)
             cp(A("cf", D * c, D * c + D), cint)
-            lin(ps(2, 1), [(mat(HB), xn)])
-            act(rr, ps(2, 1), "Identity", 128.5 + 1.0 / 2048, 1.0 / 2048)
-            act(Fl(1), IND(A("W", 0, NP + 16), A("tu" + cs_, 16, 16 + D)), "Identity")
-            act(yc, Fl(1), "Identity", -0.25, 1.0 / 16384)
-            lin(ps(2, 0), [(-1.0, xn), (1.0, yc)])
-            act(ad, ps(2, 0), "Abs", -129.0)
-            lin(ps(2, 1), [(mat(BD), ad)])
-            act(hs, ps(2, 1), "Sign", cf(THC), -1.0)
-            lin(ps(3, 0), [(16384.0, yc)])
-            tt(ps(3, 0), Fl(1), ps(3, 0), "subtract")
-            act(nv, ps(3, 0), "Relu", -8191.0)
-            tt(Fl(2), ps(3, 0), n32, "subtract")
-            act(adk, Fl(2), "Abs")
-            lin(ps(2, 0), [(-1.0, xn), (1.0, yc), (16.0, hs)])
-            act(hy, ps(2, 0), "Relu", -129.0)
-            lin(ps(3, 1), [(0.5, hs), (-1.0, nv)])
-            act(hv, ps(3, 1), "Relu", 0.5)
-            lin(ps(3, 0), [(1.0, hv)])
-            tt(ps(3, 0), Fl(2), ps(3, 0), "mult")
-            M1, MUL, PB, SL, PA = (ps(3, 0), ps(2, 1), ps(2, 0), ps(0, 1), ps(3, 1)) if NCH == 2 else (ps(0, 1), ps(0, 2), ps(0, 3), ps(1, 1), ps(1, 2))
-            tt(M1, n32, ps(3, 0), "add")
-            Eq, dd = A("Eq", c * C, (c + 1) * C), 2 * D * c
-            for a in range(16):
-                lin(A(p3, C + D * a, C + D * a + D), [(blk("Rall", a), A("cf", D * c, D * c + D))])
-            tt(Eq, ps(3, 1), A("mask", 0, C), "is_equal")
-            lin(A(p3, 400, 400 + D), [(blk("Sall", a), A("Eq", c * C + D * a, c * C + D * a + D)) for a in range(16)])
-            ts(A("dd", dd, dd + D), A(p3, 400, 400 + D), 0.0, 4096.0, "is_gt", "mult")
-            tt(A("dd", dd + D, dd + 2 * D), A("dd", dd, dd + D), cint, "add")
-            ts(A("soff", dd, dd + 2 * D, 2), A("dd", dd + D, dd + 2 * D), cf(K512), None, "min")
-            lin(ps(2, 0), [(16384.0, hs), (1.0, adk)])
-            lin(ps(2, 1), [(16384.0, hv), (1.0, adk)])
-            act(A("b" + cs_, 16 * C, 18 * C), ps(2, 0, 2), "Sign", -16384.5)
-            lin(MUL, [(A("cm", 128, 256), ONE), (mat(HB), xn), (-2048.0, rr)])
-            lin(PB, [(243.0 * 8192, ONE), (16384.0, xn), (-131072.0, hs), (16384.0, hy)])
-            if OPT & 4:
-                act(Fl(7), ps(1, 0), "Identity", MAGIC)
-                act(Fl(3), Fl(7), "Identity", -MAGIC)
-            else: ts(Fl(3), ps(1, 0), MAGIC, MAGIC, "add", "subtract")
-            tt(Fl(4), ps(1, 0), Fl(3), "subtract")
-            act(ap_, Fl(4), "Identity", 135.5, 0.125)
-            lin(ps(0, 0), [(blk("Dg", t), ONE), (-1088.0, pre), (8.0, ap_), (0.03125, ap_)])
-            tt(asl, Fl(4), ps(0, 0), "is_gt")
-            lin(ps(1, 0), [(-1.0, hv), (-1.0, asl)])
-            act(ur, ps(1, 0), "Relu", 1.0)
-            act(Fl(5), ps(1, 0), "Relu", cf(K37), cf(K37))
-            tt(MUL, ur, MUL, "mult")
-            tt(In(2), n32, MUL, "mult")
-            ts(In(3), In(2), 5, NM - 1, "arith_shift_right", "bitwise_and")
-            lin(SL, [(-0.5, g1), (1.0, asl)])
-            act(s6, SL, "Relu", -0.5)
-            tt(M1, Fl(5), M1, "add")
-            tt(In(4), In(3), M1, "add")
-            ts(nn32, In(4), NM - 1, None, "bitwise_and")
+            if c == NCH - 1:
+                pq = "ps%d" % bank["d"]
+                for a in range(16):
+                    lin(A(pq, DW * a, DW * a + DW), [(blk("Rall", a), A("cf", 0, DW))])
+                tt(A("Eq", 0, NW), A(pq, 0, NW), A("mask", 0, NW), "is_equal")
+                lin(A(pq, 424, 424 + DW), [(blk("Sall", a), A("Eq", DW * a, DW * a + DW)) for a in range(16)])
+                ts(A("dd", 0, DW), A(pq, 424, 424 + DW), 0.0, 4096.0, "is_gt", "mult")
+                tt(A("dd", DW, 2 * DW), A("dd", 0, DW), A("cint", 0, DW), "add")
+                ts(A("soff", 0, 2 * DW, 2), A("dd", DW, 2 * DW), cf(K512), None, "min")
+            lin(ps("rr"), [(mat(HB), xn)])
+            act(rr, ps("rr"), "Identity", 128.5 + 1.0 / 2048, 1.0 / 2048)
+            MUL, ADD, K3 = ps("mul"), ps("add"), ps("k3")
+            if EARLY:
+                lin(MUL, [(CM, ONE), (mat(HB), xn), (-2048.0, rr)])
+                tt(In(0), n32, MUL, "mult")
+                ts(In(1), In(0), 5, NM - 1, "arith_shift_right", "bitwise_and")
+                ts(MUL, n32, cf(K37), float(NM), "add", "add")
+                tt(Fl(3), In(1), MUL, "add")
+            act(Fl(0), IND(A("W", 0, NP + 16), A("tu" + cs_, 16, 16 + D)), "Identity")
+            act(yc, Fl(0), "Identity", YB, 1.0 / 65536)
+            lin(ps("ad"), [(-1.0, xn), (1.0, yc)])
+            act(ad, ps("ad"), "Abs", -129.0)
+            lin(ps("hs"), [(mat(BD), ad)])
+            act(hs, ps("hs"), "Sign", cf(THC), -1.0)
+            lin(K3, [(65536.0, yc), (16384.0, hs)])
+            tt(K3, Fl(0), K3, "subtract")
+            if EARLY: tt(Fl(4), Fl(3), K3, "min")
+            tt(eh, n32, K3, "is_equal")
+            act(hv, K3, "Sign", 8191.5, -1.0)
+            lin(ps("hy"), [(-1.0, xn), (1.0, yc), (16.0, hs)])
+            act(hy, ps("hy"), "Relu", -129.0)
+            ts(Fl(1), ps("sum"), MAGIC, MAGIC, "add", "subtract")
+            tt(Fl(2), ps("sum"), Fl(1), "subtract")
+            act(ap_, Fl(2), "Identity", 192.0, 16.0)
+            lin(ps("thr"), [(blk("Dg", t), ONE), (-189.0 / 16, pre), (63.0 / 1024, ap_)])
+            tt(aw, Fl(2), ps("thr"), "is_le")
+            if EARLY:
+                act(ADD, aw, "Identity", 8192.0, 32768.0)
+                tt(ADD, n32, ADD, "add")
+                tt(In(2), Fl(4), ADD, "min")
+            else:
+                lin(MUL, [(mat(HB), xn), (-2048.0, rr), (4096.0, aw)])
+                act(MUL, MUL, "Relu", 129.0 * 2048 + 1 - 4096)
+                act(ADD, aw, "Identity", 8192.0, cf(K37))
+                tt(In(0), n32, MUL, "mult")
+                ts(In(1), In(0), 5, NM - 1, "arith_shift_right", "bitwise_and")
+                tt(ADD, n32, ADD, "add")
+                tt(Fl(3), In(1), ADD, "add")
+                tt(In(2), Fl(3), K3, "min")
+            ts(nn32, In(2), NM - 1, None, "bitwise_and")
+            lin(ps("s6"), [(1.0, eh), (-0.5, hv), (-1.0, aw)])
+            act(s6, ps("s6"), "Relu", 0.5)
             if t < ST - 1:
                 cp(nn16, nn32)
-                for call in ([("b", 0, 2 * C)], [("u", 0, C), ("b", 2 * C, 3 * C)], [("n", 0, C)]):
+                for call in SENDS:
                     to = [A("r%s%d%d" % (p_, t + 1, c), lo, hi) for p_, lo, hi in call]
                     ops.append(("G", "send", None, [A("s%s%d%d" % (p_, t, c), lo, hi) for p_, lo, hi in call], (to, arr[0])))
                     for j, o in enumerate(to):
                         ops.append(("R", "recv", o, [], (arr[0], j, len(to))))
                     arr[0] += len(to)
             else:
-                lin(ps(0, 0), [(8192.0, s6)])
-                tt(A("oyt", c * C, (c + 1) * C), nn32, ps(0, 0), "add")
+                lin(ps("yt"), [(8192.0, s6)])
+                tt(A("oyt", c * C, (c + 1) * C), nn32, ps("yt"), "add")
                 dma("Y", A("yt", c * C, (c + 1) * C), A("oyt", c * C, (c + 1) * C))
                 dma("Y", A("yx", c * C, (c + 1) * C), xn)
-            lin(PA, [(245.0 * 8192, ONE), (8192.0, hn), (16384.0, xn), (-131072.0, hs), (16384.0, hy), (-16384.0, asl)])
-            tt(Fl(6), n32, PA, "add")
-            tt(A("ent", c * C, (c + 1) * C), Fl(6), PB, "min")
+            lin(ps("ent"), [(CENT, ONE), (65536.0, xn), (-524288.0 + XH / 2, hs), (65536.0, hy), (-XH, eh), (XA, aw)])
+            tt(A("ent", c * C, (c + 1) * C), n32, ps("ent"), "add")
             SPANS.append((first, len(ops), c))
-        for b in range(24):
+        for b in range(DW):
             cp(IND(A("W", 0, NP + 16), A("soff", 2 * b, 2 * b + 1)), A("ent", 16 * b, 16 * b + 16))
-    for j, lo in enumerate(range(0, NP, C)):
-        hi = min(NP, lo + C)
-        act(A("oy1", lo, hi), A("W", lo, hi), "Identity", -0.25, 1.0 / 16384)
-        lin(A("ps%d" % j, 0, hi - lo), [(16384.0, A("oy1", lo, hi))])
-        tt(A("oyk", lo, hi), A("W", lo, hi), A("ps%d" % j, 0, hi - lo), "subtract")
+    for j, lo in enumerate(range(0, NP, 256)):
+        hi = lo + 256
+        act(A("oy1", lo, hi), A("W", lo, hi), "Identity", YB, 1.0 / 65536)
+        lin(A("ps%d" % j, 0, hi - lo), [(65536.0, A("oy1", lo, hi))])
+        tt(A("oyj", lo, hi), A("W", lo, hi), A("ps%d" % j, 0, hi - lo), "subtract")
+        ts(A("oyk", lo, hi), A("oyj", lo, hi), -16384.0, float(NM), "add", "min")
     dma("Y", A("yk", 0, NP), A("oyk", 0, NP))
     act(A("oy2", 0, NP), A("oy1", 0, NP), "Identity", -129.0)
     dma("Y", A("yy", 0, NP), A("oy2", 0, NP))
@@ -349,7 +353,7 @@ def cost(op, sc=SC):
     elif ins and ins[0][0] == "@": d = 70 + sc["gather"] * n * y
     elif kind == "act": d = 20 + sc["call"] + max(64, n) * y
     elif kind == "tt":
-        d = sc["call"] + max(64, n * (1 if "ps" in (ins[0][0][:2], ins[1][0][:2]) else 1.5 if narrow(o) else 2)) * y
+        d = sc["call"] + max(64, n * (1 if "ps" in (ins[0][0][:2], ins[1][0][:2]) else 2)) * y
     else: d = sc["call"] + max(64, n * (0.5 if narrow(o) and (not ins or narrow(ins[0])) else 1)) * y
     return d, d + sc["lat"]
 
@@ -379,24 +383,13 @@ def links():
             if op[3][0][0][:2] == "sn": soft[i].add(max(sends.values()))
             sends[op[4][1]] = i
         if op[1] == "recv": soft[i].add(sends[op[4][0]])
-    lead = [i for i, op in enumerate(ops) if op[1] == "sel"][1]
-    for i, op in enumerate(ops):
-        if op[0] == "G" and not (op[1] == "sel" and i <= lead): soft[i].add(lead)
-    kinds, cls = {}, []
-    for op in ops:
-        o = op[2] or op[3][0]
-        o = o[1] if o[0] == "@" else o
-        name = o[0][:2] + o[0][3:] if o[0][:2] in ("rb", "rn", "ru", "sb", "sn", "su") else o[0]
-        whole = name[:2] in ("ca", "cb", "Gt", "Zt", "E1", "Iw", "Ra", "F", "co", "ma", "Dg") or name[:2] == "ps" and o[2] - o[1] == D
-        cls.append(kinds.setdefault((op[0], op[1], name, 0 if whole else o[1]), len(kinds)))
-    return ops, hard, soft, cls
+    return ops, hard, soft
 
 
-def plan(shift=None, window=30, base=None):
-    ops, hard, soft, cls = base or links()
-    shift = shift or SHIFT
+def plan(window=30, base=None, sc=SC, fixed=None):
+    ops, hard, soft = base or links()
     n = len(ops)
-    cst = [cost(op) for op in ops]
+    cst = [cost(op, sc) for op in ops]
     users = [[] for _ in range(n)]
     for i in range(n):
         for j in hard[i] | soft[i]: users[j].append(i)
@@ -404,12 +397,9 @@ def plan(shift=None, window=30, base=None):
     for i in range(n - 1, -1, -1):
         prio[i] = cst[i][1] + max([prio[u] for u in users[i]] + [0.0])
     for i in range(n):
-        prio[i] += 500.0 * shift.get(cls[i], 0)
         o = ops[i][2] or ops[i][3][0]
-        name = o[1][0] if o[0] == "@" else o[0]
         prio[i] -= LEAD * sum(c for lo, hi, c in SPANS[:ST * NCH] if lo <= i < hi)
         if ops[i][1] in ("act", "cp") and ops[i][3][0][0] == "@" and count(o) > C: prio[i] -= LATE
-        if name == "zero" or name == "Iw" and o[1] < 256: prio[i] += 1e6
     left = [len(hard[i] | soft[i]) for i in range(n)]
     ready = [i for i in range(n) if left[i] == 0]
     at = [0.0] * n
@@ -418,8 +408,10 @@ def plan(shift=None, window=30, base=None):
     dmafree = [0.0]
     order = []
     while ready:
-        first = min(max(at[i], free[ops[i][0]]) for i in ready)
-        i = max((i for i in ready if max(at[i], free[ops[i][0]]) <= first + window), key=lambda k: (prio[k], -k))
+        if fixed: i = fixed[len(order)]
+        else:
+            first = min(max(at[i], free[ops[i][0]]) for i in ready)
+            i = max((i for i in ready if max(at[i], free[ops[i][0]]) <= first + window), key=lambda k: (prio[k], -k))
         ready.remove(i)
         q = ops[i][0]
         start[i] = max(at[i], free[q]); free[q] = start[i] + cst[i][0]

@@ -8,15 +8,19 @@ R1 = 512 // C
 DW = NW // 16
 PIECE = C // 4
 SPANS = []
-FXP = 1024
+LOADS = (512, 1536, 2560, 3584, 4608, 5632, 6656, 7680, 8192)
 V_EVAC = (3,)
-V_DERIVE = (0, 1)
+V_DERIVE = (0, 1, 2, 3)
+G_DERIVE = ()
+V_IW = 8
 MAGIC = 1.5 * 2.0 ** 26
 XA, XH = 25600.0, 28672.0
 WTS = [1.0, -1.0, 4.0, 256.0, 6.0, 8.0, 136.0, -512.0, 65536.0, 16384.0, 16.0, 63.0 / 1024, -189.0 / 16, -2048.0, 4096.0, -0.5,
-       -524288.0 + XH / 2, XA, -XH, 8192.0]
-LEAD = 2000
-LATE = 6000
+       -524288.0 + XH / 2, XA, -XH, 8192.0, 1.0 / 2048]
+ON_S = ("sx", "se")
+LEADS = (0, 2000, 4000)
+LATES = (0, 3000, 6000)
+AGAIN = False
 SUB = 2
 EARLY = True
 SENDS = ([("b", 0, 2 * C)], [("u", 0, C), ("b", 2 * C, 3 * C)], [("n", 0, C)])
@@ -32,8 +36,8 @@ else:
 SCRATCH = {}
 for _n, _w, _d in [
         ("F", NM, "bfloat16"), ("Zt", NM, "bfloat16"),
-        ("ioa", 2048, "bfloat16"), ("zero", 128, "bfloat16"), ("Sall", 2048, "bfloat16"), ("Hall", 2048, "bfloat16"),
-        ("Pall", 2048, "bfloat16"), ("Rall", 2048, "bfloat16"), ("ioc", 256, "bfloat16"), ("mats", 128 * 8, "bfloat16"),
+        ("ioa", 144, "bfloat16"), ("zero", 128, "bfloat16"), ("Sall", 144, "bfloat16"), ("Hall", 144, "bfloat16"),
+        ("Pall", 144, "bfloat16"), ("Rall", 2048, "bfloat16"), ("ioc", 256, "bfloat16"), ("mats", 128 * 8, "bfloat16"),
         ("Iw", 128 * len(WTS), "bfloat16"), ("cm", 128 * 4, "bfloat16"), ("Dg", 128 * ST, "bfloat16"), ("ones", C, "bfloat16"),
         ("turn", C, "bfloat16"), ("base", 16, "bfloat16"), ("mask", NW, "float32"), ("coli", 32, "int32"), ("colj", 8, "int32"),
         ("colf", 32, "float32"), ("t0s", NW, "int32"), ("y0s", NP, "bfloat16"), ("k0s", NP, "int32"), ("kz", NP, "bfloat16"),
@@ -42,7 +46,7 @@ for _n, _w, _d in [
         ("oyj", NP, "float32"), ("oyk", NP, "float32")]:
     SCRATCH[_n] = ("sbuf", [128, _w], _d)
 for _c in range(NCH):
-    for _n, _w, _d in [("VF", 16 * C, "bfloat16"), ("VT", 16 * C + 16, "bfloat16"), ("ca", 16 * C, "bfloat16"), ("cb", 16 * C, "float16"),
+    for _n, _w, _d in [("VG", 16 * C, "float32"), ("VF", 16 * C, "bfloat16"), ("VT", 16 * C + 16, "bfloat16"), ("ca", 16 * C, "bfloat16"), ("cb", 16 * C, "float16"),
                        ("b", 20 * C, "bfloat16"), ("f", 5 * C, "float32"), ("i", 3 * C, "int32"),
                        ("ti", 16, "int32"), ("tu", 32, "uint16")]:
         SCRATCH[_n + str(_c)] = ("sbuf", [128, _w], _d)
@@ -54,7 +58,7 @@ for _c in range(NCH):
 for _k in range(8):
     SCRATCH["ps%d" % _k] = ("psum", [128, 512], "float32")
 DRAM = ("fx", "y0", "k0", "x0", "t0", "dw", "hw", "th", "yx", "yt", "yy", "yk")
-NDMA = NM // FXP + 8 + 3 * NCH
+NDMA = len(LOADS) + 10 + 3 * NCH
 SEMAPHORES = ["V", "S", "P", "G", "sent"] + ["d%d" % _k for _k in range(NDMA)] + ["a%d" % _k for _k in range(8 * NCH)]
 
 
@@ -89,17 +93,17 @@ def describe():
     def dma(q, o, a): ops.append((q, "dma", o, [a], None))
     def Iw(w): return A("Iw", 128 * WTS.index(w), 128 * WTS.index(w) + 128)
     def mat(j): return A("mats", 128 * j, 128 * j + 128)
-    def blk(n, a): return A(n, 128 * a, 128 * a + 128)
+    def blk(n, a):
+        return A(n, 15 - a, 143 - a) if n in ("Sall", "Pall", "Hall") else A(n, 128 * a, 128 * a + 128)
     def cf(j): return A("colf", j, j + 1)
 
-    def lin(o, terms):
+    def lin(o, terms, more=False):
         for j, (l, r) in enumerate(terms):
-            ops.append(("P", "mm", o, [Iw(l) if isinstance(l, float) else l, r], (j == 0, j == len(terms) - 1)))
+            ops.append(("P", "mm", o, [Iw(l) if isinstance(l, float) else l, r], (j == 0 and not more, j == len(terms) - 1)))
 
-    dma("Y", A("F", 0, FXP), A("fx", 0, FXP))
     dma("Y", A("t0s", 0, NW), A("t0", 0, NW))
-    for j in range(1, NM // FXP):
-        dma("Y", A("F", j * FXP, (j + 1) * FXP), A("fx", j * FXP, (j + 1) * FXP))
+    for lo, hi in zip((0,) + LOADS, LOADS):
+        dma("Y", A("F", lo, hi), A("fx", lo, hi))
     for c in range(NCH):
         dma("Y", A("rb0%d" % c, 0, C), A("x0", c * C, (c + 1) * C))
     dma("Y", A("y0s", 0, NP), A("y0", 0, NP))
@@ -107,7 +111,7 @@ def describe():
     IOC = A("ioc", 0, 128)
     io(IOC, [[1, 128]], 0, -1)
     io(A("colj", 0, 1), [[1, 1]], 0, 1)
-    io(A("ioa", 0, 2048), [[-1, 16], [1, 128]], 0, 0)
+    io(A("ioa", 0, 144), [[1, 144]], -15, 0)
     io(A("ioc", 128, 256), [[16, 8], [0, 16]], 0, 0)
     TURN = A("turn", 0, C)
     io(TURN, [[0, C // 4], [1, 4]], 0, 0)
@@ -119,7 +123,8 @@ def describe():
     ZERO = A("zero", 0, 128)
     ms(ZERO, 0.0)
     for w in WTS:
-        ts(Iw(w), IOC, 0.0, w, "is_equal", "mult")
+        if WTS.index(w) < V_IW: ts(Iw(w), IOC, 0.0, w, "is_equal", "mult")
+        else: sel(Iw(w), ZERO, [[1, 128]], w, 0, -1)
     CY1, CY2, CENT, CM = blk("cm", 0), blk("cm", 1), blk("cm", 2), blk("cm", 3)
     for o, parts in ((CY1, (-2560.0, 8.5)), (CY2, (3712.0, 7.875, 1.0 / 512)), (CENT, (121.0 * 65536, 16384.0 + XH / 2)),
                      (CM, (129.0 * 2048, 1.0))):
@@ -129,8 +134,9 @@ def describe():
         sel(blk("Rall", a), Iw(-1.0), [[16, 8], [0, 16]], 1.0, a, -1)
     ts(A("colj", 1, 2), A("colj", 0, 1), 112, None, "bitwise_and")
     ts(A("colj", 2, 3), A("colj", 0, 1), 15, None, "bitwise_and")
-    GP, KC, KH, K37, K512, KB, H1, H2, THC, PW, DN = 0, 1, 2, 3, 4, 5, 6, 7, 8, 9, 10
+    GP, KC, KH, K37, K512, KB, H1, H2, THC, PW, DN, K37B = 0, 1, 2, 3, 4, 5, 6, 7, 8, 9, 10, 13
     cp(A("colf", 0, 2), A("colj", 1, 3))
+    ts(cf(K37B), cf(KC), 37.0, float(NM), "mult", "add")
     ts(cf(KH), cf(KC), -0.5, 0.5, "mult", "add")
     ts(cf(K37), cf(KC), 37.0, None, "mult")
     ts(cf(K512), cf(KC), float(NP), None, "add")
@@ -141,10 +147,9 @@ def describe():
     ts(cf(H2), A("coli", 0, 1), 2.0, None, "mult")
     ts(cf(THC), A("coli", 8, 9), 0.5, None, "add")
     ts(A("colf", DN, DN + 3), A("coli", 16, 19), -0.5, -1.0 / 1024, "add", "mult")
-    ts(A("Sall", 0, 2048), A("ioa", 0, 2048), cf(GP), 0.5, "is_equal", "mult")
-    ts(A("Pall", 0, 2048), A("ioa", 0, 2048), cf(GP), cf(PW), "is_equal", "mult")
-    ts(A("Hall", 0, 2048), A("ioa", 0, 2048), cf(GP), cf(H1), "is_equal", "mult")
-    BD, HB, BH, LO, SHF = 0, 1, 2, 3, 4
+    for o, w in (("Sall", 0.5), ("Pall", cf(PW)), ("Hall", cf(H1))):
+        ts(A(o, 0, 144), A("ioa", 0, 144), cf(GP), w, "is_equal", "mult")
+    BD, HB, BH, LO, SHF, UP = 0, 1, 2, 3, 4, 7
     ts(mat(BD), A("ioc", 128, 256), cf(GP), None, "is_equal")
     ts(mat(HB), A("ioc", 128, 256), cf(GP), cf(H2), "is_equal", "mult")
     ts(mat(BH), A("ioc", 128, 256), cf(GP), -0.5, "is_equal", "mult")
@@ -152,6 +157,7 @@ def describe():
     ts(mat(6), IOC, -1.0, None, "is_equal")
     for j in range(2):
         tt(mat(LO + j), mat(5 + j), mat(BD), "mult")
+    if AGAIN: tt(mat(UP), mat(LO), mat(BH), "subtract")
     for t in range(ST):
         ts(blk("Dg", t), IOC, 0.0, cf(DN + t), "is_equal", "mult")
     ONE = A("ones", 0, C)
@@ -166,7 +172,9 @@ def describe():
         ms(A("rb0%d" % c, C, 2 * C), -1.0)
     for j in range(NM // 512):
         lo, hi = 512 * j, 512 * j + 512
-        if j % 2 == 0: ts(A("Zt", lo, lo + FXP), A("F", lo, lo + FXP), 16.0, -256.0, "is_lt", "mult")
+        if lo in (0,) + LOADS:
+            end = min(b for b in LOADS if b > lo)
+            ts(A("Zt", lo, end), A("F", lo, end), 16.0, -256.0, "is_lt", "mult")
         pb = A("ps%d" % (j % 8), 0, 512)
         lin(pb, [(1.0, A("F", lo, hi)), (1.0, A("Zt", lo, hi))])
         if j % 4 in V_EVAC: cp(A("Zt", lo, hi), pb)
@@ -195,36 +203,53 @@ def describe():
             x, hp, s = A(rb, 0, C), A(rb, C, 2 * C), A(rb, 2 * C, 3 * C)
             xn, hs, s6 = A(sb, 0, C), A(sb, C, 2 * C), A(sb, 2 * C, 3 * C)
             n32, nn32, nn16 = A("rn%d%d" % (t, c), 0, C), A("sn%d%d" % (t, c), 0, C), A("su%d%d" % (t, c), 0, C)
-            VF, VT, ca, cb = "VF" + cs_, "VT" + cs_, "ca" + cs_, "cb" + cs_
+            VG, VF, VT, ca, cb = "VG" + cs_, "VF" + cs_, "VT" + cs_, "ca" + cs_, "cb" + cs_
             cand, rl, Pk, e, sx, se, sg, ap_, pre, aw, yc, ad, hy, hv, eh, rr = [B(j) for j in range(16)]
             for j in range(C // PIECE):
                 lo, hi = 16 * j * PIECE, 16 * (j + 1) * PIECE
-                act(A(VF, lo, hi), IND(A("Zt", 0, NM), A("ru%d%d" % (t, c), j * PIECE, (j + 1) * PIECE)), "Identity")
+                src = IND(A("Zt", 0, NM), A("ru%d%d" % (t, c), j * PIECE, (j + 1) * PIECE))
+                if j in G_DERIVE:
+                    act(A(VG, lo, hi), src, "Identity", -2552.5, -1.0)
+                    sel(A(VT, 16 + lo, 16 + hi), A(VG, lo, hi), [[0, hi - lo]], 0.0, 1, 0)
+                    continue
+                act(A(VF, lo, hi), src, "Identity")
                 if j in V_DERIVE: ts(A(VT, 16 + lo, 16 + hi), A(VF, lo, hi), -1.0, -2552.5, "mult", "add")
                 else: act(A(VT, 16 + lo, 16 + hi), A(VF, lo, hi), "Identity", -2552.5, -1.0)
-            for h in range(R1):
-                lin(A(ps("y1")[0], h, R1 * C, R1), [(CY1, ONE), (1.0, x)])
             n, m = C // SUB, 16 // R1
             for j in range(SUB):
                 lo, hi = j * n, (j + 1) * n
+                wide = lo // PIECE in G_DERIVE
+                y1 = A(ps("y1")[0], R1 * lo, R1 * hi)
+                if G_DERIVE or j == 0:
+                    a, b = (lo, hi) if G_DERIVE else (0, C)
+                    for h in range(R1):
+                        o = A(y1[0], R1 * a + h, R1 * b, R1)
+                        if "y1" in ON_S: act(o, A(rb, a, b), "Identity", -1.0 if wide else -2551.5, -1.0 if wide else 1.0)
+                        elif wide: lin(o, [(-1.0, A("ones", a, b)), (-1.0, A(rb, a, b))])
+                        else: lin(o, [(CY1, A("ones", a, b)), (1.0, A(rb, a, b))])
                 for k in range(m):
-                    tt(A(ca, 16 * lo + R1 * k * n, 16 * lo + R1 * (k + 1) * n), A(VF, 16 * lo + k, 16 * hi, m), A(ps("y1")[0], R1 * lo, R1 * hi), "subtract")
+                    o = A(ca, 16 * lo + R1 * k * n, 16 * lo + R1 * (k + 1) * n)
+                    if wide: tt(o, y1, A(VG, 16 * lo + k, 16 * hi, m), "subtract")
+                    else: tt(o, A(VF, 16 * lo + k, 16 * hi, m), y1, "subtract")
                 lin(A(ps("cnt")[0], lo, hi), [(256.0, A(rb, 2 * C + lo, 2 * C + hi)), (4.0, A(rb, C + lo, C + hi))]
                     + [(blk("Sall", k), A(VT, 16 + 16 * lo + k, 16 + 16 * hi, 16)) for k in range(16)]
                     + [(blk("Sall", k + m * h), A(ca, 16 * lo + R1 * k * n + h, 16 * lo + R1 * (k + 1) * n, R1)) for k in range(m) for h in range(R1)])
             act(cand, ps("cnt"), "Sign", -72.0, -1.0)
             lin(ps("rl"), [(1.0, TURN), (mat(BH), cand)])
             act(rl, ps("rl"), "Relu", -7.0)
-            lin(ps("Pk"), [(1.0, TURN), (mat(LO), cand), (-1.0, rl)])
-            act(Pk, ps("Pk"), "Sign", cf(KH))
+            if AGAIN: lin(ps("rl"), [(mat(UP), cand), (-1.0, rl)], True)
+            else: lin(ps("Pk"), [(1.0, TURN), (mat(LO), cand), (-1.0, rl)])
+            act(Pk, ps("rl" if AGAIN else "Pk"), "Sign", cf(KH))
             pd = ps("idx", D)
             lin(pd, [(1.0, A("base", 0, D))] + [(blk("Pall", a), A(Pk[0], Pk[1] + a, Pk[2], 16)) for a in range(16)])
             ts(A("tu" + cs_, 0, D), pd, cf(KB), 0.0, "add", "max")
             act(e, IND(A(VT, 0, 16 * C + 16), A("tu" + cs_, 0, D)), "Relu", -160.0, -1.0 / 16)
             lin(ps("pre"), [(6.0, s), (1.0, cand), (mat(SHF), Pk)])
             act(pre, ps("pre"), "Sign", -1.5)
-            ts(sx, x, 0.0, None, "is_gt")
-            ts(se, e, 0.0, None, "is_gt")
+            if "sx" in ON_S: act(sx, x, "Sign")
+            else: ts(sx, x, 0.0, None, "is_gt")
+            if "se" in ON_S: act(se, e, "Sign")
+            else: ts(se, e, 0.0, None, "is_gt")
             lin(ps("dl"), [(1.0, x), (-1.0, e)])
             act(sg, ps("dl"), "Sign", 0.5)
             act(xn, ps("dl"), "Abs")
@@ -238,24 +263,24 @@ def describe():
             cint = A("cint", D * c, D * c + D)
             ts(cint, A("ti" + cs_, 0, D), 6, NP - 1, "arith_shift_right", "bitwise_and")
             cp(A("tu" + cs_, 16, 16 + D), cint)
-            cp(A("cf", D * c, D * c + D), cint)
             if c == NCH - 1:
                 pq = "ps%d" % bank["d"]
+                cp(A("cf", 0, DW), A("cint", 0, DW))
                 for a in range(16):
                     lin(A(pq, DW * a, DW * a + DW), [(blk("Rall", a), A("cf", 0, DW))])
                 tt(A("Eq", 0, NW), A(pq, 0, NW), A("mask", 0, NW), "is_equal")
-                lin(A(pq, 424, 424 + DW), [(blk("Sall", a), A("Eq", DW * a, DW * a + DW)) for a in range(16)])
-                ts(A("dd", 0, DW), A(pq, 424, 424 + DW), 0.0, 4096.0, "is_gt", "mult")
-                tt(A("dd", DW, 2 * DW), A("dd", 0, DW), A("cint", 0, DW), "add")
-                ts(A("soff", 0, 2 * DW, 2), A("dd", DW, 2 * DW), cf(K512), None, "min")
+                lin(A(pq, 424, 424 + DW), [(1.0 / 2048, A("cf", 0, DW))] + [(blk("Sall", a), A("Eq", DW * a, DW * a + DW)) for a in range(16)])
+                ts(A("soff", 0, 2 * DW, 2), A(pq, 424, 424 + DW), 2048.0, cf(K512), "mult", "min")
             lin(ps("rr"), [(mat(HB), xn)])
             act(rr, ps("rr"), "Identity", 128.5 + 1.0 / 2048, 1.0 / 2048)
             MUL, ADD, K3 = ps("mul"), ps("add"), ps("k3")
             if EARLY:
-                lin(MUL, [(CM, ONE), (mat(HB), xn), (-2048.0, rr)])
+                if AGAIN: lin(MUL, [(CM, ONE), (-2048.0, rr)], True)
+                else: lin(MUL, [(CM, ONE), (mat(HB), xn), (-2048.0, rr)])
                 tt(In(0), n32, MUL, "mult")
                 ts(In(1), In(0), 5, NM - 1, "arith_shift_right", "bitwise_and")
-                ts(MUL, n32, cf(K37), float(NM), "add", "add")
+                if "a1" in ON_S: act(MUL, n32, "Identity", cf(K37B))
+                else: ts(MUL, n32, cf(K37), float(NM), "add", "add")
                 tt(Fl(3), In(1), MUL, "add")
             act(Fl(0), IND(A("W", 0, NP + 16), A("tu" + cs_, 16, 16 + D)), "Identity")
             act(yc, Fl(0), "Identity", YB, 1.0 / 65536)
@@ -268,9 +293,13 @@ def describe():
             if EARLY: tt(Fl(4), Fl(3), K3, "min")
             tt(eh, n32, K3, "is_equal")
             act(hv, K3, "Sign", 8191.5, -1.0)
-            lin(ps("hy"), [(-1.0, xn), (1.0, yc), (16.0, hs)])
+            if AGAIN: lin(ps("hy"), [(16.0, hs)], True)
+            else: lin(ps("hy"), [(-1.0, xn), (1.0, yc), (16.0, hs)])
             act(hy, ps("hy"), "Relu", -129.0)
-            ts(Fl(1), ps("sum"), MAGIC, MAGIC, "add", "subtract")
+            if "mg" in ON_S:
+                act(Fl(2), ps("sum"), "Identity", MAGIC)
+                act(Fl(1), Fl(2), "Identity", -MAGIC)
+            else: ts(Fl(1), ps("sum"), MAGIC, MAGIC, "add", "subtract")
             tt(Fl(2), ps("sum"), Fl(1), "subtract")
             act(ap_, Fl(2), "Identity", 192.0, 16.0)
             lin(ps("thr"), [(blk("Dg", t), ONE), (-189.0 / 16, pre), (63.0 / 1024, ap_)])
@@ -292,7 +321,8 @@ def describe():
             lin(ps("s6"), [(1.0, eh), (-0.5, hv), (-1.0, aw)])
             act(s6, ps("s6"), "Relu", 0.5)
             if t < ST - 1:
-                cp(nn16, nn32)
+                if "u16" in ON_S: act(nn16, nn32, "Identity")
+                else: cp(nn16, nn32)
                 for call in SENDS:
                     to = [A("r%s%d%d" % (p_, t + 1, c), lo, hi) for p_, lo, hi in call]
                     ops.append(("G", "send", None, [A("s%s%d%d" % (p_, t, c), lo, hi) for p_, lo, hi in call], (to, arr[0])))
@@ -315,7 +345,7 @@ def describe():
         lin(A("ps%d" % j, 0, hi - lo), [(65536.0, A("oy1", lo, hi))])
         tt(A("oyj", lo, hi), A("W", lo, hi), A("ps%d" % j, 0, hi - lo), "subtract")
         ts(A("oyk", lo, hi), A("oyj", lo, hi), -16384.0, float(NM), "add", "min")
-    dma("Y", A("yk", 0, NP), A("oyk", 0, NP))
+        dma("Y", A("yk", lo, hi), A("oyk", lo, hi))
     act(A("oy2", 0, NP), A("oy1", 0, NP), "Identity", -129.0)
     dma("Y", A("yy", 0, NP), A("oy2", 0, NP))
     return ops
@@ -343,7 +373,7 @@ def cost(op, sc=SC):
     if kind == "mm":
         d = 20 + sc["pe"] * max(64, count(o)); return d, d + sc["lat"]
     if kind == "dma":
-        return 100, 2000 + count(o) * 128 * (2 if narrow(o) or narrow(ins[0]) else 4) / sc["bw"]
+        d = max(100, count(o) * 128 * (2 if narrow(o) or narrow(ins[0]) else 4) / sc["bw"]); return d, d + 2000
     if kind == "send": return 500, 500
     if kind == "recv":
         d = count(o) * 128 * (2 if narrow(o) else 4) / sc["lbw"]; return d, d + sc["link"]
@@ -369,7 +399,7 @@ def links():
         for r, isw in [(r, False) for r in rd] + [(r, True) for r in wr]:
             for j, lo, hi, w in hist.get(r[0], []):
                 if j != i and (w or isw) and lo < r[2] and r[1] < hi:
-                    (soft if op[0] == "P" and ops[j][0] == "P" else hard)[i].add(j)
+                    (soft if op[0] == ops[j][0] == "P" else hard)[i].add(j)
             if r[0][:2] == "ps":
                 j = bank.get(r[0])
                 if j is not None and j != i:
@@ -386,47 +416,49 @@ def links():
     return ops, hard, soft
 
 
-def plan(window=30, base=None, sc=SC, fixed=None):
-    ops, hard, soft = base or links()
-    n = len(ops)
-    cst = [cost(op, sc) for op in ops]
-    users = [[] for _ in range(n)]
-    for i in range(n):
-        for j in hard[i] | soft[i]: users[j].append(i)
-    prio = [0.0] * n
-    for i in range(n - 1, -1, -1):
-        prio[i] = cst[i][1] + max([prio[u] for u in users[i]] + [0.0])
-    for i in range(n):
-        o = ops[i][2] or ops[i][3][0]
-        prio[i] -= LEAD * sum(c for lo, hi, c in SPANS[:ST * NCH] if lo <= i < hi)
-        if ops[i][1] in ("act", "cp") and ops[i][3][0][0] == "@" and count(o) > C: prio[i] -= LATE
-    left = [len(hard[i] | soft[i]) for i in range(n)]
-    ready = [i for i in range(n) if left[i] == 0]
-    at = [0.0] * n
-    start = [0.0] * n
-    free = {q: 0.0 for q in "VSPGYR"}
-    dmafree = [0.0]
-    order = []
-    while ready:
-        if fixed: i = fixed[len(order)]
-        else:
-            first = min(max(at[i], free[ops[i][0]]) for i in ready)
-            i = max((i for i in ready if max(at[i], free[ops[i][0]]) <= first + window), key=lambda k: (prio[k], -k))
-        ready.remove(i)
-        q = ops[i][0]
-        start[i] = max(at[i], free[q]); free[q] = start[i] + cst[i][0]
-        end = start[i] + cst[i][1]
-        if ops[i][1] == "dma":
-            dmafree[0] = max(dmafree[0], start[i] + 2000) + cst[i][1] - 2000
-            end = dmafree[0]
+def schedule(q, dur, tail, prio, pre, suc, window=30):
+    n = len(q)
+    left = [len(p) for p in pre]
+    ready = {k: [i for i in range(n) if q[i] == k and not left[i]] for k in "VSPGYR"}
+    at, start, free, order, end = [0.0] * n, [0.0] * n, dict.fromkeys("VSPGYR", 0.0), [], 0.0
+    for _ in range(n):
+        first, k = min((max(free[k], min([at[i] for i in L])), k) for k, L in ready.items() if L)
+        i = max((prio[i], -i) for i in ready[k] if at[i] <= first + window)[1] * -1
+        ready[k].remove(i)
+        start[i] = max(at[i], free[k]); free[k] = start[i] + dur[i]; end = max(end, free[k] + tail[i])
         order.append(i)
-        for u in users[i]:
-            at[u] = max(at[u], end + 40 if i in hard[u] else start[i] + cst[i][0])
-            left[u] -= 1
-            if left[u] == 0: ready.append(u)
+        for u, gap in suc[i]:
+            at[u] = max(at[u], free[k] + gap); left[u] -= 1
+            if not left[u]: ready[q[u]].append(u)
+    return end, start, order
+
+
+def plan(sc=SC):
+    ops, hard, soft = links()
+    n = len(ops)
+    q, dur, tail = [op[0] for op in ops], [cost(op, sc)[0] for op in ops], [cost(op, sc)[1] - cost(op, sc)[0] for op in ops]
+    pre = [[(j, tail[j] + 40 if j in hard[i] else 0.0) for j in sorted(hard[i] | soft[i])] for i in range(n)]
+    suc = [[] for _ in range(n)]
+    for i in range(n):
+        for j, gap in pre[i]: suc[j].append((i, gap))
+    way = [0.0] * n
+    for i in range(n - 1, -1, -1):
+        way[i] = dur[i] + max([way[u] + gap for u, gap in suc[i]] + [tail[i]])
+    best = None
+    for lead in LEADS:
+        for late in LATES:
+            prio = way[:]
+            for lo, hi, c in SPANS[:ST * NCH]:
+                for i in range(lo, hi):
+                    prio[i] -= lead * c + (late if ops[i][1] == "act" and ops[i][3][0][0] == "@" and count(ops[i][2]) > C else 0)
+            for _ in range(4):
+                got = schedule(q, dur, tail, prio, pre, suc)
+                if best is None or got[0] < best[0]: best = got
+                back = schedule(q, dur, [0.0] * n, [got[1][i] + dur[i] for i in range(n)], suc, pre)[1]
+                prio = [back[i] + dur[i] for i in range(n)]
     needed = set()
     for i in range(n): needed |= hard[i]
-    return ops, hard, order, needed, start, soft
+    return ops, hard, best[2], needed, best[1], soft, best[0]
 
 
 PLAN = []

@@ -11,23 +11,38 @@ SPANS = []
 LOADS = (512, 1536, 2560, 3584, 4608, 5632, 6656, 7680, 8192)
 V_EVAC = (3,)
 V_DERIVE = (0, 1, 2, 3)
+CUT = 1
+V_GATHER = ()
 G_DERIVE = ()
-V_IW = 8
+V_IW = 14
+TRIM = True
+LEAN = 0
+FIRM = False
+YB_AT = 6
+S_ROWS = 0
+WIDE = ("out",)
 MAGIC = 1.5 * 2.0 ** 26
 XA, XH = 25600.0, 28672.0
-WTS = [1.0, -1.0, 4.0, 256.0, 6.0, 8.0, 136.0, -512.0, 65536.0, 16384.0, 16.0, 63.0 / 1024, -189.0 / 16, -2048.0, 4096.0, -0.5,
-       -524288.0 + XH / 2, XA, -XH, 8192.0, 1.0 / 2048]
-ON_S = ("sx", "se")
+ON_S = ("a1", "u16", "tu", "cand", "rl", "Pk", "pre", "sg", "rr", "yc", "hs", "hv", "hy", "s6", "d1", "aw", "add", "n32", "ti", "set")
+FC, FP, FR, FG, FH, FV = [1.0 if _n in ON_S else 2.0 for _n in ("cand", "Pk", "pre", "sg", "hs", "hv")]
+WTS = []
+for _w in [1.0, -1.0, 4.0 * FH, 256.0, 6.0, 8.0, 136.0 * FG, -512.0, 65536.0, 16384.0 * FH, 16.0 * FH, 63.0 / 1024, -189.0 / 16 * FR, -2048.0, 4096.0,
+           -0.5 * FV, (-524288.0 + XH / 2) * FH, XA, -XH, 8192.0, 1.0 / 2048, FC] + [-65536.0, -16384.0 * FH] * (len(WIDE) > 0) + [16.0] + [-8.0, FR] * (LEAN > 0):
+    if _w not in WTS and not (TRIM and _w == 4096.0) and not (LEAN and _w in (63.0 / 1024, -189.0 / 16 * FR)): WTS.append(_w)
 LEADS = (0, 2000, 4000)
 LATES = (0, 3000, 6000)
 AGAIN = False
+SCAN = ("idx", "u")
+WHOLE = False
 SUB = 2
-EARLY = True
-SENDS = ([("b", 0, 2 * C)], [("u", 0, C), ("b", 2 * C, 3 * C)], [("n", 0, C)])
+EARLY = 2
+SENDS = ([("b", 0, C)], [("u", 0, C)], [("b", C, 3 * C)])
 if NCH == 2:
     SLOTS = {"y1": ("y", 0), "cnt": ("a", 0), "rl": ("z", 0), "Pk": ("z", C), "idx": ("z", 384), "pre": ("w", 0), "dl": ("z", 0),
              "y2": ("y", 0), "sum": ("a", 0), "u": ("z", 400), "rr": ("w", C), "ad": ("z", 0), "hs": ("z", C), "k3": ("w", 0),
              "hy": ("z", 0), "thr": ("y", 0), "mul": ("w", C) if EARLY else ("z", C), "add": ("a", C), "s6": ("y", C), "yt": ("y", 0), "ent": ("z", C)}
+    if S_ROWS: SLOTS.update({"rr": ("z", C), "mul": ("z", C), "hs": ("z", 0), "k3": ("z", 0), "hy": ("z", C), "ent": ("w", 0), "q": ("w", C)})
+    else: SLOTS["q"] = SLOTS["mul"]
 else:
     SLOTS = {"y1": ("y", 0), "cnt": ("a", 0), "rl": ("y", 0), "Pk": ("a", C), "idx": ("y", C), "pre": ("a", 2 * C), "dl": ("a", 3 * C),
              "y2": ("y", 0), "sum": ("a", 0), "u": ("z", 3 * C), "rr": ("z", 0), "ad": ("z", C), "hs": ("z", 2 * C), "k3": ("z", 0),
@@ -36,10 +51,10 @@ else:
 SCRATCH = {}
 for _n, _w, _d in [
         ("F", NM, "bfloat16"), ("Zt", NM, "bfloat16"),
-        ("ioa", 144, "bfloat16"), ("zero", 128, "bfloat16"), ("Sall", 144, "bfloat16"), ("Hall", 144, "bfloat16"),
+        ("ioa", 144, "bfloat16"), ("zero", 128, "bfloat16"), ("If", 128, "float32"), ("Sall", 144, "bfloat16"), ("Hall", 144, "bfloat16"),
         ("Pall", 144, "bfloat16"), ("Rall", 2048, "bfloat16"), ("ioc", 256, "bfloat16"), ("mats", 128 * 8, "bfloat16"),
-        ("Iw", 128 * len(WTS), "bfloat16"), ("cm", 128 * 4, "bfloat16"), ("Dg", 128 * ST, "bfloat16"), ("ones", C, "bfloat16"),
-        ("turn", C, "bfloat16"), ("base", 16, "bfloat16"), ("mask", NW, "float32"), ("coli", 32, "int32"), ("colj", 8, "int32"),
+        ("Iw", 128 * len(WTS), "bfloat16"), ("cm", 128 * 5, "bfloat16"), ("Dg", 128 * ST, "bfloat16"), ("ones", C, "bfloat16"),
+        ("turn", 2 * C, "bfloat16"), ("own", 3 * C, "bfloat16"), ("base", 16, "bfloat16"), ("mask", NW, "float32"), ("coli", 32, "int32"), ("colj", 8, "int32"),
         ("colf", 32, "float32"), ("t0s", NW, "int32"), ("y0s", NP, "bfloat16"), ("k0s", NP, "int32"), ("kz", NP, "bfloat16"),
         ("W", NP + 16, "float32"), ("ent", NW, "float32"), ("cf", 24, "float16"), ("cint", 24, "int32"), ("Eq", NW, "bfloat16"),
         ("dd", 48, "float32"), ("soff", 48, "uint16"), ("oyt", NW, "float32"), ("oy1", NP, "bfloat16"), ("oy2", NP, "bfloat16"),
@@ -47,19 +62,19 @@ for _n, _w, _d in [
     SCRATCH[_n] = ("sbuf", [128, _w], _d)
 for _c in range(NCH):
     for _n, _w, _d in [("VG", 16 * C, "float32"), ("VF", 16 * C, "bfloat16"), ("VT", 16 * C + 16, "bfloat16"), ("ca", 16 * C, "bfloat16"), ("cb", 16 * C, "float16"),
-                       ("b", 20 * C, "bfloat16"), ("f", 5 * C, "float32"), ("i", 3 * C, "int32"),
+                       ("b", 20 * C, "bfloat16"), ("f", 6 * C, "float32"), ("i", 3 * C, "int32"),
                        ("ti", 16, "int32"), ("tu", 32, "uint16")]:
         SCRATCH[_n + str(_c)] = ("sbuf", [128, _w], _d)
     for _t in range(ST):
         for _p in "rs":
             SCRATCH["%sb%d%d" % (_p, _t, _c)] = ("sbuf", [128, 3 * C], "bfloat16")
-            SCRATCH["%sn%d%d" % (_p, _t, _c)] = ("sbuf", [128, C], "int32")
+            SCRATCH["%sn%d%d" % (_p, _t, _c)] = ("sbuf", [128, C], "float32" if WIDE and _p == "r" else "int32")
             SCRATCH["%su%d%d" % (_p, _t, _c)] = ("sbuf", [128, C], "uint16")
 for _k in range(8):
     SCRATCH["ps%d" % _k] = ("psum", [128, 512], "float32")
 DRAM = ("fx", "y0", "k0", "x0", "t0", "dw", "hw", "th", "yx", "yt", "yy", "yk")
 NDMA = len(LOADS) + 10 + 3 * NCH
-SEMAPHORES = ["V", "S", "P", "G", "sent"] + ["d%d" % _k for _k in range(NDMA)] + ["a%d" % _k for _k in range(8 * NCH)]
+SEMAPHORES = ["V", "S", "P", "G", "sent"] + ["d%d" % _k for _k in range(NDMA)] + ["a%d" % _k for _k in range(10 * NCH)]
 
 
 def A(name, lo, hi, step=1):
@@ -85,11 +100,12 @@ def describe():
 
     def tt(o, a, b, op): ops.append(("V", "tt", o, [a, b], op))
     def ts(o, a, s1, s2, op0, op1=None): ops.append(("V", "ts", o, [a, s1, s2], (op0, op1)))
+    def scan(o, a, b): ops.append(("V", "scan", o, [a, b], None))
     def cp(o, a): ops.append(("V", "cp", o, [a], None))
     def ms(o, v): ops.append(("V", "ms", o, [], v))
     def act(o, a, f, bias=0.0, scale=1.0): ops.append(("S", "act", o, [a, bias, scale], f))
     def io(o, pat, base, cm): ops.append(("G", "iota", o, [], (pat, base, cm)))
-    def sel(o, a, pat, fill, base, cm): ops.append(("G", "sel", o, [a], (pat, base, cm, fill)))
+    def sel(o, a, pat, fill, base, cm, op="not_equal"): ops.append(("G", "sel", o, [a], (pat, base, cm, fill, op)))
     def dma(q, o, a): ops.append((q, "dma", o, [a], None))
     def Iw(w): return A("Iw", 128 * WTS.index(w), 128 * WTS.index(w) + 128)
     def mat(j): return A("mats", 128 * j, 128 * j + 128)
@@ -97,9 +113,20 @@ def describe():
         return A(n, 15 - a, 143 - a) if n in ("Sall", "Pall", "Hall") else A(n, 128 * a, 128 * a + 128)
     def cf(j): return A("colf", j, j + 1)
 
-    def lin(o, terms, more=False):
+    def aff(name, o, a, scale=1.0, bias=0.0, relu=False):
+        if name in ON_S: act(o, a, "Relu" if relu else "Identity", bias, scale)
+        elif relu: ts(o, a, bias, 0.0, "add", "max")
+        elif scale == 1.0 and bias == 0.0: cp(o, a)
+        elif scale == 1.0: ts(o, a, bias, None, "add")
+        else: ts(o, a, scale, bias, "mult", "add")
+
+    def sign(name, o, a, bias, scale, thr):
+        if name in ON_S: act(o, a, "Sign", bias, scale)
+        else: ts(o, a, thr, 0.5, "is_gt" if scale > 0 else "is_lt", "subtract")
+
+    def lin(o, terms, more=False, close=True):
         for j, (l, r) in enumerate(terms):
-            ops.append(("P", "mm", o, [Iw(l) if isinstance(l, float) else l, r], (j == 0 and not more, j == len(terms) - 1)))
+            ops.append(("P", "mm", o, [Iw(l) if isinstance(l, float) else l, r], (j == 0 and not more, close and j == len(terms) - 1)))
 
     dma("Y", A("t0s", 0, NW), A("t0", 0, NW))
     for lo, hi in zip((0,) + LOADS, LOADS):
@@ -114,8 +141,9 @@ def describe():
     io(A("ioa", 0, 144), [[1, 144]], -15, 0)
     io(A("ioc", 128, 256), [[16, 8], [0, 16]], 0, 0)
     TURN = A("turn", 0, C)
-    io(TURN, [[0, C // 4], [1, 4]], 0, 0)
-    io(A("base", 0, D), [[256, D]], 0, 0)
+    if "rl" in ON_S: io(TURN, [[0, C // 4], [1, 4]], 0, 0)
+    else: io(A("turn", C, 2 * C), [[0, C // 4], [-1, 4]], 7, 0)
+    if not (TRIM and "idx" in SCAN): io(A("base", 0, D), [[256, D]], 0, 0)
     dma("G", A("coli", 0, 1), A("hw", 0, 1))
     dma("G", A("coli", 8, 9), A("th", 0, 1))
     dma("G", A("coli", 16, 19), A("dw", 0, 3))
@@ -125,51 +153,62 @@ def describe():
     for w in WTS:
         if WTS.index(w) < V_IW: ts(Iw(w), IOC, 0.0, w, "is_equal", "mult")
         else: sel(Iw(w), ZERO, [[1, 128]], w, 0, -1)
-    CY1, CY2, CENT, CM = blk("cm", 0), blk("cm", 1), blk("cm", 2), blk("cm", 3)
+    CY1, CY2, CENT, CM, CW = [blk("cm", j) for j in range(5)]
     for o, parts in ((CY1, (-2560.0, 8.5)), (CY2, (3712.0, 7.875, 1.0 / 512)), (CENT, (121.0 * 65536, 16384.0 + XH / 2)),
-                     (CM, (129.0 * 2048, 1.0))):
+                     (CM, (129.0 * 2048, 1.0)), (CW, (129.0 * 65536, 16384.0))):
         for j, v in enumerate(parts):
             sel(o, o if j else ZERO, [[0, 128]], v, -j, 1)
     for a in range(16):
         sel(blk("Rall", a), Iw(-1.0), [[16, 8], [0, 16]], 1.0, a, -1)
     ts(A("colj", 1, 2), A("colj", 0, 1), 112, None, "bitwise_and")
     ts(A("colj", 2, 3), A("colj", 0, 1), 15, None, "bitwise_and")
-    GP, KC, KH, K37, K512, KB, H1, H2, THC, PW, DN, K37B = 0, 1, 2, 3, 4, 5, 6, 7, 8, 9, 10, 13
+    GP, KC, KH, K37, K512, KB, H1, H2, THC, PW, DN, K37B, KM = 0, 1, 2, 3, 4, 5, 6, 7, 8, 9, 10, 13, 14
     cp(A("colf", 0, 2), A("colj", 1, 3))
-    ts(cf(K37B), cf(KC), 37.0, float(NM), "mult", "add")
-    ts(cf(KH), cf(KC), -0.5, 0.5, "mult", "add")
-    ts(cf(K37), cf(KC), 37.0, None, "mult")
-    ts(cf(K512), cf(KC), float(NP), None, "add")
-    ts(cf(KB), cf(KC), 16.0, 23.5 - 2048, "mult", "add")
-    ts(cf(PW), cf(KC), 0.0, 2047.5, "is_equal", "mult")
-    ts(cf(PW), cf(PW), 0.5, None, "add")
-    cp(cf(H1), A("coli", 0, 1))
-    ts(cf(H2), A("coli", 0, 1), 2.0, None, "mult")
-    ts(cf(THC), A("coli", 8, 9), 0.5, None, "add")
-    ts(A("colf", DN, DN + 3), A("coli", 16, 19), -0.5, -1.0 / 1024, "add", "mult")
-    for o, w in (("Sall", 0.5), ("Pall", cf(PW)), ("Hall", cf(H1))):
-        ts(A(o, 0, 144), A("ioa", 0, 144), cf(GP), w, "is_equal", "mult")
-    BD, HB, BH, LO, SHF, UP = 0, 1, 2, 3, 4, 7
+    for j, scale, bias in ((K37B, 37.0, float(NM)), (KH, -0.5 if FP == 1 else 0.5, (0.5 if "rl" in ON_S else 7.5) * (1 if FP == 1 else -1)), (K37, 37.0, 0.0), (K512, 1.0, float(NP)),
+                           (KB, 16.0, 23.5 - 2048), (KM, -4096.0, 2048.0)):
+        if not (TRIM and (j == KB and "idx" in SCAN or j == K37B and EARLY != 1 or j == K37 and EARLY == 1)): aff("set", cf(j), cf(KC), scale, bias)
+    act(cf(PW), cf(KC), "Relu", 4095.0 * FP, -4096.0 * FP)
+    aff("set", cf(PW), cf(PW), 1.0, FP)
+    aff("set", cf(H2), A("coli", 0, 1), 2.0)
+    aff("set", cf(THC), A("coli", 8, 9), 1.0, 0.5)
+    aff("set", A("colf", DN, DN + 3), A("coli", 16, 19), -1.0 / 1024, 0.5 / 1024 + (1 - 189.0 / 16) * (LEAN > 0))
+    ts(A("Sall", 0, 144), A("ioa", 0, 144), cf(GP), 0.5, "is_equal", "mult")
+    for o, j in (("Pall", PW), ("Hall", H2)):
+        if not (TRIM and ("idx" if j == PW else "u") in SCAN): aff("set", A(o, 0, 144), A("Sall", 0, 144), cf(j))
+    BD, HB, BH, LO, SHF = 0, 1, 2, 3, 4
     ts(mat(BD), A("ioc", 128, 256), cf(GP), None, "is_equal")
-    ts(mat(HB), A("ioc", 128, 256), cf(GP), cf(H2), "is_equal", "mult")
-    ts(mat(BH), A("ioc", 128, 256), cf(GP), -0.5, "is_equal", "mult")
-    ts(mat(5), IOC, 0.0, -0.5, "is_gt", "mult")
-    ts(mat(6), IOC, -1.0, None, "is_equal")
-    for j in range(2):
-        tt(mat(LO + j), mat(5 + j), mat(BD), "mult")
-    if AGAIN: tt(mat(UP), mat(LO), mat(BH), "subtract")
-    for t in range(ST):
-        ts(blk("Dg", t), IOC, 0.0, cf(DN + t), "is_equal", "mult")
+    aff("set", mat(HB), mat(BD), cf(H2))
+    aff("set", mat(BH), mat(BD), -0.5 * FC)
+    BP = 5
+    if SCAN:
+        aff("set", cf(PW + 7), cf(PW), 0.5)
+        aff("set", mat(BP), mat(BD), cf(PW + 7))
+        io(A("own", 0, C), [[0, D], [1, 16]], 0, 0)
+        io(A("own", C, 2 * C), [[16, C]], 0, 0)
+        ts(A("own", 0, C), A("own", 0, C), cf(KC), 131072.0, "not_equal", "mult")
+        tt(A("own", C, 2 * C), A("own", C, 2 * C), A("own", 0, C), "max")
+        aff("set", A("own", 2 * C, 3 * C), A("own", 0, C), -2.0, 262144.0)
+    sel(mat(LO), mat(BH), [[1, 128]], 0.0, 0, -1, "is_gt")
+    if FP > 1: aff("set", mat(6), mat(BD), FP)
+    sel(mat(SHF), mat(BD if FP == 1 else 6), [[1, 128]], 0.0, 1, -1, "is_equal")
+    if LEAN: aff("set", mat(7), mat(BD), -8.0)
+    for t in range(0 if LEAN else ST):
+        aff("set", blk("Dg", t), Iw(1.0), cf(DN + t))
+    IF = A("If", 0, 128)
+    if WIDE: act(IF, Iw(1.0), "Identity")
     ONE = A("ones", 0, C)
-    ms(ONE, 1.0)
-    ts(A("mask", 0, NW), A("mask", 0, NW), cf(KC), 0.5, "is_ge", "mult")
+    io(ONE, [[0, C]], 1, 0)
+    act(A("mask", 0, NW), A("mask", 0, NW), "Relu", cf(KM), 4096.0)
     ms(A("soff", 0, 48), 0)
     for c in range(NCH):
-        ms(A("VT%d" % c, 0, 16), -2304.0)
-        ts(A("rn0%d" % c, 0, C), A("t0s", c * C, (c + 1) * C), NM - 1, None, "bitwise_and")
-        cp(A("ru0%d" % c, 0, C), A("rn0%d" % c, 0, C))
+        io(A("VT%d" % c, 0, 16), [[0, 16]], -2304, 0)
+        n0 = A("i%d" % c if WIDE else "rn0%d" % c, 0, C)
+        ts(n0, A("t0s", c * C, (c + 1) * C), NM - 1, None, "bitwise_and")
+        aff("set", A("ru0%d" % c, 0, C), n0)
+        if WIDE: act(A("rn0%d" % c, 0, C), n0, "Identity")
         ts(A("rb0%d" % c, 2 * C, 3 * C), A("t0s", c * C, (c + 1) * C), float(NM), None, "is_ge")
-        ms(A("rb0%d" % c, C, 2 * C), -1.0)
+        if FH == 1: io(A("rb0%d" % c, C, 2 * C), [[0, C]], -1, 0)
+        else: ms(A("rb0%d" % c, C, 2 * C), -0.5)
     for j in range(NM // 512):
         lo, hi = 512 * j, 512 * j + 512
         if lo in (0,) + LOADS:
@@ -179,11 +218,12 @@ def describe():
         lin(pb, [(1.0, A("F", lo, hi)), (1.0, A("Zt", lo, hi))])
         if j % 4 in V_EVAC: cp(A("Zt", lo, hi), pb)
         else: act(A("Zt", lo, hi), pb, "Identity")
-    ms(A("W", NP, NP + 16), 0.0)
-    ts(A("kz", 0, NP), A("k0s", 0, NP), float(NM), XH, "is_ge", "mult")
-    lin(A("ps3", 0, NP), [(65536.0, A("y0s", 0, NP)), (1.0, A("kz", 0, NP))])
-    tt(A("oyj", 0, NP), A("k0s", 0, NP), A("ps3", 0, NP), "add")
-    act(A("W", 0, NP), A("oyj", 0, NP), "Identity", 129.0 * 65536 + 16384)
+    io(A("W", NP, NP + 16), [[0, 16]], 0, 0)
+    act(A("kz", 0, NP), A("k0s", 0, NP), "Relu", -XH * (NM - 1), XH)
+    for lo in range(0, NP, C):
+        hi = min(NP, lo + C)
+        lin(A("ps3", lo, hi), [(CW, A("ones", 0, hi - lo)), (65536.0, A("y0s", lo, hi)), (1.0, A("kz", lo, hi))])
+    tt(A("W", 0, NP), A("k0s", 0, NP), A("ps3", 0, NP), "add")
     YB = -0.25 - 61.0 / 128
 
     arr = [0]
@@ -204,7 +244,8 @@ def describe():
             xn, hs, s6 = A(sb, 0, C), A(sb, C, 2 * C), A(sb, 2 * C, 3 * C)
             n32, nn32, nn16 = A("rn%d%d" % (t, c), 0, C), A("sn%d%d" % (t, c), 0, C), A("su%d%d" % (t, c), 0, C)
             VG, VF, VT, ca, cb = "VG" + cs_, "VF" + cs_, "VT" + cs_, "ca" + cs_, "cb" + cs_
-            cand, rl, Pk, e, sx, se, sg, ap_, pre, aw, yc, ad, hy, hv, eh, rr = [B(j) for j in range(16)]
+            cand, rl, Pk, e, sx, se, sg, ap_, pre, aw, yc, ad, hy, hv, eh, rr, sumE = [B(j) for j in range(17)]
+            if t and SENDS[-1][-1][0] != "n": aff("n32", n32, A("ru%d%d" % (t, c), 0, C))
             for j in range(C // PIECE):
                 lo, hi = 16 * j * PIECE, 16 * (j + 1) * PIECE
                 src = IND(A("Zt", 0, NM), A("ru%d%d" % (t, c), j * PIECE, (j + 1) * PIECE))
@@ -212,7 +253,11 @@ def describe():
                     act(A(VG, lo, hi), src, "Identity", -2552.5, -1.0)
                     sel(A(VT, 16 + lo, 16 + hi), A(VG, lo, hi), [[0, hi - lo]], 0.0, 1, 0)
                     continue
-                act(A(VF, lo, hi), src, "Identity")
+                for h in range(CUT):
+                    w0, w1 = j * PIECE + h * PIECE // CUT, j * PIECE + (h + 1) * PIECE // CUT
+                    src = IND(A("Zt", 0, NM), A("ru%d%d" % (t, c), w0, w1))
+                    if (t, c, j) in V_GATHER: cp(A(VF, 16 * w0, 16 * w1), src)
+                    else: act(A(VF, 16 * w0, 16 * w1), src, "Identity")
                 if j in V_DERIVE: ts(A(VT, 16 + lo, 16 + hi), A(VF, lo, hi), -1.0, -2552.5, "mult", "add")
                 else: act(A(VT, 16 + lo, 16 + hi), A(VF, lo, hi), "Identity", -2552.5, -1.0)
             n, m = C // SUB, 16 // R1
@@ -231,38 +276,80 @@ def describe():
                     o = A(ca, 16 * lo + R1 * k * n, 16 * lo + R1 * (k + 1) * n)
                     if wide: tt(o, y1, A(VG, 16 * lo + k, 16 * hi, m), "subtract")
                     else: tt(o, A(VF, 16 * lo + k, 16 * hi, m), y1, "subtract")
-                lin(A(ps("cnt")[0], lo, hi), [(256.0, A(rb, 2 * C + lo, 2 * C + hi)), (4.0, A(rb, C + lo, C + hi))]
-                    + [(blk("Sall", k), A(VT, 16 + 16 * lo + k, 16 + 16 * hi, 16)) for k in range(16)]
-                    + [(blk("Sall", k + m * h), A(ca, 16 * lo + R1 * k * n + h, 16 * lo + R1 * (k + 1) * n, R1)) for k in range(m) for h in range(R1)])
-            act(cand, ps("cnt"), "Sign", -72.0, -1.0)
-            lin(ps("rl"), [(1.0, TURN), (mat(BH), cand)])
-            act(rl, ps("rl"), "Relu", -7.0)
-            if AGAIN: lin(ps("rl"), [(mat(UP), cand), (-1.0, rl)], True)
-            else: lin(ps("Pk"), [(1.0, TURN), (mat(LO), cand), (-1.0, rl)])
-            act(Pk, ps("rl" if AGAIN else "Pk"), "Sign", cf(KH))
-            pd = ps("idx", D)
-            lin(pd, [(1.0, A("base", 0, D))] + [(blk("Pall", a), A(Pk[0], Pk[1] + a, Pk[2], 16)) for a in range(16)])
-            ts(A("tu" + cs_, 0, D), pd, cf(KB), 0.0, "add", "max")
+                sums = [(blk("Sall", k + m * h), A(ca, 16 * lo + R1 * k * n + h, 16 * lo + R1 * (k + 1) * n, R1)) for k in range(m) for h in range(R1)]
+                if LEAN:
+                    se_ = A(sumE[0], sumE[1] + lo, sumE[1] + hi)
+                    if LEAN == 2 or j == 0:
+                        a, b = (lo, hi) if LEAN == 2 else (0, C)
+                        lin(A(ps("pre")[0], a, b), [(blk("Sall", k), A(VT, 16 + 16 * a + k, 16 + 16 * b, 16)) for k in range(16)])
+                        aff("st", A(sumE[0], sumE[1] + a, sumE[1] + b), A(ps("pre")[0], a, b), -0.125, -2560.0)
+                    lin(A(ps("cnt")[0], lo, hi), sums[:12] + [(256.0, A(rb, 2 * C + lo, 2 * C + hi)), (4.0 * FH, A(rb, C + lo, C + hi)), (-8.0, se_)] + sums[12:])
+                elif WHOLE:
+                    if j == 0: lin(ps("cnt"), [(4.0 * FH, hp)], close=False)
+                    if j == SUB - 1: lin(ps("cnt"), [(256.0, s)] + [(blk("Sall", k), A(VT, 16 + k, 16 + 16 * C, 16)) for k in range(16)], True, False)
+                    lin(A(ps("cnt")[0], lo, hi), sums, True, j == SUB - 1)
+                else:
+                    flag = [(4.0 * FH, A(rb, C + lo, C + hi))]
+                    lin(A(ps("cnt")[0], lo, hi), flag * (SENDS[0][0][2] > C)
+                        + [(blk("Sall", k), A(VT, 16 + 16 * lo + k, 16 + 16 * hi, 16)) for k in range(16)]
+                        + sums[:8] + [(256.0, A(rb, 2 * C + lo, 2 * C + hi))] + flag * (SENDS[0][0][2] == C) + sums[8:])
+            sign("cand", cand, ps("cnt"), 20480.0 * (LEAN > 0) - 72, -1.0, 20480.0 * (LEAN > 0) - 72)
+            if "rl" in ON_S:
+                lin(ps("rl"), [(1.0, TURN), (mat(BH), cand)])
+                act(rl, ps("rl"), "Relu", -7.0)
+                lin(ps("Pk"), [(1.0, TURN), (mat(LO), cand), (-1.0, rl)])
+            else:
+                lin(ps("rl"), [(mat(BH), cand)])
+                tt(rl, A("turn", C, 2 * C), ps("rl"), "max")
+                lin(ps("Pk"), [(mat(LO), cand), (-1.0, rl)])
+            sign("Pk", Pk, ps("Pk"), cf(KH), 1.0, cf(KH))
+            def pick(o): return A(o[0], o[1] + 15, o[2], 16)
+            if "idx" in SCAN:
+                lin(ps("rl"), [(1.0, A("own", C, 2 * C)), (mat(BP), Pk)])
+                scan(Fl(0), A("own", 2 * C, 3 * C), ps("rl"))
+                ts(A("tu" + cs_, 0, D), pick(Fl(0)), 23.5 - 2048, 0.0, "add", "max")
+            else:
+                pd = ps("idx", D)
+                lin(pd, [(1.0, A("base", 0, D))] + [(blk("Pall", a), A(Pk[0], Pk[1] + a, Pk[2], 16)) for a in range(16)])
+                ts(A("tu" + cs_, 0, D), pd, cf(KB), 0.0, "add", "max")
             act(e, IND(A(VT, 0, 16 * C + 16), A("tu" + cs_, 0, D)), "Relu", -160.0, -1.0 / 16)
-            lin(ps("pre"), [(6.0, s), (1.0, cand), (mat(SHF), Pk)])
-            act(pre, ps("pre"), "Sign", -1.5)
+            lin(ps("pre"), [(6.0, s), (FC, cand), (mat(SHF), Pk)])
+            sign("pre", pre, ps("pre"), -1.5, 1.0, 1.5)
             if "sx" in ON_S: act(sx, x, "Sign")
             else: ts(sx, x, 0.0, None, "is_gt")
             if "se" in ON_S: act(se, e, "Sign")
             else: ts(se, e, 0.0, None, "is_gt")
             lin(ps("dl"), [(1.0, x), (-1.0, e)])
-            act(sg, ps("dl"), "Sign", 0.5)
+            sign("sg", sg, ps("dl"), 0.5, 1.0, -0.5)
             act(xn, ps("dl"), "Abs")
-            lin(ps("y2"), [(CY2, ONE), (8.0, x), (-512.0, sx), (8.0, e), (-512.0, se), (136.0, sg), (8.0, xn)])
-            for k in range(16):
+            lin(ps("y2"), [(CY2, ONE), (8.0, x), (-512.0, sx), (8.0, e), (-512.0, se), (136.0 * FG, sg), (8.0, xn)])
+            C2 = 2560.0 - 0.125 + 1.0 / 512
+            if S_ROWS: aff("yb", rl, ps("y2"), 1.0 / 16, -C2 / 16)
+            for k in range(16 - S_ROWS):
+                if LEAN and not S_ROWS and k == YB_AT: aff("yb", rl, ps("y2"), 1.0 / 16, -C2 / 16)
                 tt(A(cb, k * C, (k + 1) * C), A(VT, 16 + k, 16 + 16 * C, 16), ps("y2"), "add")
-            lin(ps("sum"), [(blk("Sall", k), A(cb, k * C, (k + 1) * C)) for k in range(16)])
-            pu = ps("u", D)
-            lin(pu, [(blk("Hall", a), A(sb, a, C, 16)) for a in range(16)])
-            ts(A("ti" + cs_, 0, D), pu, 241.0, None, "mult")
+            for k in range(16 - S_ROWS, 16, 2):
+                pw = ps("pre")[0]
+                for h in range(2):
+                    lin(A(pw, h * C, (h + 1) * C), [(1.0, A(VT, 16 + k + h, 16 + 16 * C, 16)), (16.0, rl)])
+                act(A(cb, k * C, (k + 2) * C), A(pw, 0, 2 * C), "Identity", C2)
+            rows = sorted(range(16), key=lambda k: k if k < 16 - S_ROWS else (k - 16 + S_ROWS) // 2 * 4 + 5.5)
+            sums = [(blk("Sall", k), A(cb, k * C, (k + 1) * C)) for k in rows]
+            if LEAN: sums = [(8.0, sumE)] + sums[:12] + [(mat(7), rl), (FR, pre)] + sums[12:]
+            lin(ps("sum"), sums)
+            if "u" in SCAN:
+                lin(ps("hs"), [(1.0, A("own", 0, C)), (mat(HB), xn)])
+                scan(Fl(5), A("own", 2 * C, 3 * C), ps("hs"))
+                pu, w241 = pick(Fl(5)), 120.5
+            else:
+                pu, w241 = ps("u", D), 241.0
+                lin(pu, [(blk("Hall", a), A(sb, a, C, 16)) for a in range(16)])
+            if "ti" in ON_S: act(A("ti" + cs_, 0, D), pu, "Identity", 0.0, w241)
+            else: ts(A("ti" + cs_, 0, D), pu, w241, None, "mult")
             cint = A("cint", D * c, D * c + D)
             ts(cint, A("ti" + cs_, 0, D), 6, NP - 1, "arith_shift_right", "bitwise_and")
-            cp(A("tu" + cs_, 16, 16 + D), cint)
+            if "tu" in ON_S: act(A("tu" + cs_, 16, 16 + D), cint, "Identity")
+            else: cp(A("tu" + cs_, 16, 16 + D), cint)
             if c == NCH - 1:
                 pq = "ps%d" % bank["d"]
                 cp(A("cf", 0, DW), A("cint", 0, DW))
@@ -272,40 +359,59 @@ def describe():
                 lin(A(pq, 424, 424 + DW), [(1.0 / 2048, A("cf", 0, DW))] + [(blk("Sall", a), A("Eq", DW * a, DW * a + DW)) for a in range(16)])
                 ts(A("soff", 0, 2 * DW, 2), A(pq, 424, 424 + DW), 2048.0, cf(K512), "mult", "min")
             lin(ps("rr"), [(mat(HB), xn)])
-            act(rr, ps("rr"), "Identity", 128.5 + 1.0 / 2048, 1.0 / 2048)
+            aff("rr", rr, ps("rr"), 1.0 / 2048, 128.5 + 1.0 / 2048)
             MUL, ADD, K3 = ps("mul"), ps("add"), ps("k3")
-            if EARLY:
-                if AGAIN: lin(MUL, [(CM, ONE), (-2048.0, rr)], True)
-                else: lin(MUL, [(CM, ONE), (mat(HB), xn), (-2048.0, rr)])
+            if EARLY == 2:
+                lin(MUL, [(CM, ONE), (mat(HB), xn), (-2048.0, rr)])
+                tt(In(0), n32, MUL, "mult")
+                ts(In(1), In(0), 5, NM - 1, "arith_shift_right", "bitwise_and")
+                aff("d1", Fl(3), In(1), 1.0, cf(K37))
+                aff("add", MUL, n32, 1.0, float(NM))
+            elif EARLY:
+                lin(MUL, [(CM, ONE), (mat(HB), xn), (-2048.0, rr)])
                 tt(In(0), n32, MUL, "mult")
                 ts(In(1), In(0), 5, NM - 1, "arith_shift_right", "bitwise_and")
                 if "a1" in ON_S: act(MUL, n32, "Identity", cf(K37B))
                 else: ts(MUL, n32, cf(K37), float(NM), "add", "add")
                 tt(Fl(3), In(1), MUL, "add")
             act(Fl(0), IND(A("W", 0, NP + 16), A("tu" + cs_, 16, 16 + D)), "Identity")
-            act(yc, Fl(0), "Identity", YB, 1.0 / 65536)
+            aff("yc", yc, Fl(0), 1.0 / 65536, YB)
             lin(ps("ad"), [(-1.0, xn), (1.0, yc)])
             act(ad, ps("ad"), "Abs", -129.0)
             lin(ps("hs"), [(mat(BD), ad)])
-            act(hs, ps("hs"), "Sign", cf(THC), -1.0)
-            lin(K3, [(65536.0, yc), (16384.0, hs)])
-            tt(K3, Fl(0), K3, "subtract")
-            if EARLY: tt(Fl(4), Fl(3), K3, "min")
+            sign("hs", hs, ps("hs"), cf(THC), -1.0, cf(THC))
+            if "k3" in WIDE: lin(K3, [(IF, Fl(0)), (-65536.0, yc), (-16384.0 * FH, hs)])
+            else:
+                lin(K3, [(65536.0, yc), (16384.0 * FH, hs)])
+                tt(K3, Fl(0), K3, "subtract")
+            if EARLY == 1: tt(Fl(4), Fl(3), K3, "min")
             tt(eh, n32, K3, "is_equal")
-            act(hv, K3, "Sign", 8191.5, -1.0)
-            if AGAIN: lin(ps("hy"), [(16.0, hs)], True)
-            else: lin(ps("hy"), [(-1.0, xn), (1.0, yc), (16.0, hs)])
-            act(hy, ps("hy"), "Relu", -129.0)
-            if "mg" in ON_S:
-                act(Fl(2), ps("sum"), "Identity", MAGIC)
-                act(Fl(1), Fl(2), "Identity", -MAGIC)
-            else: ts(Fl(1), ps("sum"), MAGIC, MAGIC, "add", "subtract")
-            tt(Fl(2), ps("sum"), Fl(1), "subtract")
-            act(ap_, Fl(2), "Identity", 192.0, 16.0)
-            lin(ps("thr"), [(blk("Dg", t), ONE), (-189.0 / 16, pre), (63.0 / 1024, ap_)])
-            tt(aw, Fl(2), ps("thr"), "is_le")
-            if EARLY:
-                act(ADD, aw, "Identity", 8192.0, 32768.0)
+            sign("hv", hv, K3, 8191.5, -1.0, 8191.5)
+            lin(ps("hy"), [(-1.0, xn), (1.0, yc), (16.0 * FH, hs)])
+            aff("hy", hy, ps("hy"), 1.0, -129.0, True)
+            if LEAN:
+                aff("ap", ap_, ps("sum"), 16.0, 176.0)
+                aff("thr", Fl(1), ap_, 63.0 / 1024, cf(DN + t))
+                tt(aw, Fl(1), ps("sum"), "is_ge")
+            else:
+                if "mg" in ON_S:
+                    act(Fl(2), ps("sum"), "Identity", MAGIC)
+                    act(Fl(1), Fl(2), "Identity", -MAGIC)
+                else: ts(Fl(1), ps("sum"), MAGIC, MAGIC, "add", "subtract")
+                tt(Fl(2), ps("sum"), Fl(1), "subtract")
+                aff("ap", ap_, Fl(2), 16.0, 192.0)
+                lin(ps("thr"), [(blk("Dg", t), ONE), (-189.0 / 16 * FR, pre), (63.0 / 1024, ap_)])
+                tt(ps("thr") if EARLY == 2 else aw, Fl(2), ps("thr"), "is_le")
+            if EARLY == 2:
+                tt(Fl(4), Fl(3), ps("thr"), "mult")
+                aff("aw", aw, ps("thr"))
+                tt(Fl(3), Fl(4), MUL, "add")
+                tt(In(2), Fl(3), K3, "min")
+            elif "q" in WIDE:
+                lin(ps("q"), [(IF, n32), (8192.0, ONE), (65536.0, aw)])
+                tt(In(2), Fl(4), ps("q"), "min")
+            elif EARLY:
+                aff("add", ADD, aw, 32768.0, 8192.0)
                 tt(ADD, n32, ADD, "add")
                 tt(In(2), Fl(4), ADD, "min")
             else:
@@ -318,8 +424,8 @@ def describe():
                 tt(Fl(3), In(1), ADD, "add")
                 tt(In(2), Fl(3), K3, "min")
             ts(nn32, In(2), NM - 1, None, "bitwise_and")
-            lin(ps("s6"), [(1.0, eh), (-0.5, hv), (-1.0, aw)])
-            act(s6, ps("s6"), "Relu", 0.5)
+            lin(ps("s6"), [(1.0, eh), (-0.5 * FV, hv), (-1.0, aw)])
+            aff("s6", s6, ps("s6"), 1.0, 0.5, True)
             if t < ST - 1:
                 if "u16" in ON_S: act(nn16, nn32, "Identity")
                 else: cp(nn16, nn32)
@@ -334,17 +440,22 @@ def describe():
                 tt(A("oyt", c * C, (c + 1) * C), nn32, ps("yt"), "add")
                 dma("Y", A("yt", c * C, (c + 1) * C), A("oyt", c * C, (c + 1) * C))
                 dma("Y", A("yx", c * C, (c + 1) * C), xn)
-            lin(ps("ent"), [(CENT, ONE), (65536.0, xn), (-524288.0 + XH / 2, hs), (65536.0, hy), (-XH, eh), (XA, aw)])
-            tt(A("ent", c * C, (c + 1) * C), n32, ps("ent"), "add")
+            lin(ps("ent"), [(IF, n32)] * ("ent" in WIDE) + [(CENT, ONE), (65536.0, xn), ((-524288.0 + XH / 2) * FH, hs), (65536.0, hy), (-XH, eh), (XA, aw)])
+            if "ent" in WIDE: act(A("ent", c * C, (c + 1) * C), ps("ent"), "Identity")
+            else: tt(A("ent", c * C, (c + 1) * C), n32, ps("ent"), "add")
             SPANS.append((first, len(ops), c))
         for b in range(DW):
             cp(IND(A("W", 0, NP + 16), A("soff", 2 * b, 2 * b + 1)), A("ent", 16 * b, 16 * b + 16))
     for j, lo in enumerate(range(0, NP, 256)):
         hi = lo + 256
         act(A("oy1", lo, hi), A("W", lo, hi), "Identity", YB, 1.0 / 65536)
-        lin(A("ps%d" % j, 0, hi - lo), [(65536.0, A("oy1", lo, hi))])
-        tt(A("oyj", lo, hi), A("W", lo, hi), A("ps%d" % j, 0, hi - lo), "subtract")
-        ts(A("oyk", lo, hi), A("oyj", lo, hi), -16384.0, float(NM), "add", "min")
+        if "out" in WIDE:
+            lin(A("ps%d" % j, 0, hi - lo), [(IF, A("W", lo, hi)), (-65536.0, A("oy1", lo, hi))])
+            ts(A("oyk", lo, hi), A("ps%d" % j, 0, hi - lo), -16384.0, float(NM), "add", "min")
+        else:
+            lin(A("ps%d" % j, 0, hi - lo), [(65536.0, A("oy1", lo, hi))])
+            tt(A("oyj", lo, hi), A("W", lo, hi), A("ps%d" % j, 0, hi - lo), "subtract")
+            ts(A("oyk", lo, hi), A("oyj", lo, hi), -16384.0, float(NM), "add", "min")
         dma("Y", A("yk", lo, hi), A("oyk", lo, hi))
     act(A("oy2", 0, NP), A("oy1", 0, NP), "Identity", -129.0)
     dma("Y", A("yy", 0, NP), A("oy2", 0, NP))
@@ -365,27 +476,28 @@ def regions(op):
     return [r for r in rd if r[0] not in DRAM], [r for r in wr if r[0] not in DRAM]
 
 
-SC = {"gather": 1.56, "scatter": 3.8, "call": 40, "pe": 0.45, "lat": 80, "bw": 250.0, "link": 2500, "lbw": 60.0, "cyc": 0.9}
+SC = {"gather": 1.55, "scatter": 2.9, "call": 10, "act": 80, "psum": 25, "pe": 0.43, "mm": 10, "lat": 0, "V": 70, "S": 35, "P": 40, "same": 70, "cross": 45, "pool": 270, "bw": 290.0, "dma": 1350, "gdma": 300, "issue": 450, "first": 1800, "link": 1300, "lbw": 27.0, "row": 25, "cyc": 0.85}
 
 
 def cost(op, sc=SC):
     q, kind, o, ins, par = op
     if kind == "mm":
-        d = 20 + sc["pe"] * max(64, count(o)); return d, d + sc["lat"]
+        d = sc["mm"] + sc["pe"] * max(64, count(o)) * (1 if narrow(ins[0]) else 4); return d, d + sc["lat"] + sc.get(q, 0)
     if kind == "dma":
-        d = max(100, count(o) * 128 * (2 if narrow(o) or narrow(ins[0]) else 4) / sc["bw"]); return d, d + 2000
-    if kind == "send": return 500, 500
+        d = max(sc["gdma"] if q == "G" else 100, count(o) * 128 * (2 if narrow(o) or narrow(ins[0]) else 4) / sc["bw"]); return d, d + sc["dma"]
+    if kind == "send":
+        d = sc["issue"] + (0 if par[1] else sc.get("first", 0)); return d, d
     if kind == "recv":
-        d = count(o) * 128 * (2 if narrow(o) else 4) / sc["lbw"]; return d, d + sc["link"]
+        d = 0 if par[1] else 16 * par[2] * (sc["row"] + count(o) * (2 if narrow(o) else 4) / sc["lbw"]); return d, d + sc["link"]
     n, y = count(o), sc["cyc"]
-    if kind in ("iota", "sel"): d = 170 + 2 * n * y
+    if kind in ("iota", "sel"): d = sc.get("pool", 170) + 2 * n * y
     elif o[0] == "@": d = 60 + sc["scatter"] * n * y
     elif ins and ins[0][0] == "@": d = 70 + sc["gather"] * n * y
-    elif kind == "act": d = 20 + sc["call"] + max(64, n) * y
+    elif kind == "act": d = sc["act"] + max(64, n) * y + (sc.get("psum", 0) if "ps" in (o[0][:2], ins[0][0][:2]) else 0)
     elif kind == "tt":
         d = sc["call"] + max(64, n * (1 if "ps" in (ins[0][0][:2], ins[1][0][:2]) else 2)) * y
     else: d = sc["call"] + max(64, n * (0.5 if narrow(o) and (not ins or narrow(ins[0])) else 1)) * y
-    return d, d + sc["lat"]
+    return d, d + sc["lat"] + sc.get(q, 0)
 
 
 def links():
@@ -410,9 +522,14 @@ def links():
         for r in rd:
             hist.setdefault(r[0], []).append((i, r[1], r[2], False))
         if op[1] == "send":
-            if op[3][0][0][:2] == "sn": soft[i].add(max(sends.values()))
+            if op[3][-1][0][:2] == "sn" or op[3][0][1] >= C: soft[i].add(max(sends.values()))
             sends[op[4][1]] = i
-        if op[1] == "recv": soft[i].add(sends[op[4][0]])
+        if op[1] == "recv": soft[i].add(i - 1)
+    if FIRM:
+        loads = [i for i, op in enumerate(ops[:SPANS[0][0]]) if op[:2] == ("Y", "dma")]
+        for i, j in zip(loads, loads[1:]): soft[j].add(i)
+        store = [i for i, op in enumerate(ops) if op[2] and op[2][0] == "kz"][0]
+        soft[store].add(max(i for i in range(*SPANS[0][:2]) if ops[i][2] and ops[i][2][0] == "VF0"))
     return ops, hard, soft
 
 
@@ -437,13 +554,14 @@ def plan(sc=SC):
     ops, hard, soft = links()
     n = len(ops)
     q, dur, tail = [op[0] for op in ops], [cost(op, sc)[0] for op in ops], [cost(op, sc)[1] - cost(op, sc)[0] for op in ops]
-    pre = [[(j, tail[j] + 40 if j in hard[i] else 0.0) for j in sorted(hard[i] | soft[i])] for i in range(n)]
+    pre = [[(j, tail[j] + sc["same" if q[j] == q[i] else "cross"] if j in hard[i] else 0.0) for j in sorted(hard[i] | soft[i])] for i in range(n)]
     suc = [[] for _ in range(n)]
     for i in range(n):
         for j, gap in pre[i]: suc[j].append((i, gap))
     way = [0.0] * n
-    for i in range(n - 1, -1, -1):
-        way[i] = dur[i] + max([way[u] + gap for u, gap in suc[i]] + [tail[i]])
+    for _ in range(2):
+        for i in range(n - 1, -1, -1):
+            way[i] = dur[i] + max([way[u] + gap for u, gap in suc[i]] + [tail[i]])
     best = None
     for lead in LEADS:
         for late in LATES:
@@ -515,7 +633,7 @@ def rank_program(g, core, T, topo):
                 g.remote_dma_fused([RemoteDMATransfer(dst_ids=[DstId(rid=rid, pnc=pid)], remote_sem=T.sem["a%d" % (par[1] + j)],
                                                       dma_engine_mask=sum(1 << k for k in eng[j * m:(j + 1) * m]),
                                                       src=ap(ins[j]), dst=ap(par[0][j])) for j in range(len(ins))], local_sem=T.sem.sent)
-            total["sent"] = total.get("sent", 0) + nout
+            total["sent"] = total.get("sent", 0) + nout // len(ins) * len(ins)
             continue
         if kind == "dma":
             name = "d%d" % ndma[0]; ndma[0] += 1
@@ -527,11 +645,12 @@ def rank_program(g, core, T, topo):
         if kind == "tt": ins_ = e.tensor_tensor(ap(o), ap(ins[0]), ap(ins[1]), alu[par])
         elif kind == "ts" and par[1] is None: ins_ = e.tensor_scalar(ap(o), ap(ins[0]), ap(ins[1]), None, alu[par[0]])
         elif kind == "ts": ins_ = e.tensor_scalar(ap(o), ap(ins[0]), ap(ins[1]), ap(ins[2]), alu[par[0]], alu[par[1]])
+        elif kind == "scan": ins_ = e.tensor_tensor_scan(ap(o), ap(ins[0]), ap(ins[1]), 0.0, AluOpType.add, AluOpType.min)
         elif kind == "cp": ins_ = e.tensor_copy(ap(o), ap(ins[0]))
         elif kind == "ms": ins_ = e.memset(ap(o), par)
         elif kind == "act": ins_ = e.activation(ap(o), ap(ins[0]), fun[par], bias=ap(ins[1]), scale=ap(ins[2]))
         elif kind == "mm": ins_ = e.matmul(ap(o), ap(ins[0]), ap(ins[1]), par[0], par[1])
-        elif kind == "sel": ins_ = g.affine_select(ap(o), ap(ins[0]), par[0], AluOpType.not_equal, par[3], par[1], par[2])
+        elif kind == "sel": ins_ = g.affine_select(ap(o), ap(ins[0]), par[0], alu[par[4]], par[3], par[1], par[2])
         elif SCRATCH[o[0]][2] == "int32": ins_ = g.iota(ap(o), par[0], par[1], par[2])
         else: ins_ = g.iota(ap(o), par[0], par[1], par[2], allow_small_or_imprecise_dtypes=True)
         if i in needed:

@@ -4,71 +4,57 @@ from concourse.mybir import AluOpType, ActivationFunctionType
 NM, NP, NW, ST, SH, NR = 8192, 512, 384, 3, 3, 8
 C = 192
 NCH, D = NW // C, C // 16
-R1 = 512 // C
+R1 = 2
 DW = NW // 16
-PIECE = C // 4
+HA = 128
+WINS = [(_w, min(C, _w + HA)) for _w in range(0, C, HA)]
+CUTS = (64, 128, 192)
+SUBS = (128, 192)
+DIRECT = 1
+S_T = (2, 4, 6, 7)
 SPANS = []
-LOADS = (512, 1536, 2560, 3584, 4608, 5632, 6656, 7680, 8192)
-V_EVAC = (3,)
-V_DERIVE = (0, 1, 2, 3)
-CUT = 1
-V_GATHER = ()
-G_DERIVE = ()
-V_IW = 14
-TRIM = True
-LEAN = 0
-FIRM = False
+LOADS = (512, 1024, 2048, 3072, 4096, 5120, 6144, 7168, 7680, 8192)
+V_EVAC = (1, 3, 5, 7, 9, 11, 13, 15)
+V_GATHER = ((0, 0, 1),)
+DIAG = "SG"
+ENG = {"q": "VS", "cand": "V", "c4": "VS", "na": "VS", "ix": "V", "eb": "S", "e1": "V", "zx": "S", "sg": "S", "tu": "G", "cf": "G", "rr": "S", "a1": "S", "wg": "S", "yc": "S", "hs": "S", "k3": "P", "hv": "S", "hy": "S", "mg": "S", "u16": "G", "ent": "S", "set": "S", "col": "S", "wide": "V", "fill": "G", "grp": "S", "u": "V", "ti": "S", "Q": "V", "yb": "S", "r2": "S"}
+CANCEL = 0
 YB_AT = 6
 S_ROWS = 0
-WIDE = ("out",)
-MAGIC = 1.5 * 2.0 ** 26
-XA, XH = 25600.0, 28672.0
-ON_S = ("a1", "u16", "tu", "cand", "rl", "Pk", "pre", "sg", "rr", "yc", "hs", "hv", "hy", "s6", "d1", "aw", "add", "n32", "ti", "set")
-FC, FP, FR, FG, FH, FV = [1.0 if _n in ON_S else 2.0 for _n in ("cand", "Pk", "pre", "sg", "hs", "hv")]
-WTS = []
-for _w in [1.0, -1.0, 4.0 * FH, 256.0, 6.0, 8.0, 136.0 * FG, -512.0, 65536.0, 16384.0 * FH, 16.0 * FH, 63.0 / 1024, -189.0 / 16 * FR, -2048.0, 4096.0,
-           -0.5 * FV, (-524288.0 + XH / 2) * FH, XA, -XH, 8192.0, 1.0 / 2048, FC] + [-65536.0, -16384.0 * FH] * (len(WIDE) > 0) + [16.0] + [-8.0, FR] * (LEAN > 0):
-    if _w not in WTS and not (TRIM and _w == 4096.0) and not (LEAN and _w in (63.0 / 1024, -189.0 / 16 * FR)): WTS.append(_w)
-LEADS = (0, 2000, 4000)
-LATES = (0, 3000, 6000)
-AGAIN = False
-SCAN = ("idx", "u")
-WHOLE = False
-SUB = 2
-EARLY = 2
+FIRM = 1
+LAST = 1
+APART = 0
+DBANK = "d"
+B0 = 24592.0
+U = 32768.0
+XA, XH, KO = 25600.0, 28672.0, 6144.0
+NMAT = 56
+LEADS = (0, 3000)
+LATES = (0, 4000)
+ROUNDS = 600
 SENDS = ([("b", 0, C)], [("u", 0, C)], [("b", C, 3 * C)])
-if NCH == 2:
-    SLOTS = {"y1": ("y", 0), "cnt": ("a", 0), "rl": ("z", 0), "Pk": ("z", C), "idx": ("z", 384), "pre": ("w", 0), "dl": ("z", 0),
-             "y2": ("y", 0), "sum": ("a", 0), "u": ("z", 400), "rr": ("w", C), "ad": ("z", 0), "hs": ("z", C), "k3": ("w", 0),
-             "hy": ("z", 0), "thr": ("y", 0), "mul": ("w", C) if EARLY else ("z", C), "add": ("a", C), "s6": ("y", C), "yt": ("y", 0), "ent": ("z", C)}
-    if S_ROWS: SLOTS.update({"rr": ("z", C), "mul": ("z", C), "hs": ("z", 0), "k3": ("z", 0), "hy": ("z", C), "ent": ("w", 0), "q": ("w", C)})
-    else: SLOTS["q"] = SLOTS["mul"]
-else:
-    SLOTS = {"y1": ("y", 0), "cnt": ("a", 0), "rl": ("y", 0), "Pk": ("a", C), "idx": ("y", C), "pre": ("a", 2 * C), "dl": ("a", 3 * C),
-             "y2": ("y", 0), "sum": ("a", 0), "u": ("z", 3 * C), "rr": ("z", 0), "ad": ("z", C), "hs": ("z", 2 * C), "k3": ("z", 0),
-             "hy": ("z", C), "thr": ("y", 0), "mul": ("z", 2 * C), "add": ("a", C), "s6": ("y", C), "yt": ("y", 2 * C), "ent": ("y", 3 * C)}
+SLOTS = {"y1": ("y", 0), "cnt": ("a", 0), "c4": ("z", 0), "na": ("z", C), "idx": ("z", 0), "dl": ("z", C), "sg": ("w", 0), "y2": ("y", 0), "sum": ("a", 0), "u": ("z", 0), "rr": ("w", C), "mul": ("w", 0), "a1": ("w", C), "ad": ("z", C), "hs": ("z", 0), "k3": ("w", 0), "hy": ("z", C), "wake": ("y", 0), "yt": ("y", C), "ent": ("z", 0)}
+if NCH > 2:
+    SLOTS.update({"c4": ("a", C), "na": ("a", 2 * C), "idx": ("a", 3 * C), "dl": ("a", C), "sg": ("a", 2 * C), "ent": ("a", C)})
 
 SCRATCH = {}
 for _n, _w, _d in [
-        ("F", NM, "bfloat16"), ("Zt", NM, "bfloat16"),
-        ("ioa", 144, "bfloat16"), ("zero", 128, "bfloat16"), ("If", 128, "float32"), ("Sall", 144, "bfloat16"), ("Hall", 144, "bfloat16"),
-        ("Pall", 144, "bfloat16"), ("Rall", 2048, "bfloat16"), ("ioc", 256, "bfloat16"), ("mats", 128 * 8, "bfloat16"),
-        ("Iw", 128 * len(WTS), "bfloat16"), ("cm", 128 * 5, "bfloat16"), ("Dg", 128 * ST, "bfloat16"), ("ones", C, "bfloat16"),
-        ("turn", 2 * C, "bfloat16"), ("own", 3 * C, "bfloat16"), ("base", 16, "bfloat16"), ("mask", NW, "float32"), ("coli", 32, "int32"), ("colj", 8, "int32"),
-        ("colf", 32, "float32"), ("t0s", NW, "int32"), ("y0s", NP, "bfloat16"), ("k0s", NP, "int32"), ("kz", NP, "bfloat16"),
-        ("W", NP + 16, "float32"), ("ent", NW, "float32"), ("cf", 24, "float16"), ("cint", 24, "int32"), ("Eq", NW, "bfloat16"),
-        ("dd", 48, "float32"), ("soff", 48, "uint16"), ("oyt", NW, "float32"), ("oy1", NP, "bfloat16"), ("oy2", NP, "bfloat16"),
-        ("oyj", NP, "float32"), ("oyk", NP, "float32")]:
+        ("F", NM, "bfloat16"), ("Tt", NM, "bfloat16"), ("Mt", NM, "float16"), ("Z", NM, "float32"),
+        ("ioa", 144, "bfloat16"), ("zero", 128, "bfloat16"), ("If", 128, "float32"), ("S1", 144, "bfloat16"), ("SH", 144, "bfloat16"),
+        ("Rall", 2048, "bfloat16"), ("ioc", 256, "bfloat16"), ("mats", 128 * NMAT, "bfloat16"), ("BP", 256, "float16"),
+        ("ones", C, "bfloat16"), ("turn", C, "bfloat16"), ("own", 3 * C, "bfloat16"), ("mask", NW, "float32"), ("coli", 32, "int32"),
+        ("colj", 8, "int32"), ("colf", 48, "float32"), ("colb", 8, "bfloat16"), ("t0s", NW, "int32"), ("y0s", NP, "bfloat16"),
+        ("k0s", NP, "int32"), ("kz", NP, "bfloat16"), ("W", NP + 16, "float32"), ("W2", NP + 16, "float32"), ("ent", NW, "float32"), ("n32", 2 * NW, "float32"),
+        ("cf", 24, "float16"), ("cint", 24, "int32"), ("Eq", NW, "bfloat16"),
+        ("soff", 48, "uint16"), ("oyt", NW, "float32"), ("oy1", NP, "bfloat16"), ("oy2", NP + 16, "bfloat16"), ("oyk", NP + 16, "float32")]:
     SCRATCH[_n] = ("sbuf", [128, _w], _d)
 for _c in range(NCH):
-    for _n, _w, _d in [("VG", 16 * C, "float32"), ("VF", 16 * C, "bfloat16"), ("VT", 16 * C + 16, "bfloat16"), ("ca", 16 * C, "bfloat16"), ("cb", 16 * C, "float16"),
-                       ("b", 20 * C, "bfloat16"), ("f", 6 * C, "float32"), ("i", 3 * C, "int32"),
-                       ("ti", 16, "int32"), ("tu", 32, "uint16")]:
+    for _n, _w, _d in [("VF", 16 * C + 32, "float32"), ("ca", 16 * C, "float16"), ("cb", 16 * C, "float16"), ("b", 16 * C, "bfloat16"),
+                       ("h", 2 * C, "float16"), ("f", 4 * C, "float32"), ("i", 6 * C, "int32"), ("tu", 32, "uint16")]:
         SCRATCH[_n + str(_c)] = ("sbuf", [128, _w], _d)
     for _t in range(ST):
         for _p in "rs":
             SCRATCH["%sb%d%d" % (_p, _t, _c)] = ("sbuf", [128, 3 * C], "bfloat16")
-            SCRATCH["%sn%d%d" % (_p, _t, _c)] = ("sbuf", [128, C], "float32" if WIDE and _p == "r" else "int32")
             SCRATCH["%su%d%d" % (_p, _t, _c)] = ("sbuf", [128, C], "uint16")
 for _k in range(8):
     SCRATCH["ps%d" % _k] = ("psum", [128, 512], "float32")
@@ -96,37 +82,103 @@ def narrow(ap):
 
 
 def describe():
-    ops = []
+    head, body = [], []
+    ops, now, made = [head], [0, 0], {}
 
-    def tt(o, a, b, op): ops.append(("V", "tt", o, [a, b], op))
-    def ts(o, a, s1, s2, op0, op1=None): ops.append(("V", "ts", o, [a, s1, s2], (op0, op1)))
-    def scan(o, a, b): ops.append(("V", "scan", o, [a, b], None))
-    def cp(o, a): ops.append(("V", "cp", o, [a], None))
-    def ms(o, v): ops.append(("V", "ms", o, [], v))
-    def act(o, a, f, bias=0.0, scale=1.0): ops.append(("S", "act", o, [a, bias, scale], f))
-    def io(o, pat, base, cm): ops.append(("G", "iota", o, [], (pat, base, cm)))
-    def sel(o, a, pat, fill, base, cm, op="not_equal"): ops.append(("G", "sel", o, [a], (pat, base, cm, fill, op)))
-    def dma(q, o, a): ops.append((q, "dma", o, [a], None))
-    def Iw(w): return A("Iw", 128 * WTS.index(w), 128 * WTS.index(w) + 128)
-    def mat(j): return A("mats", 128 * j, 128 * j + 128)
+    def put(*op): ops[0].append(op)
+    def tt(o, a, b, op): put("V", "tt", o, [a, b], op)
+    def ts(o, a, s1, s2, op0, op1=None): put("V", "ts", o, [a, s1, s2], (op0, op1))
+    def scan(o, a, b): put("V", "scan", o, [a, b], None)
+    def cp(o, a): put("V", "cp", o, [a], None)
+    def ms(o, v, p=None): put("V", "ms", o, [], (v, p))
+    def act(o, a, f, bias=0.0, scale=1.0): put("S", "act", o, [a, bias, scale], f)
+    def io(o, pat, base, cm): put("G", "iota", o, [], (pat, base, cm))
+    def sel(o, a, pat, fill, base, cm, op="not_equal"): put("G", "sel", o, [a], (pat, base, cm, fill, op))
+    def dma(q, o, a): put(q, "dma", o, [a], None)
     def blk(n, a):
-        return A(n, 15 - a, 143 - a) if n in ("Sall", "Pall", "Hall") else A(n, 128 * a, 128 * a + 128)
-    def cf(j): return A("colf", j, j + 1)
+        return A(n, 15 - a, 143 - a) if n in ("S1", "SH") else A(n, 128 * a, 128 * a + 128)
+    def eng(name, t=None, c=None):
+        e, (t, c) = ENG[name], now if t is None else (t, c)
+        return e[0 if len(e) == 1 else c if len(e) == NCH else t * NCH + c]
+    def amp(name, t=None, c=None): return 1.0 if eng(name, t, c) == "S" else 2.0
 
     def aff(name, o, a, scale=1.0, bias=0.0, relu=False):
-        if name in ON_S: act(o, a, "Relu" if relu else "Identity", bias, scale)
+        e = eng(name)
+        if e == "G": sel(o, a, [[0, count(o)]], 0.0, 1, 0)
+        elif e == "S": act(o, a, "Relu" if relu else "Identity", bias, scale)
         elif relu: ts(o, a, bias, 0.0, "add", "max")
         elif scale == 1.0 and bias == 0.0: cp(o, a)
         elif scale == 1.0: ts(o, a, bias, None, "add")
+        elif bias == 0.0: ts(o, a, scale, None, "mult")
         else: ts(o, a, scale, bias, "mult", "add")
 
-    def sign(name, o, a, bias, scale, thr):
-        if name in ON_S: act(o, a, "Sign", bias, scale)
-        else: ts(o, a, thr, 0.5, "is_gt" if scale > 0 else "is_lt", "subtract")
+    def sign(name, o, a, thr, above):
+        if eng(name) == "S":
+            s = -1.0 if above else 1.0
+            act(o, a, "Sign", s * thr if isinstance(thr, float) else thr if thr[0] == "colf" else col(s * thr[0], s * thr[1]), -s)
+        else: ts(o, a, thr if isinstance(thr, float) or thr[0] == "colf" else col(*thr), 0.5, "is_gt" if above else "is_lt", "subtract")
 
-    def lin(o, terms, more=False, close=True):
+    IOC, GRP, ZERO, ONE = A("ioc", 0, 128), A("ioc", 128, 256), A("zero", 0, 128), A("ones", 0, C)
+    GP, KC, H2, H241, HLO, THC, K7, DN = [A("colf", j, j + 1) for j in range(8)]
+
+    def once(key, make):
+        if key not in made:
+            back, ops[0] = ops[0], head
+            made[key] = make(); ops[0] = back
+        return made[key]
+
+    def room(name, width, first=0):
+        made[name] = made.get(name, first) + width
+        return A(name, made[name] - width, made[name])
+
+    def col(a, b):
+        def make():
+            o = room("colf", 1, 12); aff("col", o, KC, a, b); return o
+        return once(("col", a, b), make)
+
+    def Iw(w):
+        def make():
+            o = room("mats", 128); e = DIAG[o[1] // 128 % len(DIAG)] if w != 1.0 else "V"
+            if e == "V": ts(o, IOC, 0.0, w, "is_equal", "mult")
+            elif e == "S": act(o, Iw(1.0), "Identity", 0.0, w)
+            else: sel(o, ZERO, [[1, 128]], w, 0, -1)
+            return o
+        return once(("I", w), make)
+
+    def grp(w, name="mats"):
+        def make():
+            o = room(name, 128)
+            if eng("grp") == "V" or w == 1.0: ts(o, GRP, GP, w, "is_equal", "mult")
+            else: act(o, grp(1.0), "Identity", 0.0, w)
+            return o
+        return once(("grp", w), make)
+
+    def tri(off, diag, s):
+        def make():
+            o = room("mats", 128)
+            sel(o, grp(off), [[s, 128]], 0.0, 0, -s, "is_gt"); sel(o, o, [[1, 128]], diag, 0, -1); return o
+        return once(("tri", off, diag, s), make)
+
+    def wide(parts, lanes=False):
+        def make():
+            o = room("mats", 128)
+            if lanes:
+                ts(K7, KC, 7.0, 16.0, "is_ge", "mult"); ts(o, IOC, 0.0, K7, "is_equal", "mult")
+            elif eng("wide") == "V": ms(o, 0.0)
+            for j, v in enumerate(parts):
+                if eng("wide") == "V": ms(o, v, 32 * j)
+                else: sel(o, o if j or lanes else ZERO, [[0, 128]], v, -j, 1)
+            return o
+        return once(("wide", parts), make)
+
+    def dg(t):
+        def make():
+            o = room("mats", 128); aff("set", o, Iw(1.0), A("colf", DN[1] + t, DN[1] + t + 1)); return o
+        return once(("dg", t), make)
+
+    def lin(o, terms):
         for j, (l, r) in enumerate(terms):
-            ops.append(("P", "mm", o, [Iw(l) if isinstance(l, float) else l, r], (j == 0 and not more, close and j == len(terms) - 1)))
+            put("P", "mm", o, [Iw(l) if isinstance(l, float) else l, r], (j == 0, j == len(terms) - 1))
 
     dma("Y", A("t0s", 0, NW), A("t0", 0, NW))
     for lo, hi in zip((0,) + LOADS, LOADS):
@@ -135,331 +187,264 @@ def describe():
         dma("Y", A("rb0%d" % c, 0, C), A("x0", c * C, (c + 1) * C))
     dma("Y", A("y0s", 0, NP), A("y0", 0, NP))
     dma("Y", A("k0s", 0, NP), A("k0", 0, NP))
-    IOC = A("ioc", 0, 128)
     io(IOC, [[1, 128]], 0, -1)
     io(A("colj", 0, 1), [[1, 1]], 0, 1)
     io(A("ioa", 0, 144), [[1, 144]], -15, 0)
-    io(A("ioc", 128, 256), [[16, 8], [0, 16]], 0, 0)
+    io(GRP, [[16, 8], [0, 16]], 0, 0)
     TURN = A("turn", 0, C)
-    if "rl" in ON_S: io(TURN, [[0, C // 4], [1, 4]], 0, 0)
-    else: io(A("turn", C, 2 * C), [[0, C // 4], [-1, 4]], 7, 0)
-    if not (TRIM and "idx" in SCAN): io(A("base", 0, D), [[256, D]], 0, 0)
+    io(TURN, [[0, C // 4], [1, 4]], 0, 0)
     dma("G", A("coli", 0, 1), A("hw", 0, 1))
     dma("G", A("coli", 8, 9), A("th", 0, 1))
     dma("G", A("coli", 16, 19), A("dw", 0, 3))
     io(A("mask", 0, NW), [[1, 16], [0, DW]], 0, 0)
-    ZERO = A("zero", 0, 128)
-    ms(ZERO, 0.0)
-    for w in WTS:
-        if WTS.index(w) < V_IW: ts(Iw(w), IOC, 0.0, w, "is_equal", "mult")
-        else: sel(Iw(w), ZERO, [[1, 128]], w, 0, -1)
-    CY1, CY2, CENT, CM, CW = [blk("cm", j) for j in range(5)]
-    for o, parts in ((CY1, (-2560.0, 8.5)), (CY2, (3712.0, 7.875, 1.0 / 512)), (CENT, (121.0 * 65536, 16384.0 + XH / 2)),
-                     (CM, (129.0 * 2048, 1.0)), (CW, (129.0 * 65536, 16384.0))):
-        for j, v in enumerate(parts):
-            sel(o, o if j else ZERO, [[0, 128]], v, -j, 1)
-    for a in range(16):
-        sel(blk("Rall", a), Iw(-1.0), [[16, 8], [0, 16]], 1.0, a, -1)
+    def fill(o, v):
+        if eng("fill") == "G" and v == int(v): io(o, [[0, count(o)]], int(v), 0)
+        else: ms(o, v)
+    if "G" in DIAG + ENG["wide"]: fill(ZERO, 0.0)
+    fill(ONE, 1.0)
     ts(A("colj", 1, 2), A("colj", 0, 1), 112, None, "bitwise_and")
     ts(A("colj", 2, 3), A("colj", 0, 1), 15, None, "bitwise_and")
-    GP, KC, KH, K37, K512, KB, H1, H2, THC, PW, DN, K37B, KM = 0, 1, 2, 3, 4, 5, 6, 7, 8, 9, 10, 13, 14
     cp(A("colf", 0, 2), A("colj", 1, 3))
-    for j, scale, bias in ((K37B, 37.0, float(NM)), (KH, -0.5 if FP == 1 else 0.5, (0.5 if "rl" in ON_S else 7.5) * (1 if FP == 1 else -1)), (K37, 37.0, 0.0), (K512, 1.0, float(NP)),
-                           (KB, 16.0, 23.5 - 2048), (KM, -4096.0, 2048.0)):
-        if not (TRIM and (j == KB and "idx" in SCAN or j == K37B and EARLY != 1 or j == K37 and EARLY == 1)): aff("set", cf(j), cf(KC), scale, bias)
-    act(cf(PW), cf(KC), "Relu", 4095.0 * FP, -4096.0 * FP)
-    aff("set", cf(PW), cf(PW), 1.0, FP)
-    aff("set", cf(H2), A("coli", 0, 1), 2.0)
-    aff("set", cf(THC), A("coli", 8, 9), 1.0, 0.5)
-    aff("set", A("colf", DN, DN + 3), A("coli", 16, 19), -1.0 / 1024, 0.5 / 1024 + (1 - 189.0 / 16) * (LEAN > 0))
-    ts(A("Sall", 0, 144), A("ioa", 0, 144), cf(GP), 0.5, "is_equal", "mult")
-    for o, j in (("Pall", PW), ("Hall", H2)):
-        if not (TRIM and ("idx" if j == PW else "u") in SCAN): aff("set", A(o, 0, 144), A("Sall", 0, 144), cf(j))
-    BD, HB, BH, LO, SHF = 0, 1, 2, 3, 4
-    ts(mat(BD), A("ioc", 128, 256), cf(GP), None, "is_equal")
-    aff("set", mat(HB), mat(BD), cf(H2))
-    aff("set", mat(BH), mat(BD), -0.5 * FC)
-    BP = 5
-    if SCAN:
-        aff("set", cf(PW + 7), cf(PW), 0.5)
-        aff("set", mat(BP), mat(BD), cf(PW + 7))
-        io(A("own", 0, C), [[0, D], [1, 16]], 0, 0)
-        io(A("own", C, 2 * C), [[16, C]], 0, 0)
-        ts(A("own", 0, C), A("own", 0, C), cf(KC), 131072.0, "not_equal", "mult")
-        tt(A("own", C, 2 * C), A("own", C, 2 * C), A("own", 0, C), "max")
-        aff("set", A("own", 2 * C, 3 * C), A("own", 0, C), -2.0, 262144.0)
-    sel(mat(LO), mat(BH), [[1, 128]], 0.0, 0, -1, "is_gt")
-    if FP > 1: aff("set", mat(6), mat(BD), FP)
-    sel(mat(SHF), mat(BD if FP == 1 else 6), [[1, 128]], 0.0, 1, -1, "is_equal")
-    if LEAN: aff("set", mat(7), mat(BD), -8.0)
-    for t in range(0 if LEAN else ST):
-        aff("set", blk("Dg", t), Iw(1.0), cf(DN + t))
+    for a in range(16):
+        sel(blk("Rall", a), Iw(-1.0), [[16, 8], [0, 16]], 1.0, a, -1)
+    aff("col", H2, A("coli", 0, 1), 2.0)
+    HHI = A("colf", 10, 11)
+    if "V" in ENG["u"]:
+        aff("col", H241, A("coli", 0, 1), 241.0)
+        aff("col", A("colb", 0, 1), H241)
+        aff("col", HHI, A("colb", 0, 1))
+        tt(HLO, H241, HHI, "subtract")
+    if "P" in ENG["u"]:
+        aff("col", A("colf", 11, 12), A("coli", 0, 1))
+        ts(A("SH", 0, 144), A("ioa", 0, 144), GP, A("colf", 11, 12), "is_equal", "mult")
+    aff("col", THC, A("coli", 8, 9), 1.0, 0.5)
+    aff("col", A("colf", DN[1], DN[1] + 3), A("coli", 16, 19), -U, 17 * U)
+    ts(A("S1", 0, 144), A("ioa", 0, 144), GP, 1.0 / 512, "is_equal", "mult")
+    OWNU, OWNI, OWND = A("own", 0, C), A("own", C, 2 * C), A("own", 2 * C, 3 * C)
+    io(OWNU, [[0, D], [1, 16]], 0, 0)
+    for lo, hi in WINS:
+        io(A("own", C + lo, C + hi), [[32, hi - lo]], 32, 0)
+    ts(OWNU, OWNU, KC, 2.0 ** 24, "not_equal", "mult")
+    tt(OWNI, OWNI, OWNU, "max")
+    ts(OWND, OWNU, -2.0, 2.0 ** 25, "mult", "add")
     IF = A("If", 0, 128)
-    if WIDE: act(IF, Iw(1.0), "Identity")
-    ONE = A("ones", 0, C)
-    io(ONE, [[0, C]], 1, 0)
-    act(A("mask", 0, NW), A("mask", 0, NW), "Relu", cf(KM), 4096.0)
+    aff("set", IF, Iw(1.0))
+    act(A("mask", 0, NW), A("mask", 0, NW), "Relu", col(-4096.0, 2048.0), 4096.0)
     ms(A("soff", 0, 48), 0)
     for c in range(NCH):
-        io(A("VT%d" % c, 0, 16), [[0, 16]], -2304, 0)
-        n0 = A("i%d" % c if WIDE else "rn0%d" % c, 0, C)
+        for lo, hi in WINS:
+            fill(A("VF%d" % c, 16 * lo + lo // 8, 16 * lo + lo // 8 + 16), B0 + 8 + 7680)
+        n0 = A("i%d" % c, 0, C)
         ts(n0, A("t0s", c * C, (c + 1) * C), NM - 1, None, "bitwise_and")
         aff("set", A("ru0%d" % c, 0, C), n0)
-        if WIDE: act(A("rn0%d" % c, 0, C), n0, "Identity")
         ts(A("rb0%d" % c, 2 * C, 3 * C), A("t0s", c * C, (c + 1) * C), float(NM), None, "is_ge")
-        if FH == 1: io(A("rb0%d" % c, C, 2 * C), [[0, C]], -1, 0)
-        else: ms(A("rb0%d" % c, C, 2 * C), -0.5)
+        fill(A("rb0%d" % c, C, 2 * C), -1.0 / amp("hs", 0, c))
+    fill(A("W", NP, NP + 16), 0.0)
+    ops[0] = body
     for j in range(NM // 512):
         lo, hi = 512 * j, 512 * j + 512
         if lo in (0,) + LOADS:
             end = min(b for b in LOADS if b > lo)
-            ts(A("Zt", lo, end), A("F", lo, end), 16.0, -256.0, "is_lt", "mult")
+            if LOADS.index(end) in S_T: act(A("Tt", lo, end), A("F", lo, end), "Identity", 2152.5)
+            else: ts(A("Tt", lo, end), A("F", lo, end), 2152.5, None, "add")
+            ts(A("Mt", lo, end), A("F", lo, end), 16.0, 763.0 / 64, "is_lt", "add")
         pb = A("ps%d" % (j % 8), 0, 512)
-        lin(pb, [(1.0, A("F", lo, hi)), (1.0, A("Zt", lo, hi))])
-        if j % 4 in V_EVAC: cp(A("Zt", lo, hi), pb)
-        else: act(A("Zt", lo, hi), pb, "Identity")
-    io(A("W", NP, NP + 16), [[0, 16]], 0, 0)
+        lin(pb, [(-1.0, A("F", lo, hi))] * (j not in V_EVAC) + [(-31.0, A("Tt", lo, hi)), (7680.0, A("Mt", lo, hi))])
+        if j in V_EVAC: tt(A("Z", lo, hi), pb, A("F", lo, hi), "subtract")
+        else: act(A("Z", lo, hi), pb, "Identity")
     act(A("kz", 0, NP), A("k0s", 0, NP), "Relu", -XH * (NM - 1), XH)
     for lo in range(0, NP, C):
         hi = min(NP, lo + C)
-        lin(A("ps3", lo, hi), [(CW, A("ones", 0, hi - lo)), (65536.0, A("y0s", lo, hi)), (1.0, A("kz", lo, hi))])
+        lin(A("ps3", lo, hi), [(wide((129.0 * 65536, KO)), A("ones", 0, hi - lo)), (65536.0, A("y0s", lo, hi)), (1.0, A("kz", lo, hi))])
     tt(A("W", 0, NP), A("k0s", 0, NP), A("ps3", 0, NP), "add")
-    YB = -0.25 - 61.0 / 128
+    YB = 73.0 / 128
 
-    arr = [0]
+    arr, spans = [0], []
     for t in range(ST):
         for c in range(NCH):
-            cs_, first = str(c), len(ops)
+            now[:] = [t, c]
+            cs_, first = str(c), len(body)
             def B(j): return A("b" + cs_, j * C, (j + 1) * C)
             def Fl(j): return A("f" + cs_, j * C, (j + 1) * C)
             def In(j): return A("i" + cs_, j * C, (j + 1) * C)
-            turn_ = t * NCH + c
             if NCH == 2: bank = {"y": 4 * c, "a": 4 * c + 1, "z": 4 * c + 2, "w": 4 * c + 3, "d": 2}
-            else: bank = {"y": 2 * c, "a": 2 * c + 1, "z": 6 + turn_ % 2, "d": 7 - turn_ % 2}
+            else: bank = {"y": 2 * c, "a": 2 * c + 1, "z": 6, "w": 7, "d": 7}
             def ps(name, n=C):
                 k, lo = SLOTS[name]
                 return A("ps%d" % bank[k], lo, lo + n)
+            def pick(o): return A(o[0], o[1] + 15, o[2], 16)
             rb, sb = "rb%d%d" % (t, c), "sb%d%d" % (t, c)
             x, hp, s = A(rb, 0, C), A(rb, C, 2 * C), A(rb, 2 * C, 3 * C)
             xn, hs, s6 = A(sb, 0, C), A(sb, C, 2 * C), A(sb, 2 * C, 3 * C)
-            n32, nn32, nn16 = A("rn%d%d" % (t, c), 0, C), A("sn%d%d" % (t, c), 0, C), A("su%d%d" % (t, c), 0, C)
-            VG, VF, VT, ca, cb = "VG" + cs_, "VF" + cs_, "VT" + cs_, "ca" + cs_, "cb" + cs_
-            cand, rl, Pk, e, sx, se, sg, ap_, pre, aw, yc, ad, hy, hv, eh, rr, sumE = [B(j) for j in range(17)]
-            if t and SENDS[-1][-1][0] != "n": aff("n32", n32, A("ru%d%d" % (t, c), 0, C))
-            for j in range(C // PIECE):
-                lo, hi = 16 * j * PIECE, 16 * (j + 1) * PIECE
-                src = IND(A("Zt", 0, NM), A("ru%d%d" % (t, c), j * PIECE, (j + 1) * PIECE))
-                if j in G_DERIVE:
-                    act(A(VG, lo, hi), src, "Identity", -2552.5, -1.0)
-                    sel(A(VT, 16 + lo, 16 + hi), A(VG, lo, hi), [[0, hi - lo]], 0.0, 1, 0)
-                    continue
-                for h in range(CUT):
-                    w0, w1 = j * PIECE + h * PIECE // CUT, j * PIECE + (h + 1) * PIECE // CUT
-                    src = IND(A("Zt", 0, NM), A("ru%d%d" % (t, c), w0, w1))
-                    if (t, c, j) in V_GATHER: cp(A(VF, 16 * w0, 16 * w1), src)
-                    else: act(A(VF, 16 * w0, 16 * w1), src, "Identity")
-                if j in V_DERIVE: ts(A(VT, 16 + lo, 16 + hi), A(VF, lo, hi), -1.0, -2552.5, "mult", "add")
-                else: act(A(VT, 16 + lo, 16 + hi), A(VF, lo, hi), "Identity", -2552.5, -1.0)
-            n, m = C // SUB, 16 // R1
-            for j in range(SUB):
-                lo, hi = j * n, (j + 1) * n
-                wide = lo // PIECE in G_DERIVE
-                y1 = A(ps("y1")[0], R1 * lo, R1 * hi)
-                if G_DERIVE or j == 0:
-                    a, b = (lo, hi) if G_DERIVE else (0, C)
-                    for h in range(R1):
-                        o = A(y1[0], R1 * a + h, R1 * b, R1)
-                        if "y1" in ON_S: act(o, A(rb, a, b), "Identity", -1.0 if wide else -2551.5, -1.0 if wide else 1.0)
-                        elif wide: lin(o, [(-1.0, A("ones", a, b)), (-1.0, A(rb, a, b))])
-                        else: lin(o, [(CY1, A("ones", a, b)), (1.0, A(rb, a, b))])
+            n16, nn16, nn32 = A("ru%d%d" % (t, c), 0, C), A("su%d%d" % (t, c), 0, C), In(5)
+            VF, ca, cb, tu = "VF" + cs_, "ca" + cs_, "cb" + cs_, "tu" + cs_
+            vv, cand, c4, na, eb, e1, zx, sg, rr, yc, ad, hv, hy, ap_, yb, aw = [B(j) for j in range(16)]
+            r2 = A("h" + cs_, 0, C)
+            FC, F4, FN, FG, FH, FV, FP = [amp(n) for n in ("cand", "c4", "na", "sg", "hs", "hv")] + [amp("hs", max(t - 1, 0), c)]
+            def vf(lo, hi, k=0, step=1): return A(VF, 16 * (lo + 1 + lo // HA) + k, 16 * (hi + 1 + lo // HA), step)
+            for j, (lo, hi) in enumerate(zip((0,) + CUTS, CUTS)):
+                src = IND(A("Z", 0, NM), A(n16[0], lo, hi))
+                if (t, c, j) in V_GATHER: cp(vf(lo, hi), src)
+                else: act(vf(lo, hi), src, "Identity")
+            m, y1, cnt = 16 // R1, ps("y1")[0], ps("cnt")[0]
+            for h in range(R1):
+                lin(A(y1, h, R1 * C, R1), [(1.0, x)])
+            def row(k, lo, hi): return A(ca, (k % m) * R1 * C + R1 * lo + k // m, (k % m) * R1 * C + R1 * hi, R1)
+            for lo, hi in zip((0,) + SUBS, SUBS):
                 for k in range(m):
-                    o = A(ca, 16 * lo + R1 * k * n, 16 * lo + R1 * (k + 1) * n)
-                    if wide: tt(o, y1, A(VG, 16 * lo + k, 16 * hi, m), "subtract")
-                    else: tt(o, A(VF, 16 * lo + k, 16 * hi, m), y1, "subtract")
-                sums = [(blk("Sall", k + m * h), A(ca, 16 * lo + R1 * k * n + h, 16 * lo + R1 * (k + 1) * n, R1)) for k in range(m) for h in range(R1)]
-                if LEAN:
-                    se_ = A(sumE[0], sumE[1] + lo, sumE[1] + hi)
-                    if LEAN == 2 or j == 0:
-                        a, b = (lo, hi) if LEAN == 2 else (0, C)
-                        lin(A(ps("pre")[0], a, b), [(blk("Sall", k), A(VT, 16 + 16 * a + k, 16 + 16 * b, 16)) for k in range(16)])
-                        aff("st", A(sumE[0], sumE[1] + a, sumE[1] + b), A(ps("pre")[0], a, b), -0.125, -2560.0)
-                    lin(A(ps("cnt")[0], lo, hi), sums[:12] + [(256.0, A(rb, 2 * C + lo, 2 * C + hi)), (4.0 * FH, A(rb, C + lo, C + hi)), (-8.0, se_)] + sums[12:])
-                elif WHOLE:
-                    if j == 0: lin(ps("cnt"), [(4.0 * FH, hp)], close=False)
-                    if j == SUB - 1: lin(ps("cnt"), [(256.0, s)] + [(blk("Sall", k), A(VT, 16 + k, 16 + 16 * C, 16)) for k in range(16)], True, False)
-                    lin(A(ps("cnt")[0], lo, hi), sums, True, j == SUB - 1)
-                else:
-                    flag = [(4.0 * FH, A(rb, C + lo, C + hi))]
-                    lin(A(ps("cnt")[0], lo, hi), flag * (SENDS[0][0][2] > C)
-                        + [(blk("Sall", k), A(VT, 16 + 16 * lo + k, 16 + 16 * hi, 16)) for k in range(16)]
-                        + sums[:8] + [(256.0, A(rb, 2 * C + lo, 2 * C + hi))] + flag * (SENDS[0][0][2] == C) + sums[8:])
-            sign("cand", cand, ps("cnt"), 20480.0 * (LEAN > 0) - 72, -1.0, 20480.0 * (LEAN > 0) - 72)
-            if "rl" in ON_S:
-                lin(ps("rl"), [(1.0, TURN), (mat(BH), cand)])
-                act(rl, ps("rl"), "Relu", -7.0)
-                lin(ps("Pk"), [(1.0, TURN), (mat(LO), cand), (-1.0, rl)])
-            else:
-                lin(ps("rl"), [(mat(BH), cand)])
-                tt(rl, A("turn", C, 2 * C), ps("rl"), "max")
-                lin(ps("Pk"), [(mat(LO), cand), (-1.0, rl)])
-            sign("Pk", Pk, ps("Pk"), cf(KH), 1.0, cf(KH))
-            def pick(o): return A(o[0], o[1] + 15, o[2], 16)
-            if "idx" in SCAN:
-                lin(ps("rl"), [(1.0, A("own", C, 2 * C)), (mat(BP), Pk)])
-                scan(Fl(0), A("own", 2 * C, 3 * C), ps("rl"))
-                ts(A("tu" + cs_, 0, D), pick(Fl(0)), 23.5 - 2048, 0.0, "add", "max")
-            else:
-                pd = ps("idx", D)
-                lin(pd, [(1.0, A("base", 0, D))] + [(blk("Pall", a), A(Pk[0], Pk[1] + a, Pk[2], 16)) for a in range(16)])
-                ts(A("tu" + cs_, 0, D), pd, cf(KB), 0.0, "add", "max")
-            act(e, IND(A(VT, 0, 16 * C + 16), A("tu" + cs_, 0, D)), "Relu", -160.0, -1.0 / 16)
-            lin(ps("pre"), [(6.0, s), (FC, cand), (mat(SHF), Pk)])
-            sign("pre", pre, ps("pre"), -1.5, 1.0, 1.5)
-            if "sx" in ON_S: act(sx, x, "Sign")
-            else: ts(sx, x, 0.0, None, "is_gt")
-            if "se" in ON_S: act(se, e, "Sign")
-            else: ts(se, e, 0.0, None, "is_gt")
-            lin(ps("dl"), [(1.0, x), (-1.0, e)])
-            sign("sg", sg, ps("dl"), 0.5, 1.0, -0.5)
-            act(xn, ps("dl"), "Abs")
-            lin(ps("y2"), [(CY2, ONE), (8.0, x), (-512.0, sx), (8.0, e), (-512.0, se), (136.0 * FG, sg), (8.0, xn)])
-            C2 = 2560.0 - 0.125 + 1.0 / 512
-            if S_ROWS: aff("yb", rl, ps("y2"), 1.0 / 16, -C2 / 16)
+                    tt(A(ca, k * R1 * C + R1 * lo, k * R1 * C + R1 * hi), vf(lo, hi, k, m), A(y1, R1 * lo, R1 * hi), "add")
+                sums = [(blk("S1", k + m * h), row(k + m * h, lo, hi)) for k in range(m) for h in range(R1)]
+                lin(A(cnt, lo, hi), [(wide((512.0, -25.0 / 32)) if CANCEL else -25.0 / 32, A("ones", lo, hi))] * DIRECT + sums[:10]
+                    + [(-0.25, A(rb, 2 * C + lo, 2 * C + hi)), (-FP / 64, A(rb, C + lo, C + hi))] + sums[10:])
+            q_ = A("h" + cs_, C, 2 * C) if CANCEL else In(0)
+            aff("q", q_, ps("cnt"), 1.0, 5.0 / 32 if DIRECT else -0.625)
+            if DIRECT: tt(cand, ps("cnt"), q_, "is_gt")
+            if not DIRECT or NCH == 2: tt(vv, ps("cnt"), q_, "subtract")
+            if not DIRECT: sign("cand", cand, vv, 25.0 / 32, True)
+            lin(ps("c4"), [(1.0, TURN), (tri(-1.0, 16.0, 1) if DIRECT else tri(-0.5 * FC, 8.0 * FC, 1), cand)])
+            sign("c4", c4, ps("c4"), 15.5 if DIRECT else (0.5, 7.5), True)
+            lin(ps("na"), [(tri(0.5 * F4, 2.0 * F4, -1), c4)])
+            sign("na", na, ps("na"), (0.5, -5.0), False)
+            lin(ps("idx"), [(1.0, OWNI), (grp(col(F4, 2033.0 * F4), "BP"), c4), (grp(col(FN, 2033.0 * FN), "BP"), na)])
+            scan(Fl(0), OWND, ps("idx"))
+            if DIRECT and NCH > 2: tt(vv, ps("cnt"), q_, "subtract")
+            if eng("ix") == "S": act(A(tu, 0, D), pick(Fl(0)), "Relu", -2033.0, 0.5)
+            else: ts(A(tu, 0, D), pick(Fl(0)), 0.5, -2033.0, "mult", "add")
+            for lo, hi in WINS:
+                aff("eb", A(eb[0], eb[1] + lo, eb[1] + hi), IND(vf(lo, hi, -16), A(tu, lo // 16, hi // 16)), -1.0 / 512, 160.0 + (B0 + 8) / 512)
+            aff("e1", e1, eb, 1.0, -161.0, True)
+            if eng("zx") == "S": act(zx, x, "Relu", 60.0, -60.0)
+            else: ts(zx, x, 0.5, 60.0, "is_lt", "mult")
+            if FG == 1:
+                lin(ps("sg"), [(1.0, x), (-1.0, e1)])
+                act(sg, ps("sg"), "Sign", -0.5)
+            else: tt(sg, e1, A(y1, 0, R1 * C, R1), "is_lt")
+            lin(ps("dl"), [(1.0, x), (-1.0 / 16, eb), (-15.0 / 16, e1)])
+            act(xn, ps("dl"), "Abs", 10.0 - 15.0 / 16)
+            lanes = DIRECT and not CANCEL
+            CY2 = wide((-49408.0 if FG == 1 else -45312.0, 84.0 - 16 * lanes, -1.0 / 16), lanes)
+            lin(ps("y2"), [(CY2, ONE), (-256.0, x), (-256.0, zx), (432.0, eb), (-688.0, e1), (-4096.0 * FG, sg), (-256.0, xn)])
             for k in range(16 - S_ROWS):
-                if LEAN and not S_ROWS and k == YB_AT: aff("yb", rl, ps("y2"), 1.0 / 16, -C2 / 16)
-                tt(A(cb, k * C, (k + 1) * C), A(VT, 16 + k, 16 + 16 * C, 16), ps("y2"), "add")
+                if CANCEL and k == YB_AT: aff("yb", yb, ps("y2"), -1.0 / 512, (B0 - 16 + 63.0 / 16) / 512 - 80)
+                tt(A(cb, k * C, (k + 1) * C), ps("y2"), row(k, 0, C), "subtract")
             for k in range(16 - S_ROWS, 16, 2):
-                pw = ps("pre")[0]
+                pw = ps("mul")[0]
                 for h in range(2):
-                    lin(A(pw, h * C, (h + 1) * C), [(1.0, A(VT, 16 + k + h, 16 + 16 * C, 16)), (16.0, rl)])
-                act(A(cb, k * C, (k + 2) * C), A(pw, 0, 2 * C), "Identity", C2)
-            rows = sorted(range(16), key=lambda k: k if k < 16 - S_ROWS else (k - 16 + S_ROWS) // 2 * 4 + 5.5)
-            sums = [(blk("Sall", k), A(cb, k * C, (k + 1) * C)) for k in rows]
-            if LEAN: sums = [(8.0, sumE)] + sums[:12] + [(mat(7), rl), (FR, pre)] + sums[12:]
-            lin(ps("sum"), sums)
-            if "u" in SCAN:
-                lin(ps("hs"), [(1.0, A("own", 0, C)), (mat(HB), xn)])
-                scan(Fl(5), A("own", 2 * C, 3 * C), ps("hs"))
-                pu, w241 = pick(Fl(5)), 120.5
-            else:
-                pu, w241 = ps("u", D), 241.0
-                lin(pu, [(blk("Hall", a), A(sb, a, C, 16)) for a in range(16)])
-            if "ti" in ON_S: act(A("ti" + cs_, 0, D), pu, "Identity", 0.0, w241)
-            else: ts(A("ti" + cs_, 0, D), pu, w241, None, "mult")
+                    lin(A(pw, h * C, (h + 1) * C), [(-1.0, row(k + h, 0, C)), (-512.0, yb)])
+                act(A(cb, k * C, (k + 2) * C), A(pw, 0, 2 * C), "Identity", B0 - 16 + 63.0 / 16 - 80 * 512)
+            sums = [(blk("S1", k), A(cb, k * C, (k + 1) * C)) for k in sorted(range(16), key=lambda k: k if k < 16 - S_ROWS else k - 3.5)]
+            lin(ps("sum"), [(1.0, vv), (FP / 64, hp)] + [(1.0, q_)] * CANCEL + sums[:YB_AT + 3] + [(grp(1.0), yb)] * CANCEL + sums[YB_AT + 3:])
             cint = A("cint", D * c, D * c + D)
-            ts(cint, A("ti" + cs_, 0, D), 6, NP - 1, "arith_shift_right", "bitwise_and")
-            if "tu" in ON_S: act(A("tu" + cs_, 16, 16 + D), cint, "Identity")
-            else: cp(A("tu" + cs_, 16, 16 + D), cint)
-            if c == NCH - 1:
-                pq = "ps%d" % bank["d"]
-                cp(A("cf", 0, DW), A("cint", 0, DW))
+            if eng("u") == "P":
+                pu = A(ps("u")[0], 2 * C, 2 * C + D)
+                lin(pu, [(blk("SH", a), A(sb, a, C, 16)) for a in range(16)])
+                aff("ti", A("i" + cs_, C, C + D), pu, 241.0)
+                ts(cint, A("i" + cs_, C, C + D), 6, NP - 1, "arith_shift_right", "bitwise_and")
+            else:
+                lin(ps("u"), [(1.0, OWNU), (grp(HHI), xn), (grp(HLO), xn)])
+                scan(In(1), OWND, ps("u"))
+                ts(cint, pick(In(1)), 6, NP - 1, "arith_shift_right", "bitwise_and")
+            aff("tu", A(tu, 16, 16 + D), cint)
+            each = LAST > 1 and t == ST - 1
+            if c == NCH - 1 or each:
+                pq = "ps%d" % bank[DBANK]
+                b0, nb = (D * c, D) if each else (0, DW)
+                CF = A("cf", b0, b0 + nb)
+                aff("cf", CF, A("cint", b0, b0 + nb))
                 for a in range(16):
-                    lin(A(pq, DW * a, DW * a + DW), [(blk("Rall", a), A("cf", 0, DW))])
-                tt(A("Eq", 0, NW), A(pq, 0, NW), A("mask", 0, NW), "is_equal")
-                lin(A(pq, 424, 424 + DW), [(1.0 / 2048, A("cf", 0, DW))] + [(blk("Sall", a), A("Eq", DW * a, DW * a + DW)) for a in range(16)])
-                ts(A("soff", 0, 2 * DW, 2), A(pq, 424, 424 + DW), 2048.0, cf(K512), "mult", "min")
-            lin(ps("rr"), [(mat(HB), xn)])
+                    lin(A(pq, nb * a, nb * a + nb), [(blk("Rall", a), CF)])
+                tt(A("Eq", 16 * b0, 16 * (b0 + nb)), A(pq, 0, 16 * nb), A("mask", 0, NW, DW // nb), "is_equal")
+                lin(A(pq, 424, 424 + nb), [(2.0 ** -19, CF)] + [(blk("S1", a), A("Eq", 16 * b0 + nb * a, 16 * b0 + nb * a + nb)) for a in range(16)])
+                ts(A("soff", 2 * b0, 2 * (b0 + nb), 2), A(pq, 424, 424 + nb), 2.0 ** 19, col(1.0, float(NP)), "mult", "min")
+            lin(ps("rr"), [(grp(H2), xn)])
             aff("rr", rr, ps("rr"), 1.0 / 2048, 128.5 + 1.0 / 2048)
-            MUL, ADD, K3 = ps("mul"), ps("add"), ps("k3")
-            if EARLY == 2:
-                lin(MUL, [(CM, ONE), (mat(HB), xn), (-2048.0, rr)])
-                tt(In(0), n32, MUL, "mult")
-                ts(In(1), In(0), 5, NM - 1, "arith_shift_right", "bitwise_and")
-                aff("d1", Fl(3), In(1), 1.0, cf(K37))
-                aff("add", MUL, n32, 1.0, float(NM))
-            elif EARLY:
-                lin(MUL, [(CM, ONE), (mat(HB), xn), (-2048.0, rr)])
-                tt(In(0), n32, MUL, "mult")
-                ts(In(1), In(0), 5, NM - 1, "arith_shift_right", "bitwise_and")
-                if "a1" in ON_S: act(MUL, n32, "Identity", cf(K37B))
-                else: ts(MUL, n32, cf(K37), float(NM), "add", "add")
-                tt(Fl(3), In(1), MUL, "add")
-            act(Fl(0), IND(A("W", 0, NP + 16), A("tu" + cs_, 16, 16 + D)), "Identity")
-            aff("yc", yc, Fl(0), 1.0 / 65536, YB)
-            lin(ps("ad"), [(-1.0, xn), (1.0, yc)])
-            act(ad, ps("ad"), "Abs", -129.0)
-            lin(ps("hs"), [(mat(BD), ad)])
-            sign("hs", hs, ps("hs"), cf(THC), -1.0, cf(THC))
-            if "k3" in WIDE: lin(K3, [(IF, Fl(0)), (-65536.0, yc), (-16384.0 * FH, hs)])
-            else:
-                lin(K3, [(65536.0, yc), (16384.0 * FH, hs)])
-                tt(K3, Fl(0), K3, "subtract")
-            if EARLY == 1: tt(Fl(4), Fl(3), K3, "min")
-            tt(eh, n32, K3, "is_equal")
-            sign("hv", hv, K3, 8191.5, -1.0, 8191.5)
-            lin(ps("hy"), [(-1.0, xn), (1.0, yc), (16.0 * FH, hs)])
+            lin(ps("mul"), [(wide((129.0 * 2048, 1.0)), ONE), (grp(H2), xn), (-2048.0, rr)])
+            tt(In(2), n16, ps("mul"), "mult")
+            ts(In(3), In(2), 5, NM - 1, "arith_shift_right", "bitwise_and")
+            aff("a1", ps("a1"), n16, 1.0, col(37.0, 0.0))
+            tt(Fl(1), In(3), ps("a1"), "add")
+            aff("wg", Fl(0), IND(A("W", 0, NP + 16), A(tu, 16, 16 + D)))
+            aff("yc", yc, Fl(0), -1.0 / 65536, YB)
+            lin(ps("ad"), [(1.0, xn), (1.0, yc)])
+            act(ad, ps("ad"), "Abs", 129.0)
+            lin(ps("hs"), [(grp(1.0), ad)])
+            sign("hs", hs, ps("hs"), THC, False)
+            K3 = ps("k3")
+            lin(K3, [(IF, Fl(0))] * (eng("k3") == "P") + [(65536.0, yc), (-XH / 2 * FH, hs)])
+            if eng("k3") != "P": tt(K3, Fl(0), K3, "add")
+            tt(Fl(2), Fl(1), K3, "min")
+            last = LAST and (t, c) == (ST - 1, NCH - 1)
+            if last:
+                act(Fl(3), n16, "Identity", -8192.0)
+                tt(hv, Fl(3), K3, "is_equal")
+            else: sign("hv", hv, K3, -0.5, False)
+            lin(ps("hy"), [(-1.0, xn), (-1.0, yc), (16.0 * FH, hs)])
             aff("hy", hy, ps("hy"), 1.0, -129.0, True)
-            if LEAN:
-                aff("ap", ap_, ps("sum"), 16.0, 176.0)
-                aff("thr", Fl(1), ap_, 63.0 / 1024, cf(DN + t))
-                tt(aw, Fl(1), ps("sum"), "is_ge")
+            if last:
+                lin(ps("hs"), [(1.0, xn), (1.0, hy), (-8.0 * FH, hs)])
+                act(zx, ps("hs"), "Identity", -8.0)
+                lin(ps("hy"), [(8192.0 * FH, hs), (-16384.0, hv)])
+                tt(Fl(3), n16, ps("hy"), "max")
+            if CANCEL:
+                if APART: ts(ap_, ps("sum"), 1.5 * 2.0 ** 16 + 25.0 / 32, 1.5 * 2.0 ** 16, "add", "subtract")
+                aff("r2", r2, ps("sum"), 1.0, 25.0 / 32)
             else:
-                if "mg" in ON_S:
-                    act(Fl(2), ps("sum"), "Identity", MAGIC)
-                    act(Fl(1), Fl(2), "Identity", -MAGIC)
-                else: ts(Fl(1), ps("sum"), MAGIC, MAGIC, "add", "subtract")
-                tt(Fl(2), ps("sum"), Fl(1), "subtract")
-                aff("ap", ap_, Fl(2), 16.0, 192.0)
-                lin(ps("thr"), [(blk("Dg", t), ONE), (-189.0 / 16 * FR, pre), (63.0 / 1024, ap_)])
-                tt(ps("thr") if EARLY == 2 else aw, Fl(2), ps("thr"), "is_le")
-            if EARLY == 2:
-                tt(Fl(4), Fl(3), ps("thr"), "mult")
-                aff("aw", aw, ps("thr"))
-                tt(Fl(3), Fl(4), MUL, "add")
-                tt(In(2), Fl(3), K3, "min")
-            elif "q" in WIDE:
-                lin(ps("q"), [(IF, n32), (8192.0, ONE), (65536.0, aw)])
-                tt(In(2), Fl(4), ps("q"), "min")
-            elif EARLY:
-                aff("add", ADD, aw, 32768.0, 8192.0)
-                tt(ADD, n32, ADD, "add")
-                tt(In(2), Fl(4), ADD, "min")
-            else:
-                lin(MUL, [(mat(HB), xn), (-2048.0, rr), (4096.0, aw)])
-                act(MUL, MUL, "Relu", 129.0 * 2048 + 1 - 4096)
-                act(ADD, aw, "Identity", 8192.0, cf(K37))
-                tt(In(0), n32, MUL, "mult")
-                ts(In(1), In(0), 5, NM - 1, "arith_shift_right", "bitwise_and")
-                tt(ADD, n32, ADD, "add")
-                tt(Fl(3), In(1), ADD, "add")
-                tt(In(2), Fl(3), K3, "min")
-            ts(nn32, In(2), NM - 1, None, "bitwise_and")
-            lin(ps("s6"), [(1.0, eh), (-0.5 * FV, hv), (-1.0, aw)])
-            aff("s6", s6, ps("s6"), 1.0, 0.5, True)
+                aff("mg", In(0), ps("sum"))
+                tt(r2, ps("sum"), In(0), "subtract")
+            if not (CANCEL and APART): ts(ap_, r2, 1.5 * 2.0 ** 16, 1.5 * 2.0 ** 16, "add", "subtract")
+            Q = ps("wake")
+            lin(Q, [(dg(t), ONE), (16 * U * FN, na), (8192 * U, r2), (-8064 * U, ap_)][::-1 if CANCEL and APART else 1][::-1 if CANCEL and APART else 1])
+            if last: ts(Fl(0), Q, float(NM), None, "min")
+            n32 = A("n32", t % 2 * NW + c * C, t % 2 * NW + (c + 1) * C)
+            if eng("ent") == "S" and not last or eng("Q") == "S": sel(n32, n16, [[0, C]], 0.0, 1, 0)
+            if eng("Q") == "S":
+                act(aw, Q, "Relu")
+                lin(Q, [(IF, n32), (1.0, aw)])
+            else: tt(Q, n16, Q, "max")
+            tt(In(4), Fl(2), Q, "min")
+            ts(nn32, In(4), NM - 1, None, "bitwise_and")
+            tt(s6, nn32, Q, "is_equal")
             if t < ST - 1:
-                if "u16" in ON_S: act(nn16, nn32, "Identity")
-                else: cp(nn16, nn32)
+                aff("u16", nn16, nn32)
                 for call in SENDS:
                     to = [A("r%s%d%d" % (p_, t + 1, c), lo, hi) for p_, lo, hi in call]
-                    ops.append(("G", "send", None, [A("s%s%d%d" % (p_, t, c), lo, hi) for p_, lo, hi in call], (to, arr[0])))
+                    put("G", "send", None, [A("s%s%d%d" % (p_, t, c), lo, hi) for p_, lo, hi in call], (to, arr[0]))
                     for j, o in enumerate(to):
-                        ops.append(("R", "recv", o, [], (arr[0], j, len(to))))
+                        put("R", "recv", o, [], (arr[0], j, len(to)))
                     arr[0] += len(to)
             else:
                 lin(ps("yt"), [(8192.0, s6)])
                 tt(A("oyt", c * C, (c + 1) * C), nn32, ps("yt"), "add")
                 dma("Y", A("yt", c * C, (c + 1) * C), A("oyt", c * C, (c + 1) * C))
                 dma("Y", A("yx", c * C, (c + 1) * C), xn)
-            lin(ps("ent"), [(IF, n32)] * ("ent" in WIDE) + [(CENT, ONE), (65536.0, xn), ((-524288.0 + XH / 2) * FH, hs), (65536.0, hy), (-XH, eh), (XA, aw)])
-            if "ent" in WIDE: act(A("ent", c * C, (c + 1) * C), ps("ent"), "Identity")
-            else: tt(A("ent", c * C, (c + 1) * C), n32, ps("ent"), "add")
-            SPANS.append((first, len(ops), c))
-        for b in range(DW):
-            cp(IND(A("W", 0, NP + 16), A("soff", 2 * b, 2 * b + 1)), A("ent", 16 * b, 16 * b + 16))
-    for j, lo in enumerate(range(0, NP, 256)):
-        hi = lo + 256
-        act(A("oy1", lo, hi), A("W", lo, hi), "Identity", YB, 1.0 / 65536)
-        if "out" in WIDE:
-            lin(A("ps%d" % j, 0, hi - lo), [(IF, A("W", lo, hi)), (-65536.0, A("oy1", lo, hi))])
-            ts(A("oyk", lo, hi), A("ps%d" % j, 0, hi - lo), -16384.0, float(NM), "add", "min")
-        else:
-            lin(A("ps%d" % j, 0, hi - lo), [(65536.0, A("oy1", lo, hi))])
-            tt(A("oyj", lo, hi), A("W", lo, hi), A("ps%d" % j, 0, hi - lo), "subtract")
-            ts(A("oyk", lo, hi), A("oyj", lo, hi), -16384.0, float(NM), "add", "min")
-        dma("Y", A("yk", lo, hi), A("oyk", lo, hi))
-    act(A("oy2", 0, NP), A("oy1", 0, NP), "Identity", -129.0)
+            if not last:
+                lin(ps("ent"), ([(wide((121.0 * 65536, KO + XA)), ONE)] if eng("ent") == "V" else [])
+                    + [(65536.0, xn), ((-524288.0 + XH / 2) * FH, hs), (65536.0, hy), (-XH / 2 * FV, hv), (-XA, s6)])
+                if eng("ent") == "V": tt(A("ent", c * C, (c + 1) * C), n16, ps("ent"), "add")
+                else: act(A("ent", c * C, (c + 1) * C), ps("ent"), "Identity", 121.0 * 65536 + KO + XA)
+            spans.append((first, len(body), c))
+        WT = "W2" if each else "W"
+        if each: act(A(WT, 0, NP), A("W", 0, NP), "Identity")
+        for b in range(DW - D * last):
+            o, e = IND(A(WT, 0, NP + 16), A("soff", 2 * b, 2 * b + 1)), A("ent", 16 * b, 16 * b + 16)
+            if eng("ent", t, b // D) == "V": cp(o, e)
+            else: tt(o, e, A("n32", t % 2 * NW + 16 * b, t % 2 * NW + 16 * b + 16), "add")
+    step = NP if LAST else 256
+    for j, lo in enumerate(range(0, NP, step)):
+        hi = lo + step
+        act(A("oy1", lo, hi), A(WT, lo, hi), "Identity", YB, -1.0 / 65536)
+        lin(A("ps%d" % j, 0, hi - lo), [(IF, A(WT, lo, hi)), (65536.0, A("oy1", lo, hi))])
+        ts(A("oyk", lo, hi), A("ps%d" % j, 0, hi - lo), -KO, float(NM), "add", "min")
+        if not LAST: dma("Y", A("yk", lo, hi), A("oyk", lo, hi))
+    act(A("oy2", 0, NP), A("oy1", 0, NP), "Identity", -129.0, -1.0)
+    for b in range(D if LAST else 0):
+        off, lo = A("soff", 2 * (DW - D + b), 2 * (DW - D + b) + 1), 16 * b
+        cp(IND(A("oy2", 0, NP + 16), off), A(zx[0], zx[1] + lo, zx[1] + lo + 16))
+        tt(IND(A("oyk", 0, NP + 16), off), A(Fl(0)[0], lo, lo + 16), A(Fl(0)[0], 3 * C + lo, 3 * C + lo + 16), "max")
+    if LAST: dma("S", A("yk", 0, NP), A("oyk", 0, NP))
     dma("Y", A("yy", 0, NP), A("oy2", 0, NP))
-    return ops
+    SPANS[:] = [(lo + len(head), hi + len(head), c) for lo, hi, c in spans]
+    return head + body
 
 
 def regions(op):
@@ -476,7 +461,7 @@ def regions(op):
     return [r for r in rd if r[0] not in DRAM], [r for r in wr if r[0] not in DRAM]
 
 
-SC = {"gather": 1.55, "scatter": 2.9, "call": 10, "act": 80, "psum": 25, "pe": 0.43, "mm": 10, "lat": 0, "V": 70, "S": 35, "P": 40, "same": 70, "cross": 45, "pool": 270, "bw": 290.0, "dma": 1350, "gdma": 300, "issue": 450, "first": 1800, "link": 1300, "lbw": 27.0, "row": 25, "cyc": 0.85}
+SC = {"gather": 1.55, "scatter": 2.9, "call": 24, "act": 80, "psum": 25, "pe": 0.41, "mm": 19, "lat": 15, "V": 70, "S": 35, "P": 40, "same": 70, "cross": 45, "pool": 200, "bw": 290.0, "dma": 1350, "gdma": 300, "issue": 450, "first": 1800, "link": 1300, "lbw": 27.0, "row": 25, "cyc": 0.85}
 
 
 def cost(op, sc=SC):
@@ -518,18 +503,15 @@ def links():
                     (soft if ops[j][0] == op[0] else hard)[i].add(j)
                 bank[r[0]] = i
         for r in wr:
-            hist[r[0]] = [h for h in hist.get(r[0], []) if not (r[3] == 1 and r[1] <= h[1] and h[2] <= r[2])] + [(i, r[1], r[2], True)]
+            whole = r[3] == 1 and not (op[1] == "ms" and op[4][1] is not None)
+            hist[r[0]] = [h for h in hist.get(r[0], []) if not (whole and r[1] <= h[1] and h[2] <= r[2])] + [(i, r[1], r[2], True)]
         for r in rd:
             hist.setdefault(r[0], []).append((i, r[1], r[2], False))
         if op[1] == "send":
-            if op[3][-1][0][:2] == "sn" or op[3][0][1] >= C: soft[i].add(max(sends.values()))
+            if op[3][0][1] >= C: soft[i].add(max(sends.values()))
             sends[op[4][1]] = i
         if op[1] == "recv": soft[i].add(i - 1)
-    if FIRM:
-        loads = [i for i, op in enumerate(ops[:SPANS[0][0]]) if op[:2] == ("Y", "dma")]
-        for i, j in zip(loads, loads[1:]): soft[j].add(i)
-        store = [i for i, op in enumerate(ops) if op[2] and op[2][0] == "kz"][0]
-        soft[store].add(max(i for i in range(*SPANS[0][:2]) if ops[i][2] and ops[i][2][0] == "VF0"))
+        if FIRM and op[1] == "dma" and op[2][0] == "F" and op[2][1]: soft[i].add(i - 1)
     return ops, hard, soft
 
 
@@ -566,7 +548,7 @@ def plan(sc=SC):
     for lead in LEADS:
         for late in LATES:
             prio = way[:]
-            for lo, hi, c in SPANS[:ST * NCH]:
+            for lo, hi, c in SPANS:
                 for i in range(lo, hi):
                     prio[i] -= lead * c + (late if ops[i][1] == "act" and ops[i][3][0][0] == "@" and count(ops[i][2]) > C else 0)
             for _ in range(4):
@@ -574,6 +556,18 @@ def plan(sc=SC):
                 if best is None or got[0] < best[0]: best = got
                 back = schedule(q, dur, [0.0] * n, [got[1][i] + dur[i] for i in range(n)], suc, pre)[1]
                 prio = [back[i] + dur[i] for i in range(n)]
+    cur, seed = best, [12345]
+
+    def rnd():
+        seed[0] = (seed[0] * 1103515245 + 12345) % 2147483648
+        return seed[0] / 2147483648.0
+    for _ in range(ROUNDS):
+        a, lo, w = (100, 300, 1000)[int(3 * rnd())], rnd() * cur[0], 3000 + 17000 * rnd()
+        prio = [cur[1][i] + dur[i] + ((2 * rnd() - 1) * a if lo <= cur[1][i] <= lo + w else 0) for i in range(n)]
+        back = schedule(q, dur, [0.0] * n, prio, suc, pre)[1]
+        got = schedule(q, dur, tail, [back[i] + dur[i] for i in range(n)], pre, suc)
+        if got[0] < cur[0] + 150: cur = got
+        if got[0] < best[0]: best = got
     needed = set()
     for i in range(n): needed |= hard[i]
     return ops, hard, best[2], needed, best[1], soft, best[0]
@@ -647,7 +641,8 @@ def rank_program(g, core, T, topo):
         elif kind == "ts": ins_ = e.tensor_scalar(ap(o), ap(ins[0]), ap(ins[1]), ap(ins[2]), alu[par[0]], alu[par[1]])
         elif kind == "scan": ins_ = e.tensor_tensor_scan(ap(o), ap(ins[0]), ap(ins[1]), 0.0, AluOpType.add, AluOpType.min)
         elif kind == "cp": ins_ = e.tensor_copy(ap(o), ap(ins[0]))
-        elif kind == "ms": ins_ = e.memset(ap(o), par)
+        elif kind == "ms" and par[1] is None: ins_ = e.memset(ap(o), par[0])
+        elif kind == "ms": ins_ = e.memset(T[o[0]][par[1]:par[1] + 1, o[1]:o[2]], par[0])
         elif kind == "act": ins_ = e.activation(ap(o), ap(ins[0]), fun[par], bias=ap(ins[1]), scale=ap(ins[2]))
         elif kind == "mm": ins_ = e.matmul(ap(o), ap(ins[0]), ap(ins[1]), par[0], par[1])
         elif kind == "sel": ins_ = g.affine_select(ap(o), ap(ins[0]), par[0], alu[par[4]], par[3], par[1], par[2])

@@ -4,36 +4,42 @@ from concourse.mybir import AluOpType, ActivationFunctionType
 NM, NP, NW, ST, SH, NR = 8192, 512, 384, 3, 3, 8
 C = 192
 NCH, D = NW // C, C // 16
-R1 = 2
+R1 = 4
 DW = NW // 16
 HA = 128
 WINS = [(_w, min(C, _w + HA)) for _w in range(0, C, HA)]
-CUTS = (64, 128, 192)
-SUBS = (128, 192)
+CUTS = (64, 96, 128, 192)
+SUBS = (64, 128, 192)
 DIRECT = 1
 S_T = (2, 4, 6, 7)
 SPANS = []
 LOADS = (512, 1024, 2048, 3072, 4096, 5120, 6144, 7168, 7680, 8192)
-V_EVAC = (1, 3, 5, 7, 9, 11, 13, 15)
-V_GATHER = ((0, 0, 1),)
+V_EVAC = (0, 2, 4, 6, 8, 10, 12, 13, 15)
+V_GATHER = ((0, 0, 1), (0, 0, 2), (1, 0, 1), (2, 0, 1))
 DIAG = "SG"
-ENG = {"q": "VS", "cand": "V", "c4": "VS", "na": "VS", "ix": "V", "eb": "S", "e1": "V", "zx": "S", "sg": "S", "tu": "G", "cf": "G", "rr": "S", "a1": "S", "wg": "S", "yc": "S", "hs": "S", "k3": "P", "hv": "S", "hy": "S", "mg": "S", "u16": "G", "ent": "S", "set": "S", "col": "S", "wide": "V", "fill": "G", "grp": "S", "u": "V", "ti": "S", "Q": "V", "yb": "S", "r2": "S"}
-CANCEL = 0
+ENG = {"q": "VS", "cand": "V", "c4": "VS", "na": "VS", "ix": "S", "eb": "S", "e1": "S", "zx": "S", "sg": "S", "tu": "G", "cf": "G", "rr": "S", "a1": "S", "wg": "S", "yc": "S", "hs": "S", "k3": "P", "hv": "S", "hy": "S", "mg": "S", "u16": "S", "ent": "S", "set": "S", "col": "S", "wide": "G", "fill": "G", "grp": "S", "u": "T", "ti": "S", "Q": "V", "yb": "S", "r2": "S", "ru": "S", "cm": "S", "r2x": "-", "own": "S"}
+CANCEL = 1
 YB_AT = 6
 S_ROWS = 0
 FIRM = 1
 LAST = 1
 APART = 0
-DBANK = "d"
+PSUBS = (128, 192)
+RING = 1
+DLATE = (0, 1)
+OSTEP = 256
+DBANK = "w"
 B0 = 24592.0
 U = 32768.0
 XA, XH, KO = 25600.0, 28672.0, 6144.0
 NMAT = 56
 LEADS = (0, 3000)
 LATES = (0, 4000)
-ROUNDS = 600
+ROUNDS = 1000
+SEED = 4
+SHADES = ((1.245, 2.08, 5.0, 1.4, 0.45, 0.5), (1.1, 1.3, 3.5, 1.0, 0.41, 1.0), (0.9, 1.5, 3.0, 1.0, 0.56, 0.7))
 SENDS = ([("b", 0, C)], [("u", 0, C)], [("b", C, 3 * C)])
-SLOTS = {"y1": ("y", 0), "cnt": ("a", 0), "c4": ("z", 0), "na": ("z", C), "idx": ("z", 0), "dl": ("z", C), "sg": ("w", 0), "y2": ("y", 0), "sum": ("a", 0), "u": ("z", 0), "rr": ("w", C), "mul": ("w", 0), "a1": ("w", C), "ad": ("z", C), "hs": ("z", 0), "k3": ("w", 0), "hy": ("z", C), "wake": ("y", 0), "yt": ("y", C), "ent": ("z", 0)}
+SLOTS = {"y1": ("y", 0), "cnt": ("a", 0), "c4": ("z", 0), "na": ("z", C), "idx": ("w", C), "dl": ("z", C), "sg": ("w", 0), "y2": ("y", 0), "sum": ("a", 0), "u": ("z", 0), "rr": ("w", C), "mul": ("w", 0), "a1": ("w", C), "ad": ("z", C), "hs": ("z", 0), "k3": ("w", 0), "hy": ("z", C), "wake": ("y", 0), "yt": ("y", C), "ent": ("z", 0)}
 if NCH > 2:
     SLOTS.update({"c4": ("a", C), "na": ("a", 2 * C), "idx": ("a", 3 * C), "dl": ("a", C), "sg": ("a", 2 * C), "ent": ("a", C)})
 
@@ -42,7 +48,7 @@ for _n, _w, _d in [
         ("F", NM, "bfloat16"), ("Tt", NM, "bfloat16"), ("Mt", NM, "float16"), ("Z", NM, "float32"),
         ("ioa", 144, "bfloat16"), ("zero", 128, "bfloat16"), ("If", 128, "float32"), ("S1", 144, "bfloat16"), ("SH", 144, "bfloat16"),
         ("Rall", 2048, "bfloat16"), ("ioc", 256, "bfloat16"), ("mats", 128 * NMAT, "bfloat16"), ("BP", 256, "float16"),
-        ("ones", C, "bfloat16"), ("turn", C, "bfloat16"), ("own", 3 * C, "bfloat16"), ("mask", NW, "float32"), ("coli", 32, "int32"),
+        ("ones", C, "bfloat16"), ("turn", C, "bfloat16"), ("own", 3 * C, "bfloat16"), ("mask", NW, "float32"), ("ring", 48, "float32"), ("coli", 32, "int32"),
         ("colj", 8, "int32"), ("colf", 48, "float32"), ("colb", 8, "bfloat16"), ("t0s", NW, "int32"), ("y0s", NP, "bfloat16"),
         ("k0s", NP, "int32"), ("kz", NP, "bfloat16"), ("W", NP + 16, "float32"), ("W2", NP + 16, "float32"), ("ent", NW, "float32"), ("n32", 2 * NW, "float32"),
         ("cf", 24, "float16"), ("cint", 24, "int32"), ("Eq", NW, "bfloat16"),
@@ -193,10 +199,10 @@ def describe():
     io(GRP, [[16, 8], [0, 16]], 0, 0)
     TURN = A("turn", 0, C)
     io(TURN, [[0, C // 4], [1, 4]], 0, 0)
-    dma("G", A("coli", 0, 1), A("hw", 0, 1))
-    dma("G", A("coli", 8, 9), A("th", 0, 1))
-    dma("G", A("coli", 16, 19), A("dw", 0, 3))
-    io(A("mask", 0, NW), [[1, 16], [0, DW]], 0, 0)
+    dma("Y", A("coli", 0, 1), A("hw", 0, 1))
+    dma("Y", A("coli", 8, 9), A("th", 0, 1))
+    dma("Y", A("coli", 16, 19), A("dw", 0, 3))
+    if not RING: io(A("mask", 0, NW), [[1, 16], [0, DW]], 0, 0)
     def fill(o, v):
         if eng("fill") == "G" and v == int(v): io(o, [[0, count(o)]], int(v), 0)
         else: ms(o, v)
@@ -205,8 +211,19 @@ def describe():
     ts(A("colj", 1, 2), A("colj", 0, 1), 112, None, "bitwise_and")
     ts(A("colj", 2, 3), A("colj", 0, 1), 15, None, "bitwise_and")
     cp(A("colf", 0, 2), A("colj", 1, 3))
-    for a in range(16):
+    for a in range(0 if RING else 16):
         sel(blk("Rall", a), Iw(-1.0), [[16, 8], [0, 16]], 1.0, a, -1)
+    if RING:
+        RD = [A("ring", 8 * j, 8 * j + 8) for j in range(6)]
+        RD[0], RD[1] = A("ioa", 16, 24), A("ioa", 0, 8)
+        ts(RD[2], RD[0], KC, 16.0, "is_gt", "mult")
+        tt(RD[3], RD[2], RD[0], "subtract")
+        ts(RD[4], RD[1], KC, 0.0, "add", "is_ge")
+        tt(RD[5], RD[4], RD[1], "mult")
+        for d in range(8):
+            ts(blk("Rall", d), IOC, A("ring", 24 + d, 25 + d), None, "is_equal")
+            sel(blk("Rall", d), blk("Rall", d), [[1, 128]], -1.0, 0, -1)
+            ts(blk("Rall", 8 + d), IOC, A("ring", 40 + d, 41 + d), None, "is_equal")
     aff("col", H2, A("coli", 0, 1), 2.0)
     HHI = A("colf", 10, 11)
     if "V" in ENG["u"]:
@@ -218,27 +235,32 @@ def describe():
         aff("col", A("colf", 11, 12), A("coli", 0, 1))
         ts(A("SH", 0, 144), A("ioa", 0, 144), GP, A("colf", 11, 12), "is_equal", "mult")
     aff("col", THC, A("coli", 8, 9), 1.0, 0.5)
-    aff("col", A("colf", DN[1], DN[1] + 3), A("coli", 16, 19), -U, 17 * U)
+    if CANCEL:
+        aff("col", A("colf", DN[1], DN[1] + 1), A("coli", 16, 17), -1.0 / 8192, 25.0 / 32 + 17.0 / 8192 - 1.0 / 64)
+        aff("col", A("colf", DN[1] + 1, DN[1] + 3), A("coli", 17, 19), -1.0 / 8192, 25.0 / 32 + 17.0 / 8192)
+    else: aff("col", A("colf", DN[1], DN[1] + 3), A("coli", 16, 19), -U, 17 * U)
     ts(A("S1", 0, 144), A("ioa", 0, 144), GP, 1.0 / 512, "is_equal", "mult")
     OWNU, OWNI, OWND = A("own", 0, C), A("own", C, 2 * C), A("own", 2 * C, 3 * C)
     io(OWNU, [[0, D], [1, 16]], 0, 0)
     for lo, hi in WINS:
-        io(A("own", C + lo, C + hi), [[32, hi - lo]], 32, 0)
+        if eng("own") == "V": io(A("own", C + lo, C + hi), [[32, hi - lo]], 32, 0)
+        else: io(A("mask", lo, hi), [[512, (hi - lo) // 16], [16416, 16]], 32, 0)
     ts(OWNU, OWNU, KC, 2.0 ** 24, "not_equal", "mult")
-    tt(OWNI, OWNI, OWNU, "max")
-    ts(OWND, OWNU, -2.0, 2.0 ** 25, "mult", "add")
+    if eng("own") == "V": tt(OWNI, OWNI, OWNU, "max")
+    else: act(OWNI, A("mask", 0, C), "Abs", col(-16384.0, 0.0))
+    aff("own", OWND, OWNU, -2.0, 2.0 ** 25)
     IF = A("If", 0, 128)
     aff("set", IF, Iw(1.0))
-    act(A("mask", 0, NW), A("mask", 0, NW), "Relu", col(-4096.0, 2048.0), 4096.0)
+    if not RING: act(A("mask", 0, NW), A("mask", 0, NW), "Relu", col(-4096.0, 2048.0), 4096.0)
     ms(A("soff", 0, 48), 0)
     for c in range(NCH):
         for lo, hi in WINS:
             fill(A("VF%d" % c, 16 * lo + lo // 8, 16 * lo + lo // 8 + 16), B0 + 8 + 7680)
         n0 = A("i%d" % c, 0, C)
         ts(n0, A("t0s", c * C, (c + 1) * C), NM - 1, None, "bitwise_and")
-        aff("set", A("ru0%d" % c, 0, C), n0)
+        aff("ru", A("ru0%d" % c, 0, C), n0)
         ts(A("rb0%d" % c, 2 * C, 3 * C), A("t0s", c * C, (c + 1) * C), float(NM), None, "is_ge")
-        fill(A("rb0%d" % c, C, 2 * C), -1.0 / amp("hs", 0, c))
+        if not (CANCEL and DIRECT): fill(A("rb0%d" % c, C, 2 * C), -1.0 / amp("hs", 0, c))
     fill(A("W", NP, NP + 16), 0.0)
     ops[0] = body
     for j in range(NM // 512):
@@ -287,22 +309,30 @@ def describe():
                 if (t, c, j) in V_GATHER: cp(vf(lo, hi), src)
                 else: act(vf(lo, hi), src, "Identity")
             m, y1, cnt = 16 // R1, ps("y1")[0], ps("cnt")[0]
-            for h in range(R1):
+            fits = R1 * C <= 512
+            for h in range(R1 if fits else 0):
                 lin(A(y1, h, R1 * C, R1), [(1.0, x)])
             def row(k, lo, hi): return A(ca, (k % m) * R1 * C + R1 * lo + k // m, (k % m) * R1 * C + R1 * hi, R1)
             for lo, hi in zip((0,) + SUBS, SUBS):
+                yb_, off = (y1, 0) if R1 * hi <= 512 else (ps("mul")[0], 512 // R1)
+                for h in range(0 if fits else R1):
+                    if lo in (0, 512 // R1): lin(A(yb_, h, R1 * (min(C, off + 512 // R1) - off), R1), [(1.0, A(rb, off, min(C, off + 512 // R1)))])
                 for k in range(m):
-                    tt(A(ca, k * R1 * C + R1 * lo, k * R1 * C + R1 * hi), vf(lo, hi, k, m), A(y1, R1 * lo, R1 * hi), "add")
+                    tt(A(ca, k * R1 * C + R1 * lo, k * R1 * C + R1 * hi), vf(lo, hi, k, m), A(yb_, R1 * (lo - off), R1 * (hi - off)), "add")
+                if hi not in PSUBS: continue
+                lo = max([0] + [p for p in PSUBS if p < hi])
                 sums = [(blk("S1", k + m * h), row(k + m * h, lo, hi)) for k in range(m) for h in range(R1)]
-                lin(A(cnt, lo, hi), [(wide((512.0, -25.0 / 32)) if CANCEL else -25.0 / 32, A("ones", lo, hi))] * DIRECT + sums[:10]
-                    + [(-0.25, A(rb, 2 * C + lo, 2 * C + hi)), (-FP / 64, A(rb, C + lo, C + hi))] + sums[10:])
+                flags = t > 0 or not (CANCEL and DIRECT)
+                lin(A(cnt, lo, hi), [(wide((512.0, -25.0 / 32 + (0 if flags else 1.0 / 64))) if CANCEL else -25.0 / 32, A("ones", lo, hi))] * DIRECT + sums[:10]
+                    + [(-0.25, A(rb, 2 * C + lo, 2 * C + hi))] + ([(-FP / 64, A(rb, C + lo, C + hi))] if flags else []) + sums[10:])
             q_ = A("h" + cs_, C, 2 * C) if CANCEL else In(0)
             aff("q", q_, ps("cnt"), 1.0, 5.0 / 32 if DIRECT else -0.625)
-            if DIRECT: tt(cand, ps("cnt"), q_, "is_gt")
+            straight = DIRECT and eng("cand") == "V"
+            if straight: tt(cand, ps("cnt"), q_, "is_gt")
             if not DIRECT or NCH == 2: tt(vv, ps("cnt"), q_, "subtract")
-            if not DIRECT: sign("cand", cand, vv, 25.0 / 32, True)
-            lin(ps("c4"), [(1.0, TURN), (tri(-1.0, 16.0, 1) if DIRECT else tri(-0.5 * FC, 8.0 * FC, 1), cand)])
-            sign("c4", c4, ps("c4"), 15.5 if DIRECT else (0.5, 7.5), True)
+            if not straight: sign("cand", cand, vv, 0.0 if DIRECT else 25.0 / 32, True)
+            lin(ps("c4"), [(1.0, TURN), (tri(-1.0, 16.0, 1) if straight else tri(-0.5 * FC, 8.0 * FC, 1), cand)])
+            sign("c4", c4, ps("c4"), 15.5 if straight else (0.5, 7.5), True)
             lin(ps("na"), [(tri(0.5 * F4, 2.0 * F4, -1), c4)])
             sign("na", na, ps("na"), (0.5, -5.0), False)
             lin(ps("idx"), [(1.0, OWNI), (grp(col(F4, 2033.0 * F4), "BP"), c4), (grp(col(FN, 2033.0 * FN), "BP"), na)])
@@ -315,16 +345,24 @@ def describe():
             aff("e1", e1, eb, 1.0, -161.0, True)
             if eng("zx") == "S": act(zx, x, "Relu", 60.0, -60.0)
             else: ts(zx, x, 0.5, 60.0, "is_lt", "mult")
-            if FG == 1:
+            if eng("sg") != "V":
                 lin(ps("sg"), [(1.0, x), (-1.0, e1)])
-                act(sg, ps("sg"), "Sign", -0.5)
+                if FG == 1: act(sg, ps("sg"), "Sign", -0.5)
+                else: ts(sg, ps("sg"), 0.5, None, "is_gt")
             else: tt(sg, e1, A(y1, 0, R1 * C, R1), "is_lt")
             lin(ps("dl"), [(1.0, x), (-1.0 / 16, eb), (-15.0 / 16, e1)])
             act(xn, ps("dl"), "Abs", 10.0 - 15.0 / 16)
             lanes = DIRECT and not CANCEL
             CY2 = wide((-49408.0 if FG == 1 else -45312.0, 84.0 - 16 * lanes, -1.0 / 16), lanes)
-            lin(ps("y2"), [(CY2, ONE), (-256.0, x), (-256.0, zx), (432.0, eb), (-688.0, e1), (-4096.0 * FG, sg), (-256.0, xn)])
-            for k in range(16 - S_ROWS):
+            R2 = 1 if eng("r2x") == "-" else 2
+            Y2 = A(y1, 0, R2 * C, R2)
+            for h in range(2 if eng("r2x") == "P" else 1):
+                lin(A(y1, h, R2 * C, R2), [(CY2, ONE), (-256.0, x), (-256.0, zx), (432.0, eb), (-688.0, e1), (-4096.0 * FG, sg), (-256.0, xn)])
+            if eng("r2x") == "S": act(A(y1, 1, 2 * C, 2), Y2, "Identity")
+            for k in range(8 if R2 == 2 else 0):
+                if CANCEL and k == YB_AT // 2: aff("yb", yb, Y2, -1.0 / 512, (B0 - 16 + 63.0 / 16) / 512 - 80)
+                tt(A(cb, 2 * k * C, 2 * (k + 1) * C), A(y1, 0, 2 * C), A(ca, (k % m) * R1 * C + k // m, (k % m + 1) * R1 * C, R1 // 2), "subtract")
+            for k in range(16 - S_ROWS if R2 == 1 else 0):
                 if CANCEL and k == YB_AT: aff("yb", yb, ps("y2"), -1.0 / 512, (B0 - 16 + 63.0 / 16) / 512 - 80)
                 tt(A(cb, k * C, (k + 1) * C), ps("y2"), row(k, 0, C), "subtract")
             for k in range(16 - S_ROWS, 16, 2):
@@ -333,12 +371,18 @@ def describe():
                     lin(A(pw, h * C, (h + 1) * C), [(-1.0, row(k + h, 0, C)), (-512.0, yb)])
                 act(A(cb, k * C, (k + 2) * C), A(pw, 0, 2 * C), "Identity", B0 - 16 + 63.0 / 16 - 80 * 512)
             sums = [(blk("S1", k), A(cb, k * C, (k + 1) * C)) for k in sorted(range(16), key=lambda k: k if k < 16 - S_ROWS else k - 3.5)]
-            lin(ps("sum"), [(1.0, vv), (FP / 64, hp)] + [(1.0, q_)] * CANCEL + sums[:YB_AT + 3] + [(grp(1.0), yb)] * CANCEL + sums[YB_AT + 3:])
+            if R2 == 2: sums = [(blk("S1", k + 8 * h), A(cb, 2 * k * C + h, 2 * (k + 1) * C, 2)) for k in range(8) for h in range(2)]
+            lin(ps("sum"), [(1.0, vv)] + ([(FP / 64, hp)] if flags else []) + [(1.0, q_)] * CANCEL + sums[:YB_AT + 3] + [(grp(1.0), yb)] * CANCEL + sums[YB_AT + 3:])
             cint = A("cint", D * c, D * c + D)
             if eng("u") == "P":
                 pu = A(ps("u")[0], 2 * C, 2 * C + D)
                 lin(pu, [(blk("SH", a), A(sb, a, C, 16)) for a in range(16)])
                 aff("ti", A("i" + cs_, C, C + D), pu, 241.0)
+                ts(cint, A("i" + cs_, C, C + D), 6, NP - 1, "arith_shift_right", "bitwise_and")
+            elif eng("u") == "T":
+                lin(ps("u"), [(1.0, OWNU), (grp(H2), xn)])
+                scan(Fl(3), OWND, ps("u"))
+                aff("ti", A("i" + cs_, C, C + D), pick(Fl(3)), 120.5)
                 ts(cint, A("i" + cs_, C, C + D), 6, NP - 1, "arith_shift_right", "bitwise_and")
             else:
                 lin(ps("u"), [(1.0, OWNU), (grp(HHI), xn), (grp(HLO), xn)])
@@ -346,25 +390,36 @@ def describe():
                 ts(cint, pick(In(1)), 6, NP - 1, "arith_shift_right", "bitwise_and")
             aff("tu", A(tu, 16, 16 + D), cint)
             each = LAST > 1 and t == ST - 1
-            if c == NCH - 1 or each:
+            def twins():
+                if c < NCH - 1 and not each: return
                 pq = "ps%d" % bank[DBANK]
                 b0, nb = (D * c, D) if each else (0, DW)
                 CF = A("cf", b0, b0 + nb)
                 aff("cf", CF, A("cint", b0, b0 + nb))
+                if RING:
+                    for d in range(8):
+                        lin(A(pq, nb * d, nb * d + nb), [(blk("Rall", d), CF)])
+                    ts(A("Eq", 8 * b0, 8 * (b0 + nb)), A(pq, 0, 8 * nb), 0.0, None, "is_equal")
+                    lin(A(pq, 424, 424 + nb), [(2.0 ** -10, CF)] + [(blk("Rall", 8 + d), A("Eq", 8 * b0 + nb * d, 8 * b0 + nb * d + nb)) for d in range(8)])
+                    ts(A("soff", 2 * b0, 2 * (b0 + nb), 2), A(pq, 424, 424 + nb), 2.0 ** 10, col(1.0, float(NP)), "mult", "min")
+                    return
                 for a in range(16):
                     lin(A(pq, nb * a, nb * a + nb), [(blk("Rall", a), CF)])
                 tt(A("Eq", 16 * b0, 16 * (b0 + nb)), A(pq, 0, 16 * nb), A("mask", 0, NW, DW // nb), "is_equal")
                 lin(A(pq, 424, 424 + nb), [(2.0 ** -19, CF)] + [(blk("S1", a), A("Eq", 16 * b0 + nb * a, 16 * b0 + nb * a + nb)) for a in range(16)])
                 ts(A("soff", 2 * b0, 2 * (b0 + nb), 2), A(pq, 424, 424 + nb), 2.0 ** 19, col(1.0, float(NP)), "mult", "min")
+            if t not in DLATE: twins()
             lin(ps("rr"), [(grp(H2), xn)])
             aff("rr", rr, ps("rr"), 1.0 / 2048, 128.5 + 1.0 / 2048)
-            lin(ps("mul"), [(wide((129.0 * 2048, 1.0)), ONE), (grp(H2), xn), (-2048.0, rr)])
+            lin(ps("mul"), ([(wide((129.0 * 2048, 1.0)), ONE)] if eng("cm") == "P" else []) + [(grp(H2), xn), (-2048.0, rr)])
+            if eng("cm") == "S": act(ps("mul"), ps("mul"), "Identity", 129.0 * 2048 + 1)
             tt(In(2), n16, ps("mul"), "mult")
             ts(In(3), In(2), 5, NM - 1, "arith_shift_right", "bitwise_and")
             aff("a1", ps("a1"), n16, 1.0, col(37.0, 0.0))
             tt(Fl(1), In(3), ps("a1"), "add")
+            if eng("yc") == "D": act(yc, IND(A("W", 0, NP + 16), A(tu, 16, 16 + D)), "Identity", YB, -1.0 / 65536)
             aff("wg", Fl(0), IND(A("W", 0, NP + 16), A(tu, 16, 16 + D)))
-            aff("yc", yc, Fl(0), -1.0 / 65536, YB)
+            if eng("yc") != "D": aff("yc", yc, Fl(0), -1.0 / 65536, YB)
             lin(ps("ad"), [(1.0, xn), (1.0, yc)])
             act(ad, ps("ad"), "Abs", 129.0)
             lin(ps("hs"), [(grp(1.0), ad)])
@@ -378,6 +433,7 @@ def describe():
                 act(Fl(3), n16, "Identity", -8192.0)
                 tt(hv, Fl(3), K3, "is_equal")
             else: sign("hv", hv, K3, -0.5, False)
+            if t in DLATE: twins()
             lin(ps("hy"), [(-1.0, xn), (-1.0, yc), (16.0 * FH, hs)])
             aff("hy", hy, ps("hy"), 1.0, -129.0, True)
             if last:
@@ -387,13 +443,13 @@ def describe():
                 tt(Fl(3), n16, ps("hy"), "max")
             if CANCEL:
                 if APART: ts(ap_, ps("sum"), 1.5 * 2.0 ** 16 + 25.0 / 32, 1.5 * 2.0 ** 16, "add", "subtract")
-                aff("r2", r2, ps("sum"), 1.0, 25.0 / 32)
+                aff("r2", r2, ps("sum"), 1.0, A("colf", DN[1] + t, DN[1] + t + 1))
             else:
                 aff("mg", In(0), ps("sum"))
                 tt(r2, ps("sum"), In(0), "subtract")
             if not (CANCEL and APART): ts(ap_, r2, 1.5 * 2.0 ** 16, 1.5 * 2.0 ** 16, "add", "subtract")
             Q = ps("wake")
-            lin(Q, [(dg(t), ONE), (16 * U * FN, na), (8192 * U, r2), (-8064 * U, ap_)][::-1 if CANCEL and APART else 1][::-1 if CANCEL and APART else 1])
+            lin(Q, ([] if CANCEL else [(dg(t), ONE)]) + [(16 * U * FN, na), (8192 * U, r2), (-8064 * U, ap_)])
             if last: ts(Fl(0), Q, float(NM), None, "min")
             n32 = A("n32", t % 2 * NW + c * C, t % 2 * NW + (c + 1) * C)
             if eng("ent") == "S" and not last or eng("Q") == "S": sel(n32, n16, [[0, C]], 0.0, 1, 0)
@@ -429,7 +485,7 @@ def describe():
             o, e = IND(A(WT, 0, NP + 16), A("soff", 2 * b, 2 * b + 1)), A("ent", 16 * b, 16 * b + 16)
             if eng("ent", t, b // D) == "V": cp(o, e)
             else: tt(o, e, A("n32", t % 2 * NW + 16 * b, t % 2 * NW + 16 * b + 16), "add")
-    step = NP if LAST else 256
+    step = OSTEP
     for j, lo in enumerate(range(0, NP, step)):
         hi = lo + step
         act(A("oy1", lo, hi), A(WT, lo, hi), "Identity", YB, -1.0 / 65536)
@@ -461,7 +517,7 @@ def regions(op):
     return [r for r in rd if r[0] not in DRAM], [r for r in wr if r[0] not in DRAM]
 
 
-SC = {"gather": 1.55, "scatter": 2.9, "call": 24, "act": 80, "psum": 25, "pe": 0.41, "mm": 19, "lat": 15, "V": 70, "S": 35, "P": 40, "same": 70, "cross": 45, "pool": 200, "bw": 290.0, "dma": 1350, "gdma": 300, "issue": 450, "first": 1800, "link": 1300, "lbw": 27.0, "row": 25, "cyc": 0.85}
+SC = {"gather": 1.65, "scatter": 3.0, "call": 24, "act": 80, "psum": 25, "pe": 0.435, "mm": 19, "lat": 15, "V": 70, "S": 35, "P": 40, "same": 70, "cross": 45, "pool": 220, "bw": 290.0, "dma": 1350, "gdma": 300, "issue": 450, "first": 1800, "link": 1300, "lbw": 27.0, "row": 25, "cyc": 0.86}
 
 
 def cost(op, sc=SC):
@@ -520,15 +576,23 @@ def schedule(q, dur, tail, prio, pre, suc, window=30):
     left = [len(p) for p in pre]
     ready = {k: [i for i in range(n) if q[i] == k and not left[i]] for k in "VSPGYR"}
     at, start, free, order, end = [0.0] * n, [0.0] * n, dict.fromkeys("VSPGYR", 0.0), [], 0.0
+    soon = {k: 0.0 if ready[k] else 1e18 for k in ready}
     for _ in range(n):
-        first, k = min((max(free[k], min([at[i] for i in L])), k) for k, L in ready.items() if L)
-        i = max((prio[i], -i) for i in ready[k] if at[i] <= first + window)[1] * -1
-        ready[k].remove(i)
-        start[i] = max(at[i], free[k]); free[k] = start[i] + dur[i]; end = max(end, free[k] + tail[i])
+        k = min(soon, key=soon.get)
+        L, lim, i, top = ready[k], soon[k] + window, -1, -1e18
+        for j in L:
+            if at[j] <= lim and prio[j] > top: i, top = j, prio[j]
+        L.remove(i)
+        start[i] = max(at[i], free[k]); f = free[k] = start[i] + dur[i]
+        if f + tail[i] > end: end = f + tail[i]
         order.append(i)
         for u, gap in suc[i]:
-            at[u] = max(at[u], free[k] + gap); left[u] -= 1
-            if not left[u]: ready[q[u]].append(u)
+            if f + gap > at[u]: at[u] = f + gap
+            left[u] -= 1
+            if not left[u]:
+                ready[q[u]].append(u)
+                soon[q[u]] = min(soon[q[u]], max(at[u], free[q[u]]))
+        soon[k] = max(f, min([at[j] for j in L])) if L else 1e18
     return end, start, order
 
 
@@ -556,7 +620,28 @@ def plan(sc=SC):
                 if best is None or got[0] < best[0]: best = got
                 back = schedule(q, dur, [0.0] * n, [got[1][i] + dur[i] for i in range(n)], suc, pre)[1]
                 prio = [back[i] + dur[i] for i in range(n)]
-    cur, seed = best, [12345]
+    others = []
+    for x, g_, s_, far, pe, weight in SHADES:
+        so = dict(sc, gather=g_, scatter=s_, cyc=x, pe=pe)
+        so.update({k: sc[k] * far for k in ("link", "issue", "first", "row")})
+        cs = [cost(op, so) for op in ops]
+        others.append(([a for a, b in cs], [b - a for a, b in cs], weight,
+                       [[(j, cs[j][1] + so["same" if q[j] == q[i] else "cross"] if j in hard[i] else cs[j][0]) for j, gap in pre[i]] for i in range(n)]))
+
+    def worth(got):
+        total = got[0]
+        for d, tl, weight, pr in others:
+            st, free, end = [0.0] * n, dict.fromkeys("VSPGYR", 0.0), 0.0
+            for i in got[2]:
+                s = free[q[i]]
+                for j, gap in pr[i]:
+                    if st[j] + gap > s: s = st[j] + gap
+                st[i] = s; s += d[i]; free[q[i]] = s
+                if s + tl[i] > end: end = s + tl[i]
+            total += weight * end
+        return total
+    cur, seed = best, [SEED]
+    wc = wb = worth(best)
 
     def rnd():
         seed[0] = (seed[0] * 1103515245 + 12345) % 2147483648
@@ -566,8 +651,10 @@ def plan(sc=SC):
         prio = [cur[1][i] + dur[i] + ((2 * rnd() - 1) * a if lo <= cur[1][i] <= lo + w else 0) for i in range(n)]
         back = schedule(q, dur, [0.0] * n, prio, suc, pre)[1]
         got = schedule(q, dur, tail, [back[i] + dur[i] for i in range(n)], pre, suc)
-        if got[0] < cur[0] + 150: cur = got
-        if got[0] < best[0]: best = got
+        if got[0] > best[0] + 2500: continue
+        wg = worth(got)
+        if wg < wc + 150 * (1 + len(others)): cur, wc = got, wg
+        if wg < wb: best, wb = got, wg
     needed = set()
     for i in range(n): needed |= hard[i]
     return ops, hard, best[2], needed, best[1], soft, best[0]
@@ -598,6 +685,7 @@ def rank_program(g, core, T, topo):
     def ap(a):
         if not isinstance(a, tuple): return a
         if a[0] == "@": return ap(a[1]).indirect(ap(a[2]))
+        if a[0] in ("hw", "th", "dw"): return T[a[0]][:]
         return T[a[0]][:, a[1]:a[2]] if a[3] == 1 else T[a[0]][:, a[1]:a[2]:a[3]]
 
     mark, total, seen, ndma = {}, {}, {}, [0]

from concourse.bass import DstId, RemoteDMATransfer
from concourse.mybir import AluOpType, ActivationFunctionType

NM, NP, NW, ST, SH, NR = 8192, 512, 384, 3, 3, 8
C = 192
NCH, D = NW // C, C // 16
R1 = 4
DW = NW // 16
HA = 128
WINS = [(_w, min(C, _w + HA)) for _w in range(0, C, HA)]
CUTS = (64, 96, 128, 192)
SUBS = (64, 128, 192)
DIRECT = 1
S_T = (2, 4, 6, 7)
SPANS = []
LOADS = (512, 1024, 2048, 3072, 4096, 5120, 6144, 7168, 7680, 8192)
V_EVAC = (0, 2, 4, 6, 8, 10, 12, 13, 15)
V_GATHER = ((0, 0, 1), (0, 0, 2), (1, 0, 1), (2, 0, 1))
DIAG = "SG"
ENG = {"q": "VS", "cand": "V", "c4": "VS", "na": "VS", "ix": "S", "eb": "S", "e1": "S", "zx": "S", "sg": "S", "tu": "G", "cf": "G", "rr": "S", "a1": "S", "wg": "S", "yc": "S", "hs": "S", "k3": "P", "hv": "S", "hy": "S", "mg": "S", "u16": "S", "ent": "S", "set": "S", "col": "S", "wide": "G", "fill": "G", "grp": "S", "u": "T", "ti": "S", "Q": "V", "yb": "S", "r2": "S", "ru": "S", "cm": "S", "r2x": "-", "own": "S"}
CANCEL = 1
YB_AT = 6
S_ROWS = 0
FIRM = 1
LAST = 1
APART = 0
PSUBS = (128, 192)
RING = 1
DLATE = (0, 1)
OSTEP = 256
DBANK = "w"
B0 = 24592.0
U = 32768.0
XA, XH, KO = 25600.0, 28672.0, 6144.0
NMAT = 56
LEADS = (0, 3000)
LATES = (0, 4000)
ROUNDS = 1000
SEED = 4
SHADES = ((1.245, 2.08, 5.0, 1.4, 0.45, 0.5), (1.1, 1.3, 3.5, 1.0, 0.41, 1.0), (0.9, 1.5, 3.0, 1.0, 0.56, 0.7))
SENDS = ([("b", 0, C)], [("u", 0, C)], [("b", C, 3 * C)])
SLOTS = {"y1": ("y", 0), "cnt": ("a", 0), "c4": ("z", 0), "na": ("z", C), "idx": ("w", C), "dl": ("z", C), "sg": ("w", 0), "y2": ("y", 0), "sum": ("a", 0), "u": ("z", 0), "rr": ("w", C), "mul": ("w", 0), "a1": ("w", C), "ad": ("z", C), "hs": ("z", 0), "k3": ("w", 0), "hy": ("z", C), "wake": ("y", 0), "yt": ("y", C), "ent": ("z", 0)}
if NCH > 2:
    SLOTS.update({"c4": ("a", C), "na": ("a", 2 * C), "idx": ("a", 3 * C), "dl": ("a", C), "sg": ("a", 2 * C), "ent": ("a", C)})

SCRATCH = {}
for _n, _w, _d in [
        ("F", NM, "bfloat16"), ("Tt", NM, "bfloat16"), ("Mt", NM, "float16"), ("Z", NM, "float32"),
        ("ioa", 144, "bfloat16"), ("zero", 128, "bfloat16"), ("If", 128, "float32"), ("S1", 144, "bfloat16"), ("SH", 144, "bfloat16"),
        ("Rall", 2048, "bfloat16"), ("ioc", 256, "bfloat16"), ("mats", 128 * NMAT, "bfloat16"), ("BP", 256, "float16"),
        ("ones", C, "bfloat16"), ("turn", C, "bfloat16"), ("own", 3 * C, "bfloat16"), ("mask", NW, "float32"), ("ring", 48, "float32"), ("coli", 32, "int32"),
        ("colj", 8, "int32"), ("colf", 48, "float32"), ("colb", 8, "bfloat16"), ("t0s", NW, "int32"), ("y0s", NP, "bfloat16"),
        ("k0s", NP, "int32"), ("kz", NP, "bfloat16"), ("W", NP + 16, "float32"), ("W2", NP + 16, "float32"), ("ent", NW, "float32"), ("n32", 2 * NW, "float32"),
        ("cf", 24, "float16"), ("cint", 24, "int32"), ("Eq", NW, "bfloat16"),
        ("soff", 48, "uint16"), ("oyt", NW, "float32"), ("oy1", NP, "bfloat16"), ("oy2", NP + 16, "bfloat16"), ("oyk", NP + 16, "float32")]:
    SCRATCH[_n] = ("sbuf", [128, _w], _d)
for _c in range(NCH):
    for _n, _w, _d in [("VF", 16 * C + 32, "float32"), ("ca", 16 * C, "float16"), ("cb", 16 * C, "float16"), ("b", 16 * C, "bfloat16"),
                       ("h", 2 * C, "float16"), ("f", 4 * C, "float32"), ("i", 6 * C, "int32"), ("tu", 32, "uint16")]:
        SCRATCH[_n + str(_c)] = ("sbuf", [128, _w], _d)
    for _t in range(ST):
        for _p in "rs":
            SCRATCH["%sb%d%d" % (_p, _t, _c)] = ("sbuf", [128, 3 * C], "bfloat16")
            SCRATCH["%su%d%d" % (_p, _t, _c)] = ("sbuf", [128, C], "uint16")
for _k in range(8):
    SCRATCH["ps%d" % _k] = ("psum", [128, 512], "float32")
DRAM = ("fx", "y0", "k0", "x0", "t0", "dw", "hw", "th", "yx", "yt", "yy", "yk")
NDMA = len(LOADS) + 10 + 3 * NCH
SEMAPHORES = ["V", "S", "P", "G", "sent"] + ["d%d" % _k for _k in range(NDMA)] + ["a%d" % _k for _k in range(10 * NCH)]


def A(name, lo, hi, step=1):
    return (name, lo, hi, step)


def IND(win, off):
    return ("@", win, off)


def count(ap):
    if ap[0] == "@":
        return 16 * (ap[2][2] - ap[2][1])
    return (ap[2] - ap[1] + ap[3] - 1) // ap[3]


def narrow(ap):
    return ap[0] in SCRATCH and SCRATCH[ap[0]][2] in ("bfloat16", "float16", "uint16")


def describe():
    head, body = [], []
    ops, now, made = [head], [0, 0], {}

    def put(*op): ops[0].append(op)
    def tt(o, a, b, op): put("V", "tt", o, [a, b], op)
    def ts(o, a, s1, s2, op0, op1=None): put("V", "ts", o, [a, s1, s2], (op0, op1))
    def scan(o, a, b): put("V", "scan", o, [a, b], None)
    def cp(o, a): put("V", "cp", o, [a], None)
    def ms(o, v, p=None): put("V", "ms", o, [], (v, p))
    def act(o, a, f, bias=0.0, scale=1.0): put("S", "act", o, [a, bias, scale], f)
    def io(o, pat, base, cm): put("G", "iota", o, [], (pat, base, cm))
    def sel(o, a, pat, fill, base, cm, op="not_equal"): put("G", "sel", o, [a], (pat, base, cm, fill, op))
    def dma(q, o, a): put(q, "dma", o, [a], None)
    def blk(n, a):
        return A(n, 15 - a, 143 - a) if n in ("S1", "SH") else A(n, 128 * a, 128 * a + 128)
    def eng(name, t=None, c=None):
        e, (t, c) = ENG[name], now if t is None else (t, c)
        return e[0 if len(e) == 1 else c if len(e) == NCH else t * NCH + c]
    def amp(name, t=None, c=None): return 1.0 if eng(name, t, c) == "S" else 2.0

    def aff(name, o, a, scale=1.0, bias=0.0, relu=False):
        e = eng(name)
        if e == "G": sel(o, a, [[0, count(o)]], 0.0, 1, 0)
        elif e == "S": act(o, a, "Relu" if relu else "Identity", bias, scale)
        elif relu: ts(o, a, bias, 0.0, "add", "max")
        elif scale == 1.0 and bias == 0.0: cp(o, a)
        elif scale == 1.0: ts(o, a, bias, None, "add")
        elif bias == 0.0: ts(o, a, scale, None, "mult")
        else: ts(o, a, scale, bias, "mult", "add")

    def sign(name, o, a, thr, above):
        if eng(name) == "S":
            s = -1.0 if above else 1.0
            act(o, a, "Sign", s * thr if isinstance(thr, float) else thr if thr[0] == "colf" else col(s * thr[0], s * thr[1]), -s)
        else: ts(o, a, thr if isinstance(thr, float) or thr[0] == "colf" else col(*thr), 0.5, "is_gt" if above else "is_lt", "subtract")

    IOC, GRP, ZERO, ONE = A("ioc", 0, 128), A("ioc", 128, 256), A("zero", 0, 128), A("ones", 0, C)
    GP, KC, H2, H241, HLO, THC, K7, DN = [A("colf", j, j + 1) for j in range(8)]

    def once(key, make):
        if key not in made:
            back, ops[0] = ops[0], head
            made[key] = make(); ops[0] = back
        return made[key]

    def room(name, width, first=0):
        made[name] = made.get(name, first) + width
        return A(name, made[name] - width, made[name])

    def col(a, b):
        def make():
            o = room("colf", 1, 12); aff("col", o, KC, a, b); return o
        return once(("col", a, b), make)

    def Iw(w):
        def make():
            o = room("mats", 128); e = DIAG[o[1] // 128 % len(DIAG)] if w != 1.0 else "V"
            if e == "V": ts(o, IOC, 0.0, w, "is_equal", "mult")
            elif e == "S": act(o, Iw(1.0), "Identity", 0.0, w)
            else: sel(o, ZERO, [[1, 128]], w, 0, -1)
            return o
        return once(("I", w), make)

    def grp(w, name="mats"):
        def make():
            o = room(name, 128)
            if eng("grp") == "V" or w == 1.0: ts(o, GRP, GP, w, "is_equal", "mult")
            else: act(o, grp(1.0), "Identity", 0.0, w)
            return o
        return once(("grp", w), make)

    def tri(off, diag, s):
        def make():
            o = room("mats", 128)
            sel(o, grp(off), [[s, 128]], 0.0, 0, -s, "is_gt"); sel(o, o, [[1, 128]], diag, 0, -1); return o
        return once(("tri", off, diag, s), make)

    def wide(parts, lanes=False):
        def make():
            o = room("mats", 128)
            if lanes:
                ts(K7, KC, 7.0, 16.0, "is_ge", "mult"); ts(o, IOC, 0.0, K7, "is_equal", "mult")
            elif eng("wide") == "V": ms(o, 0.0)
            for j, v in enumerate(parts):
                if eng("wide") == "V": ms(o, v, 32 * j)
                else: sel(o, o if j or lanes else ZERO, [[0, 128]], v, -j, 1)
            return o
        return once(("wide", parts), make)

    def dg(t):
        def make():
            o = room("mats", 128); aff("set", o, Iw(1.0), A("colf", DN[1] + t, DN[1] + t + 1)); return o
        return once(("dg", t), make)

    def lin(o, terms):
        for j, (l, r) in enumerate(terms):
            put("P", "mm", o, [Iw(l) if isinstance(l, float) else l, r], (j == 0, j == len(terms) - 1))

    dma("Y", A("t0s", 0, NW), A("t0", 0, NW))
    for lo, hi in zip((0,) + LOADS, LOADS):
        dma("Y", A("F", lo, hi), A("fx", lo, hi))
    for c in range(NCH):
        dma("Y", A("rb0%d" % c, 0, C), A("x0", c * C, (c + 1) * C))
    dma("Y", A("y0s", 0, NP), A("y0", 0, NP))
    dma("Y", A("k0s", 0, NP), A("k0", 0, NP))
    io(IOC, [[1, 128]], 0, -1)
    io(A("colj", 0, 1), [[1, 1]], 0, 1)
    io(A("ioa", 0, 144), [[1, 144]], -15, 0)
    io(GRP, [[16, 8], [0, 16]], 0, 0)
    TURN = A("turn", 0, C)
    io(TURN, [[0, C // 4], [1, 4]], 0, 0)
    dma("Y", A("coli", 0, 1), A("hw", 0, 1))
    dma("Y", A("coli", 8, 9), A("th", 0, 1))
    dma("Y", A("coli", 16, 19), A("dw", 0, 3))
    if not RING: io(A("mask", 0, NW), [[1, 16], [0, DW]], 0, 0)
    def fill(o, v):
        if eng("fill") == "G" and v == int(v): io(o, [[0, count(o)]], int(v), 0)
        else: ms(o, v)
    if "G" in DIAG + ENG["wide"]: fill(ZERO, 0.0)
    fill(ONE, 1.0)
    ts(A("colj", 1, 2), A("colj", 0, 1), 112, None, "bitwise_and")
    ts(A("colj", 2, 3), A("colj", 0, 1), 15, None, "bitwise_and")
    cp(A("colf", 0, 2), A("colj", 1, 3))
    for a in range(0 if RING else 16):
        sel(blk("Rall", a), Iw(-1.0), [[16, 8], [0, 16]], 1.0, a, -1)
    if RING:
        RD = [A("ring", 8 * j, 8 * j + 8) for j in range(6)]
        RD[0], RD[1] = A("ioa", 16, 24), A("ioa", 0, 8)
        ts(RD[2], RD[0], KC, 16.0, "is_gt", "mult")
        tt(RD[3], RD[2], RD[0], "subtract")
        ts(RD[4], RD[1], KC, 0.0, "add", "is_ge")
        tt(RD[5], RD[4], RD[1], "mult")
        for d in range(8):
            ts(blk("Rall", d), IOC, A("ring", 24 + d, 25 + d), None, "is_equal")
            sel(blk("Rall", d), blk("Rall", d), [[1, 128]], -1.0, 0, -1)
            ts(blk("Rall", 8 + d), IOC, A("ring", 40 + d, 41 + d), None, "is_equal")
    aff("col", H2, A("coli", 0, 1), 2.0)
    HHI = A("colf", 10, 11)
    if "V" in ENG["u"]:
        aff("col", H241, A("coli", 0, 1), 241.0)
        aff("col", A("colb", 0, 1), H241)
        aff("col", HHI, A("colb", 0, 1))
        tt(HLO, H241, HHI, "subtract")
    if "P" in ENG["u"]:
        aff("col", A("colf", 11, 12), A("coli", 0, 1))
        ts(A("SH", 0, 144), A("ioa", 0, 144), GP, A("colf", 11, 12), "is_equal", "mult")
    aff("col", THC, A("coli", 8, 9), 1.0, 0.5)
    if CANCEL:
        aff("col", A("colf", DN[1], DN[1] + 1), A("coli", 16, 17), -1.0 / 8192, 25.0 / 32 + 17.0 / 8192 - 1.0 / 64)
        aff("col", A("colf", DN[1] + 1, DN[1] + 3), A("coli", 17, 19), -1.0 / 8192, 25.0 / 32 + 17.0 / 8192)
    else: aff("col", A("colf", DN[1], DN[1] + 3), A("coli", 16, 19), -U, 17 * U)
    ts(A("S1", 0, 144), A("ioa", 0, 144), GP, 1.0 / 512, "is_equal", "mult")
    OWNU, OWNI, OWND = A("own", 0, C), A("own", C, 2 * C), A("own", 2 * C, 3 * C)
    io(OWNU, [[0, D], [1, 16]], 0, 0)
    for lo, hi in WINS:
        if eng("own") == "V": io(A("own", C + lo, C + hi), [[32, hi - lo]], 32, 0)
        else: io(A("mask", lo, hi), [[512, (hi - lo) // 16], [16416, 16]], 32, 0)
    ts(OWNU, OWNU, KC, 2.0 ** 24, "not_equal", "mult")
    if eng("own") == "V": tt(OWNI, OWNI, OWNU, "max")
    else: act(OWNI, A("mask", 0, C), "Abs", col(-16384.0, 0.0))
    aff("own", OWND, OWNU, -2.0, 2.0 ** 25)
    IF = A("If", 0, 128)
    aff("set", IF, Iw(1.0))
    if not RING: act(A("mask", 0, NW), A("mask", 0, NW), "Relu", col(-4096.0, 2048.0), 4096.0)
    ms(A("soff", 0, 48), 0)
    for c in range(NCH):
        for lo, hi in WINS:
            fill(A("VF%d" % c, 16 * lo + lo // 8, 16 * lo + lo // 8 + 16), B0 + 8 + 7680)
        n0 = A("i%d" % c, 0, C)
        ts(n0, A("t0s", c * C, (c + 1) * C), NM - 1, None, "bitwise_and")
        aff("ru", A("ru0%d" % c, 0, C), n0)
        ts(A("rb0%d" % c, 2 * C, 3 * C), A("t0s", c * C, (c + 1) * C), float(NM), None, "is_ge")
        if not (CANCEL and DIRECT): fill(A("rb0%d" % c, C, 2 * C), -1.0 / amp("hs", 0, c))
    fill(A("W", NP, NP + 16), 0.0)
    ops[0] = body
    for j in range(NM // 512):
        lo, hi = 512 * j, 512 * j + 512
        if lo in (0,) + LOADS:
            end = min(b for b in LOADS if b > lo)
            if LOADS.index(end) in S_T: act(A("Tt", lo, end), A("F", lo, end), "Identity", 2152.5)
            else: ts(A("Tt", lo, end), A("F", lo, end), 2152.5, None, "add")
            ts(A("Mt", lo, end), A("F", lo, end), 16.0, 763.0 / 64, "is_lt", "add")
        pb = A("ps%d" % (j % 8), 0, 512)
        lin(pb, [(-1.0, A("F", lo, hi))] * (j not in V_EVAC) + [(-31.0, A("Tt", lo, hi)), (7680.0, A("Mt", lo, hi))])
        if j in V_EVAC: tt(A("Z", lo, hi), pb, A("F", lo, hi), "subtract")
        else: act(A("Z", lo, hi), pb, "Identity")
    act(A("kz", 0, NP), A("k0s", 0, NP), "Relu", -XH * (NM - 1), XH)
    for lo in range(0, NP, C):
        hi = min(NP, lo + C)
        lin(A("ps3", lo, hi), [(wide((129.0 * 65536, KO)), A("ones", 0, hi - lo)), (65536.0, A("y0s", lo, hi)), (1.0, A("kz", lo, hi))])
    tt(A("W", 0, NP), A("k0s", 0, NP), A("ps3", 0, NP), "add")
    YB = 73.0 / 128

    arr, spans = [0], []
    for t in range(ST):
        for c in range(NCH):
            now[:] = [t, c]
            cs_, first = str(c), len(body)
            def B(j): return A("b" + cs_, j * C, (j + 1) * C)
            def Fl(j): return A("f" + cs_, j * C, (j + 1) * C)
            def In(j): return A("i" + cs_, j * C, (j + 1) * C)
            if NCH == 2: bank = {"y": 4 * c, "a": 4 * c + 1, "z": 4 * c + 2, "w": 4 * c + 3, "d": 2}
            else: bank = {"y": 2 * c, "a": 2 * c + 1, "z": 6, "w": 7, "d": 7}
            def ps(name, n=C):
                k, lo = SLOTS[name]
                return A("ps%d" % bank[k], lo, lo + n)
            def pick(o): return A(o[0], o[1] + 15, o[2], 16)
            rb, sb = "rb%d%d" % (t, c), "sb%d%d" % (t, c)
            x, hp, s = A(rb, 0, C), A(rb, C, 2 * C), A(rb, 2 * C, 3 * C)
            xn, hs, s6 = A(sb, 0, C), A(sb, C, 2 * C), A(sb, 2 * C, 3 * C)
            n16, nn16, nn32 = A("ru%d%d" % (t, c), 0, C), A("su%d%d" % (t, c), 0, C), In(5)
            VF, ca, cb, tu = "VF" + cs_, "ca" + cs_, "cb" + cs_, "tu" + cs_
            vv, cand, c4, na, eb, e1, zx, sg, rr, yc, ad, hv, hy, ap_, yb, aw = [B(j) for j in range(16)]
            r2 = A("h" + cs_, 0, C)
            FC, F4, FN, FG, FH, FV, FP = [amp(n) for n in ("cand", "c4", "na", "sg", "hs", "hv")] + [amp("hs", max(t - 1, 0), c)]
            def vf(lo, hi, k=0, step=1): return A(VF, 16 * (lo + 1 + lo // HA) + k, 16 * (hi + 1 + lo // HA), step)
            for j, (lo, hi) in enumerate(zip((0,) + CUTS, CUTS)):
                src = IND(A("Z", 0, NM), A(n16[0], lo, hi))
                if (t, c, j) in V_GATHER: cp(vf(lo, hi), src)
                else: act(vf(lo, hi), src, "Identity")
            m, y1, cnt = 16 // R1, ps("y1")[0], ps("cnt")[0]
            fits = R1 * C <= 512
            for h in range(R1 if fits else 0):
                lin(A(y1, h, R1 * C, R1), [(1.0, x)])
            def row(k, lo, hi): return A(ca, (k % m) * R1 * C + R1 * lo + k // m, (k % m) * R1 * C + R1 * hi, R1)
            for lo, hi in zip((0,) + SUBS, SUBS):
                yb_, off = (y1, 0) if R1 * hi <= 512 else (ps("mul")[0], 512 // R1)
                for h in range(0 if fits else R1):
                    if lo in (0, 512 // R1): lin(A(yb_, h, R1 * (min(C, off + 512 // R1) - off), R1), [(1.0, A(rb, off, min(C, off + 512 // R1)))])
                for k in range(m):
                    tt(A(ca, k * R1 * C + R1 * lo, k * R1 * C + R1 * hi), vf(lo, hi, k, m), A(yb_, R1 * (lo - off), R1 * (hi - off)), "add")
                if hi not in PSUBS: continue
                lo = max([0] + [p for p in PSUBS if p < hi])
                sums = [(blk("S1", k + m * h), row(k + m * h, lo, hi)) for k in range(m) for h in range(R1)]
                flags = t > 0 or not (CANCEL and DIRECT)
                lin(A(cnt, lo, hi), [(wide((512.0, -25.0 / 32 + (0 if flags else 1.0 / 64))) if CANCEL else -25.0 / 32, A("ones", lo, hi))] * DIRECT + sums[:10]
                    + [(-0.25, A(rb, 2 * C + lo, 2 * C + hi))] + ([(-FP / 64, A(rb, C + lo, C + hi))] if flags else []) + sums[10:])
            q_ = A("h" + cs_, C, 2 * C) if CANCEL else In(0)
            aff("q", q_, ps("cnt"), 1.0, 5.0 / 32 if DIRECT else -0.625)
            straight = DIRECT and eng("cand") == "V"
            if straight: tt(cand, ps("cnt"), q_, "is_gt")
            if not DIRECT or NCH == 2: tt(vv, ps("cnt"), q_, "subtract")
            if not straight: sign("cand", cand, vv, 0.0 if DIRECT else 25.0 / 32, True)
            lin(ps("c4"), [(1.0, TURN), (tri(-1.0, 16.0, 1) if straight else tri(-0.5 * FC, 8.0 * FC, 1), cand)])
            sign("c4", c4, ps("c4"), 15.5 if straight else (0.5, 7.5), True)
            lin(ps("na"), [(tri(0.5 * F4, 2.0 * F4, -1), c4)])
            sign("na", na, ps("na"), (0.5, -5.0), False)
            lin(ps("idx"), [(1.0, OWNI), (grp(col(F4, 2033.0 * F4), "BP"), c4), (grp(col(FN, 2033.0 * FN), "BP"), na)])
            scan(Fl(0), OWND, ps("idx"))
            if DIRECT and NCH > 2: tt(vv, ps("cnt"), q_, "subtract")
            if eng("ix") == "S": act(A(tu, 0, D), pick(Fl(0)), "Relu", -2033.0, 0.5)
            else: ts(A(tu, 0, D), pick(Fl(0)), 0.5, -2033.0, "mult", "add")
            for lo, hi in WINS:
                aff("eb", A(eb[0], eb[1] + lo, eb[1] + hi), IND(vf(lo, hi, -16), A(tu, lo // 16, hi // 16)), -1.0 / 512, 160.0 + (B0 + 8) / 512)
            aff("e1", e1, eb, 1.0, -161.0, True)
            if eng("zx") == "S": act(zx, x, "Relu", 60.0, -60.0)
            else: ts(zx, x, 0.5, 60.0, "is_lt", "mult")
            if eng("sg") != "V":
                lin(ps("sg"), [(1.0, x), (-1.0, e1)])
                if FG == 1: act(sg, ps("sg"), "Sign", -0.5)
                else: ts(sg, ps("sg"), 0.5, None, "is_gt")
            else: tt(sg, e1, A(y1, 0, R1 * C, R1), "is_lt")
            lin(ps("dl"), [(1.0, x), (-1.0 / 16, eb), (-15.0 / 16, e1)])
            act(xn, ps("dl"), "Abs", 10.0 - 15.0 / 16)
            lanes = DIRECT and not CANCEL
            CY2 = wide((-49408.0 if FG == 1 else -45312.0, 84.0 - 16 * lanes, -1.0 / 16), lanes)
            R2 = 1 if eng("r2x") == "-" else 2
            Y2 = A(y1, 0, R2 * C, R2)
            for h in range(2 if eng("r2x") == "P" else 1):
                lin(A(y1, h, R2 * C, R2), [(CY2, ONE), (-256.0, x), (-256.0, zx), (432.0, eb), (-688.0, e1), (-4096.0 * FG, sg), (-256.0, xn)])
            if eng("r2x") == "S": act(A(y1, 1, 2 * C, 2), Y2, "Identity")
            for k in range(8 if R2 == 2 else 0):
                if CANCEL and k == YB_AT // 2: aff("yb", yb, Y2, -1.0 / 512, (B0 - 16 + 63.0 / 16) / 512 - 80)
                tt(A(cb, 2 * k * C, 2 * (k + 1) * C), A(y1, 0, 2 * C), A(ca, (k % m) * R1 * C + k // m, (k % m + 1) * R1 * C, R1 // 2), "subtract")
            for k in range(16 - S_ROWS if R2 == 1 else 0):
                if CANCEL and k == YB_AT: aff("yb", yb, ps("y2"), -1.0 / 512, (B0 - 16 + 63.0 / 16) / 512 - 80)
                tt(A(cb, k * C, (k + 1) * C), ps("y2"), row(k, 0, C), "subtract")
            for k in range(16 - S_ROWS, 16, 2):
                pw = ps("mul")[0]
                for h in range(2):
                    lin(A(pw, h * C, (h + 1) * C), [(-1.0, row(k + h, 0, C)), (-512.0, yb)])
                act(A(cb, k * C, (k + 2) * C), A(pw, 0, 2 * C), "Identity", B0 - 16 + 63.0 / 16 - 80 * 512)
            sums = [(blk("S1", k), A(cb, k * C, (k + 1) * C)) for k in sorted(range(16), key=lambda k: k if k < 16 - S_ROWS else k - 3.5)]
            if R2 == 2: sums = [(blk("S1", k + 8 * h), A(cb, 2 * k * C + h, 2 * (k + 1) * C, 2)) for k in range(8) for h in range(2)]
            lin(ps("sum"), [(1.0, vv)] + ([(FP / 64, hp)] if flags else []) + [(1.0, q_)] * CANCEL + sums[:YB_AT + 3] + [(grp(1.0), yb)] * CANCEL + sums[YB_AT + 3:])
            cint = A("cint", D * c, D * c + D)
            if eng("u") == "P":
                pu = A(ps("u")[0], 2 * C, 2 * C + D)
                lin(pu, [(blk("SH", a), A(sb, a, C, 16)) for a in range(16)])
                aff("ti", A("i" + cs_, C, C + D), pu, 241.0)
                ts(cint, A("i" + cs_, C, C + D), 6, NP - 1, "arith_shift_right", "bitwise_and")
            elif eng("u") == "T":
                lin(ps("u"), [(1.0, OWNU), (grp(H2), xn)])
                scan(Fl(3), OWND, ps("u"))
                aff("ti", A("i" + cs_, C, C + D), pick(Fl(3)), 120.5)
                ts(cint, A("i" + cs_, C, C + D), 6, NP - 1, "arith_shift_right", "bitwise_and")
            else:
                lin(ps("u"), [(1.0, OWNU), (grp(HHI), xn), (grp(HLO), xn)])
                scan(In(1), OWND, ps("u"))
                ts(cint, pick(In(1)), 6, NP - 1, "arith_shift_right", "bitwise_and")
            aff("tu", A(tu, 16, 16 + D), cint)
            each = LAST > 1 and t == ST - 1
            def twins():
                if c < NCH - 1 and not each: return
                pq = "ps%d" % bank[DBANK]
                b0, nb = (D * c, D) if each else (0, DW)
                CF = A("cf", b0, b0 + nb)
                aff("cf", CF, A("cint", b0, b0 + nb))
                if RING:
                    for d in range(8):
                        lin(A(pq, nb * d, nb * d + nb), [(blk("Rall", d), CF)])
                    ts(A("Eq", 8 * b0, 8 * (b0 + nb)), A(pq, 0, 8 * nb), 0.0, None, "is_equal")
                    lin(A(pq, 424, 424 + nb), [(2.0 ** -10, CF)] + [(blk("Rall", 8 + d), A("Eq", 8 * b0 + nb * d, 8 * b0 + nb * d + nb)) for d in range(8)])
                    ts(A("soff", 2 * b0, 2 * (b0 + nb), 2), A(pq, 424, 424 + nb), 2.0 ** 10, col(1.0, float(NP)), "mult", "min")
                    return
                for a in range(16):
                    lin(A(pq, nb * a, nb * a + nb), [(blk("Rall", a), CF)])
                tt(A("Eq", 16 * b0, 16 * (b0 + nb)), A(pq, 0, 16 * nb), A("mask", 0, NW, DW // nb), "is_equal")
                lin(A(pq, 424, 424 + nb), [(2.0 ** -19, CF)] + [(blk("S1", a), A("Eq", 16 * b0 + nb * a, 16 * b0 + nb * a + nb)) for a in range(16)])
                ts(A("soff", 2 * b0, 2 * (b0 + nb), 2), A(pq, 424, 424 + nb), 2.0 ** 19, col(1.0, float(NP)), "mult", "min")
            if t not in DLATE: twins()
            lin(ps("rr"), [(grp(H2), xn)])
            aff("rr", rr, ps("rr"), 1.0 / 2048, 128.5 + 1.0 / 2048)
            lin(ps("mul"), ([(wide((129.0 * 2048, 1.0)), ONE)] if eng("cm") == "P" else []) + [(grp(H2), xn), (-2048.0, rr)])
            if eng("cm") == "S": act(ps("mul"), ps("mul"), "Identity", 129.0 * 2048 + 1)
            tt(In(2), n16, ps("mul"), "mult")
            ts(In(3), In(2), 5, NM - 1, "arith_shift_right", "bitwise_and")
            aff("a1", ps("a1"), n16, 1.0, col(37.0, 0.0))
            tt(Fl(1), In(3), ps("a1"), "add")
            if eng("yc") == "D": act(yc, IND(A("W", 0, NP + 16), A(tu, 16, 16 + D)), "Identity", YB, -1.0 / 65536)
            aff("wg", Fl(0), IND(A("W", 0, NP + 16), A(tu, 16, 16 + D)))
            if eng("yc") != "D": aff("yc", yc, Fl(0), -1.0 / 65536, YB)
            lin(ps("ad"), [(1.0, xn), (1.0, yc)])
            act(ad, ps("ad"), "Abs", 129.0)
            lin(ps("hs"), [(grp(1.0), ad)])
            sign("hs", hs, ps("hs"), THC, False)
            K3 = ps("k3")
            lin(K3, [(IF, Fl(0))] * (eng("k3") == "P") + [(65536.0, yc), (-XH / 2 * FH, hs)])
            if eng("k3") != "P": tt(K3, Fl(0), K3, "add")
            tt(Fl(2), Fl(1), K3, "min")
            last = LAST and (t, c) == (ST - 1, NCH - 1)
            if last:
                act(Fl(3), n16, "Identity", -8192.0)
                tt(hv, Fl(3), K3, "is_equal")
            else: sign("hv", hv, K3, -0.5, False)
            if t in DLATE: twins()
            lin(ps("hy"), [(-1.0, xn), (-1.0, yc), (16.0 * FH, hs)])
            aff("hy", hy, ps("hy"), 1.0, -129.0, True)
            if last:
                lin(ps("hs"), [(1.0, xn), (1.0, hy), (-8.0 * FH, hs)])
                act(zx, ps("hs"), "Identity", -8.0)
                lin(ps("hy"), [(8192.0 * FH, hs), (-16384.0, hv)])
                tt(Fl(3), n16, ps("hy"), "max")
            if CANCEL:
                if APART: ts(ap_, ps("sum"), 1.5 * 2.0 ** 16 + 25.0 / 32, 1.5 * 2.0 ** 16, "add", "subtract")
                aff("r2", r2, ps("sum"), 1.0, A("colf", DN[1] + t, DN[1] + t + 1))
            else:
                aff("mg", In(0), ps("sum"))
                tt(r2, ps("sum"), In(0), "subtract")
            if not (CANCEL and APART): ts(ap_, r2, 1.5 * 2.0 ** 16, 1.5 * 2.0 ** 16, "add", "subtract")
            Q = ps("wake")
            lin(Q, ([] if CANCEL else [(dg(t), ONE)]) + [(16 * U * FN, na), (8192 * U, r2), (-8064 * U, ap_)])
            if last: ts(Fl(0), Q, float(NM), None, "min")
            n32 = A("n32", t % 2 * NW + c * C, t % 2 * NW + (c + 1) * C)
            if eng("ent") == "S" and not last or eng("Q") == "S": sel(n32, n16, [[0, C]], 0.0, 1, 0)
            if eng("Q") == "S":
                act(aw, Q, "Relu")
                lin(Q, [(IF, n32), (1.0, aw)])
            else: tt(Q, n16, Q, "max")
            tt(In(4), Fl(2), Q, "min")
            ts(nn32, In(4), NM - 1, None, "bitwise_and")
            tt(s6, nn32, Q, "is_equal")
            if t < ST - 1:
                aff("u16", nn16, nn32)
                for call in SENDS:
                    to = [A("r%s%d%d" % (p_, t + 1, c), lo, hi) for p_, lo, hi in call]
                    put("G", "send", None, [A("s%s%d%d" % (p_, t, c), lo, hi) for p_, lo, hi in call], (to, arr[0]))
                    for j, o in enumerate(to):
                        put("R", "recv", o, [], (arr[0], j, len(to)))
                    arr[0] += len(to)
            else:
                lin(ps("yt"), [(8192.0, s6)])
                tt(A("oyt", c * C, (c + 1) * C), nn32, ps("yt"), "add")
                dma("Y", A("yt", c * C, (c + 1) * C), A("oyt", c * C, (c + 1) * C))
                dma("Y", A("yx", c * C, (c + 1) * C), xn)
            if not last:
                lin(ps("ent"), ([(wide((121.0 * 65536, KO + XA)), ONE)] if eng("ent") == "V" else [])
                    + [(65536.0, xn), ((-524288.0 + XH / 2) * FH, hs), (65536.0, hy), (-XH / 2 * FV, hv), (-XA, s6)])
                if eng("ent") == "V": tt(A("ent", c * C, (c + 1) * C), n16, ps("ent"), "add")
                else: act(A("ent", c * C, (c + 1) * C), ps("ent"), "Identity", 121.0 * 65536 + KO + XA)
            spans.append((first, len(body), c))
        WT = "W2" if each else "W"
        if each: act(A(WT, 0, NP), A("W", 0, NP), "Identity")
        for b in range(DW - D * last):
            o, e = IND(A(WT, 0, NP + 16), A("soff", 2 * b, 2 * b + 1)), A("ent", 16 * b, 16 * b + 16)
            if eng("ent", t, b // D) == "V": cp(o, e)
            else: tt(o, e, A("n32", t % 2 * NW + 16 * b, t % 2 * NW + 16 * b + 16), "add")
    step = OSTEP
    for j, lo in enumerate(range(0, NP, step)):
        hi = lo + step
        act(A("oy1", lo, hi), A(WT, lo, hi), "Identity", YB, -1.0 / 65536)
        lin(A("ps%d" % j, 0, hi - lo), [(IF, A(WT, lo, hi)), (65536.0, A("oy1", lo, hi))])
        ts(A("oyk", lo, hi), A("ps%d" % j, 0, hi - lo), -KO, float(NM), "add", "min")
        if not LAST: dma("Y", A("yk", lo, hi), A("oyk", lo, hi))
    act(A("oy2", 0, NP), A("oy1", 0, NP), "Identity", -129.0, -1.0)
    for b in range(D if LAST else 0):
        off, lo = A("soff", 2 * (DW - D + b), 2 * (DW - D + b) + 1), 16 * b
        cp(IND(A("oy2", 0, NP + 16), off), A(zx[0], zx[1] + lo, zx[1] + lo + 16))
        tt(IND(A("oyk", 0, NP + 16), off), A(Fl(0)[0], lo, lo + 16), A(Fl(0)[0], 3 * C + lo, 3 * C + lo + 16), "max")
    if LAST: dma("S", A("yk", 0, NP), A("oyk", 0, NP))
    dma("Y", A("yy", 0, NP), A("oy2", 0, NP))
    SPANS[:] = [(lo + len(head), hi + len(head), c) for lo, hi, c in spans]
    return head + body


def regions(op):
    rd, wr = [], []
    for a in op[3]:
        if isinstance(a, tuple):
            rd += [a[1], a[2]] if a[0] == "@" else [a]
    o = op[2]
    if o is not None:
        if o[0] == "@":
            wr.append(o[1]); rd.append(o[2])
        else:
            wr.append(o)
    return [r for r in rd if r[0] not in DRAM], [r for r in wr if r[0] not in DRAM]


SC = {"gather": 1.65, "scatter": 3.0, "call": 24, "act": 80, "psum": 25, "pe": 0.435, "mm": 19, "lat": 15, "V": 70, "S": 35, "P": 40, "same": 70, "cross": 45, "pool": 220, "bw": 290.0, "dma": 1350, "gdma": 300, "issue": 450, "first": 1800, "link": 1300, "lbw": 27.0, "row": 25, "cyc": 0.86}


def cost(op, sc=SC):
    q, kind, o, ins, par = op
    if kind == "mm":
        d = sc["mm"] + sc["pe"] * max(64, count(o)) * (1 if narrow(ins[0]) else 4); return d, d + sc["lat"] + sc.get(q, 0)
    if kind == "dma":
        d = max(sc["gdma"] if q == "G" else 100, count(o) * 128 * (2 if narrow(o) or narrow(ins[0]) else 4) / sc["bw"]); return d, d + sc["dma"]
    if kind == "send":
        d = sc["issue"] + (0 if par[1] else sc.get("first", 0)); return d, d
    if kind == "recv":
        d = 0 if par[1] else 16 * par[2] * (sc["row"] + count(o) * (2 if narrow(o) else 4) / sc["lbw"]); return d, d + sc["link"]
    n, y = count(o), sc["cyc"]
    if kind in ("iota", "sel"): d = sc.get("pool", 170) + 2 * n * y
    elif o[0] == "@": d = 60 + sc["scatter"] * n * y
    elif ins and ins[0][0] == "@": d = 70 + sc["gather"] * n * y
    elif kind == "act": d = sc["act"] + max(64, n) * y + (sc.get("psum", 0) if "ps" in (o[0][:2], ins[0][0][:2]) else 0)
    elif kind == "tt":
        d = sc["call"] + max(64, n * (1 if "ps" in (ins[0][0][:2], ins[1][0][:2]) else 2)) * y
    else: d = sc["call"] + max(64, n * (0.5 if narrow(o) and (not ins or narrow(ins[0])) else 1)) * y
    return d, d + sc["lat"] + sc.get(q, 0)


def links():
    ops = describe()
    n = len(ops)
    hard = [set() for _ in range(n)]
    soft = [set() for _ in range(n)]
    hist, bank, sends = {}, {}, {}
    for i, op in enumerate(ops):
        rd, wr = regions(op)
        for r, isw in [(r, False) for r in rd] + [(r, True) for r in wr]:
            for j, lo, hi, w in hist.get(r[0], []):
                if j != i and (w or isw) and lo < r[2] and r[1] < hi:
                    (soft if op[0] == ops[j][0] == "P" else hard)[i].add(j)
            if r[0][:2] == "ps":
                j = bank.get(r[0])
                if j is not None and j != i:
                    (soft if ops[j][0] == op[0] else hard)[i].add(j)
                bank[r[0]] = i
        for r in wr:
            whole = r[3] == 1 and not (op[1] == "ms" and op[4][1] is not None)
            hist[r[0]] = [h for h in hist.get(r[0], []) if not (whole and r[1] <= h[1] and h[2] <= r[2])] + [(i, r[1], r[2], True)]
        for r in rd:
            hist.setdefault(r[0], []).append((i, r[1], r[2], False))
        if op[1] == "send":
            if op[3][0][1] >= C: soft[i].add(max(sends.values()))
            sends[op[4][1]] = i
        if op[1] == "recv": soft[i].add(i - 1)
        if FIRM and op[1] == "dma" and op[2][0] == "F" and op[2][1]: soft[i].add(i - 1)
    return ops, hard, soft


def schedule(q, dur, tail, prio, pre, suc, window=30):
    n = len(q)
    left = [len(p) for p in pre]
    ready = {k: [i for i in range(n) if q[i] == k and not left[i]] for k in "VSPGYR"}
    at, start, free, order, end = [0.0] * n, [0.0] * n, dict.fromkeys("VSPGYR", 0.0), [], 0.0
    soon = {k: 0.0 if ready[k] else 1e18 for k in ready}
    for _ in range(n):
        k = min(soon, key=soon.get)
        L, lim, i, top = ready[k], soon[k] + window, -1, -1e18
        for j in L:
            if at[j] <= lim and prio[j] > top: i, top = j, prio[j]
        L.remove(i)
        start[i] = max(at[i], free[k]); f = free[k] = start[i] + dur[i]
        if f + tail[i] > end: end = f + tail[i]
        order.append(i)
        for u, gap in suc[i]:
            if f + gap > at[u]: at[u] = f + gap
            left[u] -= 1
            if not left[u]:
                ready[q[u]].append(u)
                soon[q[u]] = min(soon[q[u]], max(at[u], free[q[u]]))
        soon[k] = max(f, min([at[j] for j in L])) if L else 1e18
    return end, start, order


def plan(sc=SC):
    ops, hard, soft = links()
    n = len(ops)
    q, dur, tail = [op[0] for op in ops], [cost(op, sc)[0] for op in ops], [cost(op, sc)[1] - cost(op, sc)[0] for op in ops]
    pre = [[(j, tail[j] + sc["same" if q[j] == q[i] else "cross"] if j in hard[i] else 0.0) for j in sorted(hard[i] | soft[i])] for i in range(n)]
    suc = [[] for _ in range(n)]
    for i in range(n):
        for j, gap in pre[i]: suc[j].append((i, gap))
    way = [0.0] * n
    for _ in range(2):
        for i in range(n - 1, -1, -1):
            way[i] = dur[i] + max([way[u] + gap for u, gap in suc[i]] + [tail[i]])
    best = None
    for lead in LEADS:
        for late in LATES:
            prio = way[:]
            for lo, hi, c in SPANS:
                for i in range(lo, hi):
                    prio[i] -= lead * c + (late if ops[i][1] == "act" and ops[i][3][0][0] == "@" and count(ops[i][2]) > C else 0)
            for _ in range(4):
                got = schedule(q, dur, tail, prio, pre, suc)
                if best is None or got[0] < best[0]: best = got
                back = schedule(q, dur, [0.0] * n, [got[1][i] + dur[i] for i in range(n)], suc, pre)[1]
                prio = [back[i] + dur[i] for i in range(n)]
    others = []
    for x, g_, s_, far, pe, weight in SHADES:
        so = dict(sc, gather=g_, scatter=s_, cyc=x, pe=pe)
        so.update({k: sc[k] * far for k in ("link", "issue", "first", "row")})
        cs = [cost(op, so) for op in ops]
        others.append(([a for a, b in cs], [b - a for a, b in cs], weight,
                       [[(j, cs[j][1] + so["same" if q[j] == q[i] else "cross"] if j in hard[i] else cs[j][0]) for j, gap in pre[i]] for i in range(n)]))

    def worth(got):
        total = got[0]
        for d, tl, weight, pr in others:
            st, free, end = [0.0] * n, dict.fromkeys("VSPGYR", 0.0), 0.0
            for i in got[2]:
                s = free[q[i]]
                for j, gap in pr[i]:
                    if st[j] + gap > s: s = st[j] + gap
                st[i] = s; s += d[i]; free[q[i]] = s
                if s + tl[i] > end: end = s + tl[i]
            total += weight * end
        return total
    cur, seed = best, [SEED]
    wc = wb = worth(best)

    def rnd():
        seed[0] = (seed[0] * 1103515245 + 12345) % 2147483648
        return seed[0] / 2147483648.0
    for _ in range(ROUNDS):
        a, lo, w = (100, 300, 1000)[int(3 * rnd())], rnd() * cur[0], 3000 + 17000 * rnd()
        prio = [cur[1][i] + dur[i] + ((2 * rnd() - 1) * a if lo <= cur[1][i] <= lo + w else 0) for i in range(n)]
        back = schedule(q, dur, [0.0] * n, prio, suc, pre)[1]
        got = schedule(q, dur, tail, [back[i] + dur[i] for i in range(n)], pre, suc)
        if got[0] > best[0] + 2500: continue
        wg = worth(got)
        if wg < wc + 150 * (1 + len(others)): cur, wc = got, wg
        if wg < wb: best, wb = got, wg
    needed = set()
    for i in range(n): needed |= hard[i]
    return ops, hard, best[2], needed, best[1], soft, best[0]


PLAN = []


def rank_program(g, core, T, topo):
    rank = T.rank_of(core)
    if rank is None:
        return
    if not PLAN:
        PLAN.append(plan())
    ops, hard, order, needed = PLAN[0][:4]
    dst = T.cores[(rank + SH) % NR]
    src = T.cores[(rank - SH) % NR]
    rid, pid, _e = topo.addr(dst)
    nout, nin = len(topo.engines(core, dst)), len(topo.engines(src, core))
    queue = {"V": g.vector, "S": g.scalar, "P": g.tensor, "G": g, "Y": g.sync}
    alu = {"add": AluOpType.add, "subtract": AluOpType.subtract, "mult": AluOpType.mult, "max": AluOpType.max, "min": AluOpType.min,
           "is_ge": AluOpType.is_ge, "is_gt": AluOpType.is_gt, "is_le": AluOpType.is_le, "is_lt": AluOpType.is_lt,
           "is_equal": AluOpType.is_equal, "not_equal": AluOpType.not_equal, "bitwise_and": AluOpType.bitwise_and,
           "arith_shift_right": AluOpType.arith_shift_right}
    fun = {"Identity": ActivationFunctionType.Identity, "Sign": ActivationFunctionType.Sign, "Relu": ActivationFunctionType.Relu,
           "Abs": ActivationFunctionType.Abs}

    def ap(a):
        if not isinstance(a, tuple): return a
        if a[0] == "@": return ap(a[1]).indirect(ap(a[2]))
        if a[0] in ("hw", "th", "dw"): return T[a[0]][:]
        return T[a[0]][:, a[1]:a[2]] if a[3] == 1 else T[a[0]][:, a[1]:a[2]:a[3]]

    mark, total, seen, ndma = {}, {}, {}, [0]

    def wait(q, name, val):
        if seen.get((q, name), 0) < val:
            queue[q].wait_ge(T.sem[name], val)
            seen[(q, name)] = val

    for i in order:
        q, kind, o, ins, par = ops[i]
        if kind == "recv":
            name = "a%d" % (par[0] + par[1])
            mark[i] = (name, nin // par[2]); total[name] = nin // par[2]
            continue
        want = {}
        for j in hard[i]:
            want[mark[j][0]] = max(want.get(mark[j][0], 0), mark[j][1])
        for name in sorted(want):
            wait(q, name, want[name])
        e = queue[q]
        if kind == "send":
            if len(ins) == 1:
                g.remote_dma(ap(par[0][0]), ap(ins[0]), T.sem["a%d" % par[1]], T.sem.sent, pid, rid, topo.mask(core, dst))
            else:
                eng, m = topo.engines(core, dst), nout // len(ins)
                g.remote_dma_fused([RemoteDMATransfer(dst_ids=[DstId(rid=rid, pnc=pid)], remote_sem=T.sem["a%d" % (par[1] + j)],
                                                      dma_engine_mask=sum(1 << k for k in eng[j * m:(j + 1) * m]),
                                                      src=ap(ins[j]), dst=ap(par[0][j])) for j in range(len(ins))], local_sem=T.sem.sent)
            total["sent"] = total.get("sent", 0) + nout // len(ins) * len(ins)
            continue
        if kind == "dma":
            name = "d%d" % ndma[0]; ndma[0] += 1
            if q == "G": ins_ = g.dma_start(ap(o), ap(ins[0]), allow_slow_non_contiguous=True)
            else: ins_ = e.dma_start(ap(o), ap(ins[0]))
            ins_.then_inc(T.sem[name], 16)
            mark[i] = (name, 16); total[name] = 16
            continue
        if kind == "tt": ins_ = e.tensor_tensor(ap(o), ap(ins[0]), ap(ins[1]), alu[par])
        elif kind == "ts" and par[1] is None: ins_ = e.tensor_scalar(ap(o), ap(ins[0]), ap(ins[1]), None, alu[par[0]])
        elif kind == "ts": ins_ = e.tensor_scalar(ap(o), ap(ins[0]), ap(ins[1]), ap(ins[2]), alu[par[0]], alu[par[1]])
        elif kind == "scan": ins_ = e.tensor_tensor_scan(ap(o), ap(ins[0]), ap(ins[1]), 0.0, AluOpType.add, AluOpType.min)
        elif kind == "cp": ins_ = e.tensor_copy(ap(o), ap(ins[0]))
        elif kind == "ms" and par[1] is None: ins_ = e.memset(ap(o), par[0])
        elif kind == "ms": ins_ = e.memset(T[o[0]][par[1]:par[1] + 1, o[1]:o[2]], par[0])
        elif kind == "act": ins_ = e.activation(ap(o), ap(ins[0]), fun[par], bias=ap(ins[1]), scale=ap(ins[2]))
        elif kind == "mm": ins_ = e.matmul(ap(o), ap(ins[0]), ap(ins[1]), par[0], par[1])
        elif kind == "sel": ins_ = g.affine_select(ap(o), ap(ins[0]), par[0], alu[par[4]], par[3], par[1], par[2])
        elif SCRATCH[o[0]][2] == "int32": ins_ = g.iota(ap(o), par[0], par[1], par[2])
        else: ins_ = g.iota(ap(o), par[0], par[1], par[2], allow_small_or_imprecise_dtypes=True)
        if i in needed:
            total[q] = total.get(q, 0) + 1
            ins_.then_inc(T.sem[q], 1)
            mark[i] = (q, total[q])
    for name in sorted(total):
        wait("G", name, total[name])
